import numpy as np
import ml_dtypes


def mxq(x, axis, fmt="e4m3"):
    dtype, down = {"e4m3": (ml_dtypes.float8_e4m3fn, 7), "e5m2": (ml_dtypes.float8_e5m2, 14)}[fmt]
    v = np.moveaxis(np.asarray(x, np.float32).astype(ml_dtypes.bfloat16).astype(np.float64), axis, -1)
    blocks = v.reshape(v.shape[:-1] + (-1, 32))
    amax = np.abs(blocks).max(-1, keepdims=True)
    byte = np.maximum(np.where(amax > 0, np.frexp(amax)[1] - 1 + 127, 0) - down, 1)
    scale = np.exp2(byte - 127.0)
    codes = (blocks / scale).astype(np.float32).astype(dtype).astype(np.float64)
    return np.moveaxis((codes * scale).reshape(v.shape), -1, axis)


WIDE = False


def mx_kscale(k):
    if not WIDE:
        return np.ones(k)
    levels = np.array([10, -10, 5, -5, 0])
    if k % 512:
        return np.exp2(np.random.permutation(np.resize(levels, k // 32))).repeat(32)
    a = np.empty((k // 512, 16))
    for p in range(k // 512):
        a[p, :8] = np.random.permutation(np.resize(levels, 8))
        for g in range(8):
            far = levels[np.abs(levels - a[p, g]) >= 10]
            a[p, g + 8] = far[np.random.randint(len(far))]
    return np.exp2(a.ravel()).repeat(32)


def f64(x):
    return np.asarray(x).astype(np.float64)


def striped(idx):
    return np.tile(idx.reshape(-1, 16).T, (8, 1)).astype(np.uint16)


def unstriped(offs):
    return offs[:16].T.reshape(-1).astype(np.int64)


E2M1 = np.array([0.0, 0.5, 1.0, 1.5, 2.0, 3.0, 4.0, 6.0, -0.0, -0.5, -1.0, -1.5, -2.0, -3.0, -4.0, -6.0])


def pack_weight(w, fmt):
    k, n = w.shape
    w = f64(np.asarray(w, np.float32).astype(ml_dtypes.bfloat16)).reshape(k // 32, 32, n)
    amax = np.abs(w).max(1)
    if fmt == "e4m3":
        byte = np.frexp(amax)[1] - 1 + 127 - 7
    else:
        mant, ex = np.frexp(amax / 6.0)
        byte = np.where(mant > 0.5, ex, ex - 1) + 127
    byte = np.clip(np.where(amax > 0, byte, 1), 1, 254)
    scaled = (w * np.exp2(127.0 - byte)[:, None, :]).reshape(k, n).astype(np.float32)
    by_word = np.ascontiguousarray(scaled.reshape(k // 512, 128, 4, n).transpose(0, 1, 3, 2))
    if fmt == "e4m3":
        words = by_word.astype(ml_dtypes.float8_e4m3fn).view(np.uint8)
    else:
        c = by_word.astype(ml_dtypes.float4_e2m1fn).view(np.uint8) & 0xF
        words = (c[..., 0::2] | (c[..., 1::2] << 4)).reshape(k // 512, 128, 2 * n)
    return np.ascontiguousarray(words), np.ascontiguousarray(byte.astype(np.uint8).reshape(k // 512, 16, n))


def unpack_weight(words, scales, fmt):
    g, _, n = scales.shape
    words = np.ascontiguousarray(words).reshape(g, 128, n, -1)
    if fmt == "e4m3":
        vals = words.view(ml_dtypes.float8_e4m3fn).astype(np.float64)
    else:
        nib = np.empty((g, 128, n, 4), np.uint8)
        nib[..., 0::2] = words & 0xF
        nib[..., 1::2] = words >> 4
        vals = E2M1[nib]
    vals = vals * np.repeat(np.exp2(scales.astype(np.float64) - 127.0), 8, axis=1)[..., None]
    return vals.transpose(0, 1, 3, 2).reshape(g * 512, n)


def gelu(v):
    return 0.5 * v * (1.0 + np.tanh(np.sqrt(2.0 / np.pi) * (v + 0.044715 * v**3)))


def often(T, S):
    return np.random.permutation(T)[(T * np.random.uniform(0, 1, S) ** 4).astype(np.int64)]


K, T, S, T2, P, H, N = 1024, 4096, 1024, 1024, 512, 1024, 384

def setup_inputs():
    n = np.random.standard_normal
    s = mx_kscale(K)[:, None]
    u = mx_kscale(H)[:, None]
    d = {}
    d["tab_words"], d["tab_scales"] = pack_weight(n((K, T)) * s, "e4m3")
    d["offs"] = striped(np.random.permutation(T)[:S])
    d["pos1"] = striped(often(S, P))
    d["tab2_words"], d["tab2_scales"] = pack_weight(n((K, T2)) * s, "e4m3")
    d["offs2"] = striped(np.random.permutation(T2)[:P])
    d["w1"] = (n((K, H)) / np.sqrt(K) / s * u.T).astype(np.float32)
    d["b1"] = (0.5 * n(H) * u[:, 0]).astype(np.float32)
    d["w4_words"], d["w4_scales"] = pack_weight(n((K, H)) / np.sqrt(K) / s * u.T, "e2m1")
    d["w8_words"], d["w8_scales"] = pack_weight(1.5 * n((K, H)) / np.sqrt(K) / s * u.T, "e4m3")
    d["wo"] = (1.5 * n((H, N)) / np.sqrt(H) / u).astype(np.float32)
    return d

def reference(tab_words, tab_scales, offs, pos1, tab2_words, tab2_scales, offs2,
              w1, b1, w4_words, w4_scales, w8_words, w8_scales, wo):
    v = unpack_weight(tab_words, tab_scales, "e4m3")[:, unstriped(offs)]
    v2 = unpack_weight(tab2_words, tab2_scales, "e4m3")[:, unstriped(offs2)]
    w4 = unpack_weight(w4_words, w4_scales, "e2m1")
    w8 = unpack_weight(w8_words, w8_scales, "e4m3")
    c = np.maximum((mxq(f64(w1), 0, "e4m3").T @ v) + f64(b1)[:, None], 0.0)
    x = np.maximum((w4.T @ v) + c, 0.0)
    a = x[:, unstriped(pos1)]
    b = w8.T @ v2
    h = np.maximum(b - a, 0.0)
    return mxq(f64(wo), 0, "e4m3").T @ mxq(h, 0, "e4m3")

@@ -1,0 +1,309 @@
+from contextlib import ExitStack
+
+import concourse.mybir as mybir
+from concourse.masks import make_identity
+
+K, T, S, T2, M, H, N = 1024, 4096, 1024, 1024, 512, 1024, 384
+FLOPS = 2 * K * H * S * 2 + 2 * K * H * M + 2 * H * N * M
+
+F32 = mybir.dt.float32
+BF16 = mybir.dt.bfloat16
+I32 = mybir.dt.int32
+U32 = mybir.dt.uint32
+U16 = mybir.dt.uint16
+U8 = mybir.dt.uint8
+FP8X4 = mybir.dt.float8_e4m3fn_x4
+FP4X4 = mybir.dt.float4_e2m1fn_x4
+ALU = mybir.AluOpType
+RELU = mybir.ActivationFunctionType.Relu
+
+P = 128
+BANK = 512
+
+
+def tile_list_excess_delay_causes_kernel(tc, tab_words, tab_scales, offs, pos1, tab2_words, tab2_scales, offs2,
+                                                   w1, b1, w4_words, w4_scales, w8_words, w8_scales, wo, out):
+    nc = tc.nc
+    with ExitStack() as ctx:
+        keep = ctx.enter_context(tc.tile_pool(name="keep", bufs=1))
+        ring = ctx.enter_context(tc.tile_pool(name="ring", bufs=2))
+        psum = ctx.enter_context(tc.psum_pool(name="psum", bufs=3))
+
+        def held(name, shape, dtype):
+            return keep.tile(shape, dtype, name=name, align_bytes=64)
+
+        offs_t = keep.tile([P, S // 16], U16, name="offs_t")
+        pos_t = keep.tile([P, M // 16], U16, name="pos_t")
+        offs2_t = keep.tile([P, M // 16], U16, name="offs2_t")
+
+        tab_w = [held("tab_w%d" % a, [P, T], I32) for a in range(2)]
+        tab_s = held("tab_s", [P, 2, T], U8)
+        tab2_w = held("tab2_w", [P, 2, T2], I32)
+        tab2_s = held("tab2_s", [P, T2], U8)
+        w4_raw = held("w4_raw", [P, 2, 2 * H], U8)
+        w4s_raw = held("w4s_raw", [P, 2, H], U8)
+        w8_raw = held("w8_raw", [P, 2, H], I32)
+        w8s_raw = held("w8s_raw", [P, H], U8)
+        bias_rows = held("bias_rows", [P, P], F32)
+        ident = held("ident", [P, P], F32)
+        bias = held("bias", [P, 8], F32)
+        warm = held("warm", [P, 8], F32)
+
+        nc.vector.memset(tab2_s[:].bitcast(I32), 0)
+        nc.vector.memset(tab_s[:].bitcast(I32), 0)
+        nc.gpsimd.memset(warm[:], 0.0)
+        nc.gpsimd.memset(w4s_raw[:].bitcast(I32), 0)
+        nc.gpsimd.memset(bias_rows[:], 0.0)
+        nc.gpsimd.memset(w8s_raw[:].bitcast(I32), 0)
+        make_identity(nc, ident[:])
+        nc.scalar.activation(warm[:, 4:8], warm[:, 0:4], RELU)
+
+        def load(dst, src):
+            nc.sync.dma_start(dst, src)
+
+        def load_tab_words(a, half):
+            cols = slice(half * T // 2, (half + 1) * T // 2)
+            load(tab_w[a][:, cols], tab_words[a].rearrange("p t i -> p (t i)").bitcast(I32)[:, cols])
+
+        def load_side_by_side(dst, scales, q):
+            load(dst[32 * q : 32 * q + 4, :, :].bitcast(I32), scales[:, 4 * q : 4 * q + 4, :].rearrange("a r n -> r a n").bitcast(I32))
+
+        def load_stacked(dst, scales, q):
+            load(dst[32 * q : 32 * q + 8, :].bitcast(I32), scales[:, 4 * q : 4 * q + 4, :].bitcast(I32))
+
+        w1_raw = {}
+
+        def load_w1(a, b):
+            w1_raw[a, b] = ring.tile([P, 4, 512], F32, name="w1_raw", bufs=3)
+            load(w1_raw[a, b][:], w1[512 * a : 512 * (a + 1), 512 * b : 512 * (b + 1)].rearrange("(p j) c -> p j c", j=4))
+
+        wo_raw = [held("wo_raw%d" % b, [P, 4, N], F32) for b in range(2)]
+
+        def load_wo(b, t):
+            load(wo_raw[b][:, t, :], wo[512 * b : 512 * (b + 1), :].rearrange("(q t i) n -> t q i n", t=4, i=8)[t])
+
+        load(tab2_w[:], tab2_words.rearrange("a p t i -> p a (t i)").bitcast(I32))
+        load(offs2_t[:], offs2)
+        load_stacked(tab2_s, tab2_scales, 0)
+        load_stacked(tab2_s, tab2_scales, 1)
+        load_tab_words(0, 0)
+        load_stacked(tab2_s, tab2_scales, 2)
+        load_stacked(tab2_s, tab2_scales, 3)
+        load(offs_t[:], offs)
+        load_tab_words(0, 1)
+        for q in range(3):
+            load_side_by_side(tab_s, tab_scales, q)
+        load_w1(0, 0)
+        load_side_by_side(tab_s, tab_scales, 3)
+        load(w4_raw[:].bitcast(I32), w4_words.rearrange("a p e -> p a e").bitcast(I32))
+        load_side_by_side(w4s_raw, w4_scales, 0)
+        load_w1(1, 0)
+        for q in range(1, 4):
+            load_side_by_side(w4s_raw, w4_scales, q)
+        load_tab_words(1, 0)
+        for b in range(2):
+            load(bias_rows[4 * b : 4 * b + 4, :], b1[512 * b : 512 * (b + 1)].rearrange("(q t i) -> t q i", t=4, i=8))
+        load(pos_t[:], pos1)
+        load_tab_words(1, 1)
+        load(w8_raw[:], w8_words.rearrange("a p e i -> p a (e i)").bitcast(I32))
+        for q in range(4):
+            load_stacked(w8s_raw, w8_scales, q)
+        load_w1(0, 1)
+        load_w1(1, 1)
+        for b in range(2):
+            for t in range(4):
+                load_wo(b, t)
+
+        v2_w = [held("v2_w%d" % a, [P, M], U32) for a in range(2)]
+        v2_s = held("v2_s", [P, M], U8)
+        for a in range(2):
+            nc.vector.tensor_copy(v2_w[a][:], tab2_w[:, a, :].bitcast(U32).indirect(offs2_t[:]))
+        nc.vector.tensor_copy(v2_s[:], tab2_s[:].indirect(offs2_t[:]))
+
+        v_s = [held("v_s%d" % a, [P, S], U8) for a in range(2)]
+        v_w = {(a, hf): held("v_w%d%d" % (a, hf), [P, BANK], U32) for a in range(2) for hf in range(2)}
+
+        def gather_words(a, hf):
+            nc.vector.tensor_copy(v_w[a, hf][:], tab_w[a][:].bitcast(U32).indirect(offs_t[:, 32 * hf : 32 * (hf + 1)]))
+
+        nc.vector.tensor_copy(v_s[0][:], tab_s[:, 0, :].indirect(offs_t[:]))
+        gather_words(0, 0)
+        gather_words(0, 1)
+        nc.vector.tensor_copy(v_s[1][:], tab_s[:, 1, :].indirect(offs_t[:]))
+
+        bias_ps = psum.tile([P, BANK], F32, name="bias_ps", tag="pb", bufs=2)
+        nc.tensor.transpose(bias_ps[:, 0:P], bias_rows[:], ident[:])
+        nc.scalar.copy(bias[:], bias_ps[:, 0:8])
+
+        w4_p = [held("w4_p%d" % b, [P, 2, H], U8) for b in range(2)]
+        w4s_p = [held("w4s_p%d" % b, [P, 2, H // 2], U8) for b in range(2)]
+        w8_p = [held("w8_p%d" % b, [P, 2, H // 2], I32) for b in range(2)]
+        w8s_p = held("w8s_p", [P, H], U8)
+
+        def reorder(dst, src, b, run):
+            width = 64 * run
+            nc.vector.tensor_copy(dst.rearrange("p a (t q i) -> p a t q i", t=4, i=run),
+                                  src[:, :, b * width : (b + 1) * width].rearrange("p a (q t i) -> p a t q i", t=4, i=run))
+
+        def reorder_w4(b):
+            reorder(w4_p[b][:].bitcast(I32), w4_raw[:].bitcast(I32), b, 4)
+            reorder(w4s_p[b][:].bitcast(I32), w4s_raw[:].bitcast(I32), b, 2)
+
+        def reorder_w8_scales():
+            nc.vector.tensor_copy(w8s_p[:].bitcast(I32).rearrange("p (b t q i) -> p b t q i", b=2, t=4, i=2),
+                                  w8s_raw[:].bitcast(I32).rearrange("p (b q t i) -> p b t q i", b=2, t=4, i=2))
+
+        w1_c = {(a, b): held("w1_c%d%d" % (a, b), [P, 512], U32) for a in range(2) for b in range(2)}
+        w1_s = {(a, b): held("w1_s%d%d" % (a, b), [P, 512], U8) for a in range(2) for b in range(2)}
+        w1_g = {}
+
+        def cast_w1(a, b, t):
+            w1_g[a, b, t] = ring.tile([P, 512], BF16, name="w1_g", bufs=8, align_bytes=64)
+            nc.scalar.copy(w1_g[a, b, t][:].rearrange("p (q u i j) -> p q u j i", u=2, i=4, j=4),
+                           w1_raw[a, b][:].rearrange("p j (q t u i) -> p t q u j i", t=4, u=2, i=4)[:, t])
+
+        def quantize_w1(a, b, t):
+            cols = slice(P * t, P * (t + 1))
+            nc.vector.quantize_mx(out=w1_c[a, b][:, cols].bitcast(FP8X4), scales=w1_s[a, b][:, cols], in_=w1_g[a, b, t][:])
+
+        wo_g = held("wo_g", [P, 2, N, 4], BF16)
+        wo_c = held("wo_c", [P, 2 * N], U32)
+        wo_s = held("wo_s", [P, 2 * N], U8)
+
+        def cast_wo(b):
+            nc.scalar.copy(wo_g[:, b].rearrange("p (c i) t -> p c t i", i=4), wo_raw[b][:].rearrange("p t (c i) -> p c t i", i=4))
+
+        def quantize_wo():
+            flat = wo_g[:].rearrange("p b n t -> p (b n t)")
+            for lo, hi in ((0, 512), (512, 768)):
+                nc.vector.quantize_mx(out=wo_c[:, lo:hi].bitcast(FP8X4), scales=wo_s[:, lo:hi], in_=flat[:, 4 * lo : 4 * hi])
+
+        reorder_w4(0)
+        for t in range(4):
+            cast_w1(0, 0, t)
+        for t in range(4):
+            cast_w1(1, 0, t)
+        for t in range(4):
+            quantize_w1(0, 0, t)
+        for t in range(4):
+            quantize_w1(1, 0, t)
+        reorder_w4(1)
+        gather_words(1, 0)
+        gather_words(1, 1)
+
+        x_pre = {}
+        picked = {}
+        own = {}
+        diff = [held("diff%d" % b, [P, 4, M], F32) for b in range(2)]
+
+        def caller_half(b, t, hf):
+            cols = slice(P * t, P * (t + 1))
+            jc = slice(BANK * hf, BANK * (hf + 1))
+            p1 = psum.tile([P, BANK], F32, name="p1", tag="p1")
+            p4 = psum.tile([P, BANK], F32, name="p4", tag="p4")
+            for a in range(2):
+                nc.tensor.matmul_mx(out=p1[:], lhsT=w1_c[a, b][:, cols].bitcast(FP8X4), lhsT_scale=w1_s[a, b][:, cols],
+                                    rhs=v_w[a, hf][:].bitcast(FP8X4), rhs_scale=v_s[a][:, jc], start=(a == 0), stop=(a == 1))
+            for a in range(2):
+                nc.tensor.matmul_mx(out=p4[:], lhsT=w4_p[b][:, a, 2 * P * t : 2 * P * (t + 1)].bitcast(FP4X4), lhsT_scale=w4s_p[b][:, a, cols],
+                                    rhs=v_w[a, hf][:].bitcast(FP8X4), rhs_scale=v_s[a][:, jc], start=(a == 0), stop=(a == 1))
+            c = ring.tile([P, BANK], F32, name="c", bufs=3)
+            nc.scalar.activation(c[:], p1[:], RELU, bias=bias[:, 4 * b + t : 4 * b + t + 1])
+            if hf == 0:
+                x_pre[b, t] = ring.tile([P, S], F32, name="x_pre", bufs=2)
+            nc.vector.tensor_tensor(x_pre[b, t][:, jc], p4[:], c[:], ALU.add)
+
+        def callee_product(b, t):
+            own[b, t] = psum.tile([P, BANK], F32, name="own", tag="pb", bufs=2)
+            for a in range(2):
+                nc.tensor.matmul_mx(out=own[b, t][:], lhsT=w8_p[b][:, a, P * t : P * (t + 1)].bitcast(FP8X4),
+                                    lhsT_scale=w8s_p[4 * a : P, 512 * b + P * t : 512 * b + P * (t + 1)],
+                                    rhs=v2_w[a][:].bitcast(FP8X4), rhs_scale=v2_s[4 * a : P, :], start=(a == 0), stop=(a == 1))
+
+        def pick(b, t, lo, hi):
+            picked[b, t, lo] = ring.tile([P, hi - lo], F32, name="picked", bufs=3)
+            nc.vector.tensor_copy(picked[b, t, lo][:], x_pre[b, t][:].indirect(pos_t[:, lo // 16 : hi // 16]))
+
+        def subtract(b, t, lo, hi):
+            nc.vector.scalar_tensor_tensor(diff[b][:, t, lo:hi], picked[b, t, lo][:], 0.0, own[b, t][:, lo:hi], ALU.max, ALU.subtract)
+
+        h_g = {}
+        h_c = {}
+        h_s = {}
+
+        def views(b, lo, hi):
+            h_g[b, lo] = held("h_g%d_%d" % (b, lo), [P, hi - lo, 4], BF16)
+            return (h_g[b, lo][:].rearrange("p (c i) t -> p c t i", i=4), diff[b][:, :, lo:hi].rearrange("p t (c i) -> p c t i", i=4))
+
+        def relu_scalar(b, lo, hi):
+            dst, src = views(b, lo, hi)
+            nc.scalar.activation(dst, src, RELU, scale=-1.0)
+
+        def relu_vector(b, lo, hi):
+            dst, src = views(b, lo, hi)
+            nc.vector.tensor_scalar(dst, src, -1.0, 0.0, ALU.mult, ALU.max)
+
+        def quantize_h(b, lo, hi):
+            h_c[b, lo] = held("h_c%d_%d" % (b, lo), [P, hi - lo], U32)
+            h_s[b, lo] = held("h_s%d_%d" % (b, lo), [P, hi - lo], U8)
+            nc.vector.quantize_mx(out=h_c[b, lo][:].bitcast(FP8X4), scales=h_s[b, lo][:], in_=h_g[b, lo][:].rearrange("p m t -> p (m t)"))
+
+        tiles = [(b, t) for b in range(2) for t in range(4)]
+        for n, (b, t) in enumerate(tiles):
+            caller_half(b, t, 0)
+            if n == 0:
+                reorder_w8_scales()
+                reorder(w8_p[0][:], w8_raw[:], 0, 8)
+            else:
+                callee_product(*tiles[n - 1])
+                pick(*tiles[n - 1], 0, M)
+            if n in (1, 2):
+                for tt in range(2):
+                    cast_w1(n - 1, 1, tt)
+            caller_half(b, t, 1)
+            if n > 0:
+                subtract(*tiles[n - 1], 0, M)
+            if n in (1, 2):
+                for tt in range(2, 4):
+                    cast_w1(n - 1, 1, tt)
+            if n in (2, 3):
+                for tt in range(4):
+                    quantize_w1(n - 2, 1, tt)
+            if n == 3:
+                reorder(w8_p[1][:], w8_raw[:], 1, 8)
+            if n == 4:
+                relu_scalar(0, 0, M)
+            if n in (5, 6):
+                cast_wo(n - 5)
+            if n == 5:
+                quantize_h(0, 0, M)
+
+        half = M // 2
+        callee_product(1, 3)
+        quantize_wo()
+        pick(1, 3, 0, half)
+        pick(1, 3, half, M)
+        subtract(1, 3, 0, half)
+        relu_scalar(1, 0, half)
+        subtract(1, 3, half, M)
+        scores = {}
+        for hf in range(2):
+            for c3 in range(3):
+                scores[hf, c3] = psum.tile([P, BANK], F32, name="scores", tag="p1" if hf == 0 else "p4")
+                nc.tensor.matmul_mx(out=scores[hf, c3][:, 0:half], lhsT=wo_c[:, P * c3 : P * (c3 + 1)].bitcast(FP8X4), lhsT_scale=wo_s[:, P * c3 : P * (c3 + 1)],
+                                    rhs=h_c[0, 0][:, half * hf : half * (hf + 1)].bitcast(FP8X4), rhs_scale=h_s[0, 0][:, half * hf : half * (hf + 1)],
+                                    start=True, stop=False)
+        relu_vector(1, half, M)
+        quantize_h(1, 0, half)
+        quantize_h(1, half, M)
+        for hf in range(2):
+            staged = held("staged%d" % hf, [P, 3, half], F32)
+            for c3 in range(3):
+                cols = slice(N + P * c3, N + P * (c3 + 1))
+                nc.tensor.matmul_mx(out=scores[hf, c3][:, 0:half], lhsT=wo_c[:, cols].bitcast(FP8X4), lhsT_scale=wo_s[:, cols],
+                                    rhs=h_c[1, half * hf][:].bitcast(FP8X4), rhs_scale=h_s[1, half * hf][:], start=False, stop=True)
+                if hf == 1 and c3 == 1:
+                    nc.vector.tensor_copy(staged[:, c3, :], scores[hf, c3][:, 0:half])
+                else:
+                    nc.scalar.copy(staged[:, c3, :], scores[hf, c3][:, 0:half])
+            nc.sync.dma_start(out.rearrange("(c p) m -> p c m", p=P)[:, :, half * hf : half * (hf + 1)], staged[:])

@@ -19,6 +19,7 @@ RELU = mybir.ActivationFunctionType.Relu
 
 P = 128
 BANK = 512
+V_AT, V2_AT, W4_AT, W8_AT, ROW = 0, 1024, 1536, 2560, 3584
 
 
 def tile_list_excess_delay_causes_kernel(tc, tab_words, tab_scales, offs, pos1, tab2_words, tab2_scales, offs2,
@@ -36,109 +37,96 @@ def tile_list_excess_delay_causes_kernel(tc, tab_words, tab_scales, offs, pos1, 
         pos_t = keep.tile([P, M // 16], U16, name="pos_t")
         offs2_t = keep.tile([P, M // 16], U16, name="offs2_t")
 
-        tab_w = [held("tab_w%d" % a, [P, T], I32) for a in range(2)]
-        tab_s = held("tab_s", [P, 2, T], U8)
-        tab2_w = held("tab2_w", [P, 2, T2], I32)
+        def slot(name, shape, dtype, tag):
+            return keep.tile(shape, dtype, name=name, tag=tag, align_bytes=64)
+
+        tab_s = held("tab_s", [P, T], U8)
+        tab2_w = slot("tab2_w", [P, 2, T2], I32, "slot_c")
         tab2_s = held("tab2_s", [P, T2], U8)
         w4_raw = held("w4_raw", [P, 2, 2 * H], U8)
-        w4s_raw = held("w4s_raw", [P, 2, H], U8)
-        w8_raw = held("w8_raw", [P, 2, H], I32)
-        w8s_raw = held("w8s_raw", [P, H], U8)
+        w4s_raw = held("w4s_raw", [32, H], U8)
+        w8s_raw = held("w8s_raw", [32, H], U8)
+        planes = held("planes", [P, 2, ROW], U8)
         bias_rows = held("bias_rows", [P, P], F32)
         ident = held("ident", [P, P], F32)
         bias = held("bias", [P, 8], F32)
         warm = held("warm", [P, 8], F32)
 
-        nc.vector.memset(tab2_s[:].bitcast(I32), 0)
-        nc.vector.memset(tab_s[:].bitcast(I32), 0)
+        for window in (tab_s, tab2_s):
+            nc.vector.memset(window[32:64, :].bitcast(I32), 0)
+            nc.vector.memset(window[64:128, :].bitcast(I32), 0)
+        nc.vector.memset(planes[:].bitcast(I32), 0)
         nc.gpsimd.memset(warm[:], 0.0)
-        nc.gpsimd.memset(w4s_raw[:].bitcast(I32), 0)
         nc.gpsimd.memset(bias_rows[:], 0.0)
-        nc.gpsimd.memset(w8s_raw[:].bitcast(I32), 0)
         make_identity(nc, ident[:])
         nc.scalar.activation(warm[:, 4:8], warm[:, 0:4], RELU)
 
         def load(dst, src):
             nc.sync.dma_start(dst, src)
 
-        def load_tab_words(a, half):
-            cols = slice(half * T // 2, (half + 1) * T // 2)
-            load(tab_w[a][:, cols], tab_words[a].rearrange("p t i -> p (t i)").bitcast(I32)[:, cols])
+        def load_scale_rows(dst, scales):
+            load(dst[0:32, :].bitcast(I32), scales.rearrange("a q n -> (a q) n").bitcast(I32))
 
-        def load_side_by_side(dst, scales, q):
-            load(dst[32 * q : 32 * q + 4, :, :].bitcast(I32), scales[:, 4 * q : 4 * q + 4, :].rearrange("a r n -> r a n").bitcast(I32))
+        tab_w = {}
 
-        def load_stacked(dst, scales, q):
-            load(dst[32 * q : 32 * q + 8, :].bitcast(I32), scales[:, 4 * q : 4 * q + 4, :].bitcast(I32))
+        def load_tab_words(a):
+            tab_w[a] = slot("tab_w", [P, T], I32, "slot_c" if a == 1 else "slot_d")
+            load(tab_w[a][:], tab_words[a].rearrange("p t i -> p (t i)").bitcast(I32))
 
         w1_raw = {}
 
-        def load_w1(a, b):
-            w1_raw[a, b] = ring.tile([P, 4, 512], F32, name="w1_raw", bufs=3)
+        def load_w1(a, b, tag):
+            w1_raw[a, b] = slot("w1_raw", [P, 4, 512], F32, tag)
             load(w1_raw[a, b][:], w1[512 * a : 512 * (a + 1), 512 * b : 512 * (b + 1)].rearrange("(p j) c -> p j c", j=4))
 
-        wo_raw = [held("wo_raw%d" % b, [P, 4, N], F32) for b in range(2)]
-
-        def load_wo(b, t):
-            load(wo_raw[b][:, t, :], wo[512 * b : 512 * (b + 1), :].rearrange("(q t i) n -> t q i n", t=4, i=8)[t])
-
-        load(tab2_w[:], tab2_words.rearrange("a p t i -> p a (t i)").bitcast(I32))
-        load(offs2_t[:], offs2)
-        load_stacked(tab2_s, tab2_scales, 0)
-        load_stacked(tab2_s, tab2_scales, 1)
-        load_tab_words(0, 0)
-        load_stacked(tab2_s, tab2_scales, 2)
-        load_stacked(tab2_s, tab2_scales, 3)
         load(offs_t[:], offs)
-        load_tab_words(0, 1)
-        for q in range(3):
-            load_side_by_side(tab_s, tab_scales, q)
-        load_w1(0, 0)
-        load_side_by_side(tab_s, tab_scales, 3)
+        load_scale_rows(tab_s, tab_scales)
+        load(offs2_t[:], offs2)
+        load_scale_rows(tab2_s, tab2_scales)
+        load(tab2_w[:], tab2_words.rearrange("a p t i -> p a (t i)").bitcast(I32))
+        load_scale_rows(w4s_raw, w4_scales)
+        load_scale_rows(w8s_raw, w8_scales)
+        load_tab_words(0)
         load(w4_raw[:].bitcast(I32), w4_words.rearrange("a p e -> p a e").bitcast(I32))
-        load_side_by_side(w4s_raw, w4_scales, 0)
-        load_w1(1, 0)
-        for q in range(1, 4):
-            load_side_by_side(w4s_raw, w4_scales, q)
-        load_tab_words(1, 0)
+        load_w1(0, 0, "slot_a")
+        load(pos_t[:], pos1)
         for b in range(2):
             load(bias_rows[4 * b : 4 * b + 4, :], b1[512 * b : 512 * (b + 1)].rearrange("(q t i) -> t q i", t=4, i=8))
-        load(pos_t[:], pos1)
-        load_tab_words(1, 1)
-        load(w8_raw[:], w8_words.rearrange("a p e i -> p a (e i)").bitcast(I32))
-        for q in range(4):
-            load_stacked(w8s_raw, w8_scales, q)
-        load_w1(0, 1)
-        load_w1(1, 1)
-        for b in range(2):
-            for t in range(4):
-                load_wo(b, t)
+
+        load_w1(1, 0, "slot_b")
+        stage = held("stage", [32, ROW], U8)
+        v_s = held("v_s", [P, S], U8)
+        v2_s = held("v2_s", [P, M], U8)
+        nc.vector.tensor_copy(v_s[:], tab_s[:].indirect(offs_t[:]))
+        nc.vector.tensor_copy(v2_s[:], tab2_s[:].indirect(offs2_t[:]))
+        for raw, at in ((w4s_raw, W4_AT), (w8s_raw, W8_AT)):
+            nc.vector.tensor_copy(stage[:, at : at + H].bitcast(I32).rearrange("p (b t q i) -> p b t q i", b=2, t=4, i=2),
+                                  raw[:].bitcast(I32).rearrange("p (b q t i) -> p b t q i", b=2, t=4, i=2))
+        nc.vector.tensor_copy(stage[:, V_AT : V_AT + S].bitcast(I32), v_s[0:32, :].bitcast(I32))
+        nc.vector.tensor_copy(stage[:, V2_AT : V2_AT + M].bitcast(I32), v2_s[0:32, :].bitcast(I32))
+        for a in range(2):
+            for r in range(4):
+                nc.scalar.dma_start(planes[r:P:32, a, :].bitcast(I32), stage[16 * a + r : 16 * a + 16 : 4, :].bitcast(I32))
 
         v2_w = [held("v2_w%d" % a, [P, M], U32) for a in range(2)]
-        v2_s = held("v2_s", [P, M], U8)
         for a in range(2):
             nc.vector.tensor_copy(v2_w[a][:], tab2_w[:, a, :].bitcast(U32).indirect(offs2_t[:]))
-        nc.vector.tensor_copy(v2_s[:], tab2_s[:].indirect(offs2_t[:]))
 
-        v_s = [held("v_s%d" % a, [P, S], U8) for a in range(2)]
         v_w = {(a, hf): held("v_w%d%d" % (a, hf), [P, BANK], U32) for a in range(2) for hf in range(2)}
 
         def gather_words(a, hf):
             nc.vector.tensor_copy(v_w[a, hf][:], tab_w[a][:].bitcast(U32).indirect(offs_t[:, 32 * hf : 32 * (hf + 1)]))
 
-        nc.vector.tensor_copy(v_s[0][:], tab_s[:, 0, :].indirect(offs_t[:]))
         gather_words(0, 0)
         gather_words(0, 1)
-        nc.vector.tensor_copy(v_s[1][:], tab_s[:, 1, :].indirect(offs_t[:]))
+        load_tab_words(1)
 
         bias_ps = psum.tile([P, BANK], F32, name="bias_ps", tag="pb", bufs=2)
         nc.tensor.transpose(bias_ps[:, 0:P], bias_rows[:], ident[:])
         nc.scalar.copy(bias[:], bias_ps[:, 0:8])
 
         w4_p = [held("w4_p%d" % b, [P, 2, H], U8) for b in range(2)]
-        w4s_p = [held("w4s_p%d" % b, [P, 2, H // 2], U8) for b in range(2)]
         w8_p = [held("w8_p%d" % b, [P, 2, H // 2], I32) for b in range(2)]
-        w8s_p = held("w8s_p", [P, H], U8)
 
         def reorder(dst, src, b, run):
             width = 64 * run
@@ -147,31 +135,28 @@ def tile_list_excess_delay_causes_kernel(tc, tab_words, tab_scales, offs, pos1, 
 
         def reorder_w4(b):
             reorder(w4_p[b][:].bitcast(I32), w4_raw[:].bitcast(I32), b, 4)
-            reorder(w4s_p[b][:].bitcast(I32), w4s_raw[:].bitcast(I32), b, 2)
-
-        def reorder_w8_scales():
-            nc.vector.tensor_copy(w8s_p[:].bitcast(I32).rearrange("p (b t q i) -> p b t q i", b=2, t=4, i=2),
-                                  w8s_raw[:].bitcast(I32).rearrange("p (b q t i) -> p b t q i", b=2, t=4, i=2))
 
         w1_c = {(a, b): held("w1_c%d%d" % (a, b), [P, 512], U32) for a in range(2) for b in range(2)}
         w1_s = {(a, b): held("w1_s%d%d" % (a, b), [P, 512], U8) for a in range(2) for b in range(2)}
         w1_g = {}
 
         def cast_w1(a, b, t):
-            w1_g[a, b, t] = ring.tile([P, 512], BF16, name="w1_g", bufs=8, align_bytes=64)
-            nc.scalar.copy(w1_g[a, b, t][:].rearrange("p (q u i j) -> p q u j i", u=2, i=4, j=4),
-                           w1_raw[a, b][:].rearrange("p j (q t u i) -> p t q u j i", t=4, u=2, i=4)[:, t])
+            if t == 0:
+                w1_g[a, b] = ring.tile([P, 2048], BF16, name="w1_g", bufs=2, align_bytes=64)
+            copy = nc.vector.tensor_copy if b == 0 else nc.scalar.copy
+            copy(w1_g[a, b][:, 512 * t : 512 * (t + 1)].rearrange("p (q u i j) -> p q u j i", u=2, i=4, j=4),
+                 w1_raw[a, b][:].rearrange("p j (q t u i) -> p t q u j i", t=4, u=2, i=4)[:, t])
 
-        def quantize_w1(a, b, t):
-            cols = slice(P * t, P * (t + 1))
-            nc.vector.quantize_mx(out=w1_c[a, b][:, cols].bitcast(FP8X4), scales=w1_s[a, b][:, cols], in_=w1_g[a, b, t][:])
+        def quantize_w1(a, b, lo, hi):
+            cols = slice(P * lo, P * hi)
+            nc.vector.quantize_mx(out=w1_c[a, b][:, cols].bitcast(FP8X4), scales=w1_s[a, b][:, cols], in_=w1_g[a, b][:, 512 * lo : 512 * hi])
 
         wo_g = held("wo_g", [P, 2, N, 4], BF16)
         wo_c = held("wo_c", [P, 2 * N], U32)
         wo_s = held("wo_s", [P, 2 * N], U8)
 
         def cast_wo(b):
-            nc.scalar.copy(wo_g[:, b].rearrange("p (c i) t -> p c t i", i=4), wo_raw[b][:].rearrange("p t (c i) -> p c t i", i=4))
+            nc.scalar.copy(wo_g[:, b].rearrange("p (c i) t -> p c t i", i=4), wo_raw[:, b].rearrange("p t (c i) -> p c t i", i=4))
 
         def quantize_wo():
             flat = wo_g[:].rearrange("p b n t -> p (b n t)")
@@ -179,17 +164,21 @@ def tile_list_excess_delay_causes_kernel(tc, tab_words, tab_scales, offs, pos1, 
                 nc.vector.quantize_mx(out=wo_c[:, lo:hi].bitcast(FP8X4), scales=wo_s[:, lo:hi], in_=flat[:, 4 * lo : 4 * hi])
 
         reorder_w4(0)
-        for t in range(4):
-            cast_w1(0, 0, t)
-        for t in range(4):
-            cast_w1(1, 0, t)
-        for t in range(4):
-            quantize_w1(0, 0, t)
-        for t in range(4):
-            quantize_w1(1, 0, t)
         reorder_w4(1)
+        for a in range(2):
+            for t in range(4):
+                cast_w1(a, 0, t)
+            quantize_w1(a, 0, 0, 4)
         gather_words(1, 0)
         gather_words(1, 1)
+
+        w8_raw = slot("w8_raw", [P, 2, H], I32, "slot_a")
+        load(w8_raw[:], w8_words.rearrange("a p e i -> p a (e i)").bitcast(I32))
+        wo_raw = slot("wo_raw", [P, 2, 4, N], F32, "slot_c")
+        for b in range(2):
+            for t in range(4):
+                load(wo_raw[:, b, t, :], wo[512 * b : 512 * (b + 1), :].rearrange("(q t i) n -> t q i n", t=4, i=8)[t])
+        load_w1(0, 1, "slot_b")
 
         x_pre = {}
         picked = {}
@@ -203,10 +192,10 @@ def tile_list_excess_delay_causes_kernel(tc, tab_words, tab_scales, offs, pos1, 
             p4 = psum.tile([P, BANK], F32, name="p4", tag="p4")
             for a in range(2):
                 nc.tensor.matmul_mx(out=p1[:], lhsT=w1_c[a, b][:, cols].bitcast(FP8X4), lhsT_scale=w1_s[a, b][:, cols],
-                                    rhs=v_w[a, hf][:].bitcast(FP8X4), rhs_scale=v_s[a][:, jc], start=(a == 0), stop=(a == 1))
+                                    rhs=v_w[a, hf][:].bitcast(FP8X4), rhs_scale=planes[:, a, V_AT + BANK * hf : V_AT + BANK * (hf + 1)], start=(a == 0), stop=(a == 1))
             for a in range(2):
-                nc.tensor.matmul_mx(out=p4[:], lhsT=w4_p[b][:, a, 2 * P * t : 2 * P * (t + 1)].bitcast(FP4X4), lhsT_scale=w4s_p[b][:, a, cols],
-                                    rhs=v_w[a, hf][:].bitcast(FP8X4), rhs_scale=v_s[a][:, jc], start=(a == 0), stop=(a == 1))
+                nc.tensor.matmul_mx(out=p4[:], lhsT=w4_p[b][:, a, 2 * P * t : 2 * P * (t + 1)].bitcast(FP4X4), lhsT_scale=planes[:, a, W4_AT + 512 * b + P * t : W4_AT + 512 * b + P * (t + 1)],
+                                    rhs=v_w[a, hf][:].bitcast(FP8X4), rhs_scale=planes[:, a, V_AT + BANK * hf : V_AT + BANK * (hf + 1)], start=(a == 0), stop=(a == 1))
             c = ring.tile([P, BANK], F32, name="c", bufs=3)
             nc.scalar.activation(c[:], p1[:], RELU, bias=bias[:, 4 * b + t : 4 * b + t + 1])
             if hf == 0:
@@ -217,8 +206,8 @@ def tile_list_excess_delay_causes_kernel(tc, tab_words, tab_scales, offs, pos1, 
             own[b, t] = psum.tile([P, BANK], F32, name="own", tag="pb", bufs=2)
             for a in range(2):
                 nc.tensor.matmul_mx(out=own[b, t][:], lhsT=w8_p[b][:, a, P * t : P * (t + 1)].bitcast(FP8X4),
-                                    lhsT_scale=w8s_p[4 * a : P, 512 * b + P * t : 512 * b + P * (t + 1)],
-                                    rhs=v2_w[a][:].bitcast(FP8X4), rhs_scale=v2_s[4 * a : P, :], start=(a == 0), stop=(a == 1))
+                                    lhsT_scale=planes[:, a, W8_AT + 512 * b + P * t : W8_AT + 512 * b + P * (t + 1)],
+                                    rhs=v2_w[a][:].bitcast(FP8X4), rhs_scale=planes[:, a, V2_AT : V2_AT + M], start=(a == 0), stop=(a == 1))
 
         def pick(b, t, lo, hi):
             picked[b, t, lo] = ring.tile([P, hi - lo], F32, name="picked", bufs=3)
@@ -251,26 +240,24 @@ def tile_list_excess_delay_causes_kernel(tc, tab_words, tab_scales, offs, pos1, 
         tiles = [(b, t) for b in range(2) for t in range(4)]
         for n, (b, t) in enumerate(tiles):
             caller_half(b, t, 0)
-            if n == 0:
-                reorder_w8_scales()
-                reorder(w8_p[0][:], w8_raw[:], 0, 8)
-            else:
+            if n > 0:
                 callee_product(*tiles[n - 1])
                 pick(*tiles[n - 1], 0, M)
             if n in (1, 2):
                 for tt in range(2):
                     cast_w1(n - 1, 1, tt)
             caller_half(b, t, 1)
+            if n == 0:
+                reorder(w8_p[0][:], w8_raw[:], 0, 8)
+                reorder(w8_p[1][:], w8_raw[:], 1, 8)
+                load_w1(1, 1, "slot_a")
             if n > 0:
                 subtract(*tiles[n - 1], 0, M)
             if n in (1, 2):
                 for tt in range(2, 4):
                     cast_w1(n - 1, 1, tt)
             if n in (2, 3):
-                for tt in range(4):
-                    quantize_w1(n - 2, 1, tt)
-            if n == 3:
-                reorder(w8_p[1][:], w8_raw[:], 1, 8)
+                quantize_w1(n - 2, 1, 0, 4)
             if n == 4:
                 relu_scalar(0, 0, M)
             if n in (5, 6):

@@ -41,12 +41,12 @@ def tile_list_excess_delay_causes_kernel(tc, tab_words, tab_scales, offs, pos1, 
             return keep.tile(shape, dtype, name=name, tag=tag, align_bytes=64)
 
         tab_s = held("tab_s", [P, T], U8)
-        tab2_w = slot("tab2_w", [P, 2, T2], I32, "slot_c")
+        tab2_w = slot("tab2_w", [P, 2, T2], I32, "slot_d")
         tab2_s = held("tab2_s", [P, T2], U8)
-        w4_raw = held("w4_raw", [P, 2, 2 * H], U8)
+        w4_raw = slot("w4_raw", [P, 2, 2 * H], U8, "slot_b")
         w4s_raw = held("w4s_raw", [32, H], U8)
         w8s_raw = held("w8s_raw", [32, H], U8)
-        planes = held("planes", [P, 2, ROW], U8)
+        planes = {0: held("plane0", [P, ROW], U8)}
         bias_rows = held("bias_rows", [P, P], F32)
         ident = held("ident", [P, P], F32)
         bias = held("bias", [P, 8], F32)
@@ -55,9 +55,9 @@ def tile_list_excess_delay_causes_kernel(tc, tab_words, tab_scales, offs, pos1, 
         for window in (tab_s, tab2_s):
             nc.vector.memset(window[32:64, :].bitcast(I32), 0)
             nc.vector.memset(window[64:128, :].bitcast(I32), 0)
-        nc.vector.memset(planes[:].bitcast(I32), 0)
-        nc.gpsimd.memset(warm[:], 0.0)
         nc.gpsimd.memset(bias_rows[:], 0.0)
+        nc.gpsimd.memset(warm[:], 0.0)
+        nc.gpsimd.memset(planes[0][:].bitcast(I32), 0)
         make_identity(nc, ident[:])
         nc.scalar.activation(warm[:, 4:8], warm[:, 0:4], RELU)
 
@@ -70,7 +70,7 @@ def tile_list_excess_delay_causes_kernel(tc, tab_words, tab_scales, offs, pos1, 
         tab_w = {}
 
         def load_tab_words(a):
-            tab_w[a] = slot("tab_w", [P, T], I32, "slot_c" if a == 1 else "slot_d")
+            tab_w[a] = slot("tab_w", [P, T], I32, "slot_c")
             load(tab_w[a][:], tab_words[a].rearrange("p t i -> p (t i)").bitcast(I32))
 
         w1_raw = {}
@@ -83,17 +83,16 @@ def tile_list_excess_delay_causes_kernel(tc, tab_words, tab_scales, offs, pos1, 
         load_scale_rows(tab_s, tab_scales)
         load(offs2_t[:], offs2)
         load_scale_rows(tab2_s, tab2_scales)
-        load(tab2_w[:], tab2_words.rearrange("a p t i -> p a (t i)").bitcast(I32))
         load_scale_rows(w4s_raw, w4_scales)
         load_scale_rows(w8s_raw, w8_scales)
-        load_tab_words(0)
         load(w4_raw[:].bitcast(I32), w4_words.rearrange("a p e -> p a e").bitcast(I32))
-        load_w1(0, 0, "slot_a")
-        load(pos_t[:], pos1)
+        load(tab2_w[:], tab2_words.rearrange("a p t i -> p a (t i)").bitcast(I32))
         for b in range(2):
             load(bias_rows[4 * b : 4 * b + 4, :], b1[512 * b : 512 * (b + 1)].rearrange("(q t i) -> t q i", t=4, i=8))
+        load_tab_words(0)
+        load(pos_t[:], pos1)
+        load_w1(0, 0, "slot_a")
 
-        load_w1(1, 0, "slot_b")
         stage = held("stage", [32, ROW], U8)
         v_s = held("v_s", [P, S], U8)
         v2_s = held("v2_s", [P, M], U8)
@@ -104,13 +103,32 @@ def tile_list_excess_delay_causes_kernel(tc, tab_words, tab_scales, offs, pos1, 
                                   raw[:].bitcast(I32).rearrange("p (b q t i) -> p b t q i", b=2, t=4, i=2))
         nc.vector.tensor_copy(stage[:, V_AT : V_AT + S].bitcast(I32), v_s[0:32, :].bitcast(I32))
         nc.vector.tensor_copy(stage[:, V2_AT : V2_AT + M].bitcast(I32), v2_s[0:32, :].bitcast(I32))
-        for a in range(2):
-            for r in range(4):
-                nc.scalar.dma_start(planes[r:P:32, a, :].bitcast(I32), stage[16 * a + r : 16 * a + 16 : 4, :].bitcast(I32))
 
+        def move_scale_rows(a):
+            for r in range(4):
+                nc.scalar.dma_start(planes[a][r:P:32, :].bitcast(I32), stage[16 * a + r : 16 * a + 16 : 4, :].bitcast(I32))
+
+        move_scale_rows(0)
+        w4_p = [held("w4_p%d" % b, [P, 2, H], U8) for b in range(2)]
+        w8_p = [held("w8_p%d" % b, [P, 2, H // 2], I32) for b in range(2)]
+
+        def reorder(dst, src, b, run):
+            width = 64 * run
+            nc.vector.tensor_copy(dst.rearrange("p a (t q i) -> p a t q i", t=4, i=run),
+                                  src[:, :, b * width : (b + 1) * width].rearrange("p a (q t i) -> p a t q i", t=4, i=run))
+
+        def reorder_w4(b):
+            reorder(w4_p[b][:].bitcast(I32), w4_raw[:].bitcast(I32), b, 4)
+
+        reorder_w4(0)
+        reorder_w4(1)
+        load_w1(1, 0, "slot_b")
         v2_w = [held("v2_w%d" % a, [P, M], U32) for a in range(2)]
         for a in range(2):
             nc.vector.tensor_copy(v2_w[a][:], tab2_w[:, a, :].bitcast(U32).indirect(offs2_t[:]))
+        planes[1] = slot("plane1", [P, ROW], U8, "slot_d")
+        nc.gpsimd.memset(planes[1][:].bitcast(I32), 0)
+        move_scale_rows(1)
 
         v_w = {(a, hf): held("v_w%d%d" % (a, hf), [P, BANK], U32) for a in range(2) for hf in range(2)}
 
@@ -125,17 +143,6 @@ def tile_list_excess_delay_causes_kernel(tc, tab_words, tab_scales, offs, pos1, 
         nc.tensor.transpose(bias_ps[:, 0:P], bias_rows[:], ident[:])
         nc.scalar.copy(bias[:], bias_ps[:, 0:8])
 
-        w4_p = [held("w4_p%d" % b, [P, 2, H], U8) for b in range(2)]
-        w8_p = [held("w8_p%d" % b, [P, 2, H // 2], I32) for b in range(2)]
-
-        def reorder(dst, src, b, run):
-            width = 64 * run
-            nc.vector.tensor_copy(dst.rearrange("p a (t q i) -> p a t q i", t=4, i=run),
-                                  src[:, :, b * width : (b + 1) * width].rearrange("p a (q t i) -> p a t q i", t=4, i=run))
-
-        def reorder_w4(b):
-            reorder(w4_p[b][:].bitcast(I32), w4_raw[:].bitcast(I32), b, 4)
-
         w1_c = {(a, b): held("w1_c%d%d" % (a, b), [P, 512], U32) for a in range(2) for b in range(2)}
         w1_s = {(a, b): held("w1_s%d%d" % (a, b), [P, 512], U8) for a in range(2) for b in range(2)}
         w1_g = {}
@@ -143,8 +150,7 @@ def tile_list_excess_delay_causes_kernel(tc, tab_words, tab_scales, offs, pos1, 
         def cast_w1(a, b, t):
             if t == 0:
                 w1_g[a, b] = ring.tile([P, 2048], BF16, name="w1_g", bufs=2, align_bytes=64)
-            copy = nc.vector.tensor_copy if b == 0 else nc.scalar.copy
-            copy(w1_g[a, b][:, 512 * t : 512 * (t + 1)].rearrange("p (q u i j) -> p q u j i", u=2, i=4, j=4),
+            nc.scalar.copy(w1_g[a, b][:, 512 * t : 512 * (t + 1)].rearrange("p (q u i j) -> p q u j i", u=2, i=4, j=4),
                  w1_raw[a, b][:].rearrange("p j (q t u i) -> p t q u j i", t=4, u=2, i=4)[:, t])
 
         def quantize_w1(a, b, lo, hi):
@@ -163,8 +169,6 @@ def tile_list_excess_delay_causes_kernel(tc, tab_words, tab_scales, offs, pos1, 
             for lo, hi in ((0, 512), (512, 768)):
                 nc.vector.quantize_mx(out=wo_c[:, lo:hi].bitcast(FP8X4), scales=wo_s[:, lo:hi], in_=flat[:, 4 * lo : 4 * hi])
 
-        reorder_w4(0)
-        reorder_w4(1)
         for a in range(2):
             for t in range(4):
                 cast_w1(a, 0, t)
@@ -172,13 +176,9 @@ def tile_list_excess_delay_causes_kernel(tc, tab_words, tab_scales, offs, pos1, 
         gather_words(1, 0)
         gather_words(1, 1)
 
-        w8_raw = slot("w8_raw", [P, 2, H], I32, "slot_a")
+        w8_raw = slot("w8_raw", [P, 2, H], I32, "slot_b")
         load(w8_raw[:], w8_words.rearrange("a p e i -> p a (e i)").bitcast(I32))
-        wo_raw = slot("wo_raw", [P, 2, 4, N], F32, "slot_c")
-        for b in range(2):
-            for t in range(4):
-                load(wo_raw[:, b, t, :], wo[512 * b : 512 * (b + 1), :].rearrange("(q t i) n -> t q i n", t=4, i=8)[t])
-        load_w1(0, 1, "slot_b")
+        load_w1(0, 1, "slot_c")
 
         x_pre = {}
         picked = {}
@@ -192,10 +192,10 @@ def tile_list_excess_delay_causes_kernel(tc, tab_words, tab_scales, offs, pos1, 
             p4 = psum.tile([P, BANK], F32, name="p4", tag="p4")
             for a in range(2):
                 nc.tensor.matmul_mx(out=p1[:], lhsT=w1_c[a, b][:, cols].bitcast(FP8X4), lhsT_scale=w1_s[a, b][:, cols],
-                                    rhs=v_w[a, hf][:].bitcast(FP8X4), rhs_scale=planes[:, a, V_AT + BANK * hf : V_AT + BANK * (hf + 1)], start=(a == 0), stop=(a == 1))
+                                    rhs=v_w[a, hf][:].bitcast(FP8X4), rhs_scale=planes[a][:, V_AT + BANK * hf : V_AT + BANK * (hf + 1)], start=(a == 0), stop=(a == 1))
             for a in range(2):
-                nc.tensor.matmul_mx(out=p4[:], lhsT=w4_p[b][:, a, 2 * P * t : 2 * P * (t + 1)].bitcast(FP4X4), lhsT_scale=planes[:, a, W4_AT + 512 * b + P * t : W4_AT + 512 * b + P * (t + 1)],
-                                    rhs=v_w[a, hf][:].bitcast(FP8X4), rhs_scale=planes[:, a, V_AT + BANK * hf : V_AT + BANK * (hf + 1)], start=(a == 0), stop=(a == 1))
+                nc.tensor.matmul_mx(out=p4[:], lhsT=w4_p[b][:, a, 2 * P * t : 2 * P * (t + 1)].bitcast(FP4X4), lhsT_scale=planes[a][:, W4_AT + 512 * b + P * t : W4_AT + 512 * b + P * (t + 1)],
+                                    rhs=v_w[a, hf][:].bitcast(FP8X4), rhs_scale=planes[a][:, V_AT + BANK * hf : V_AT + BANK * (hf + 1)], start=(a == 0), stop=(a == 1))
             c = ring.tile([P, BANK], F32, name="c", bufs=3)
             nc.scalar.activation(c[:], p1[:], RELU, bias=bias[:, 4 * b + t : 4 * b + t + 1])
             if hf == 0:
@@ -206,11 +206,11 @@ def tile_list_excess_delay_causes_kernel(tc, tab_words, tab_scales, offs, pos1, 
             own[b, t] = psum.tile([P, BANK], F32, name="own", tag="pb", bufs=2)
             for a in range(2):
                 nc.tensor.matmul_mx(out=own[b, t][:], lhsT=w8_p[b][:, a, P * t : P * (t + 1)].bitcast(FP8X4),
-                                    lhsT_scale=planes[:, a, W8_AT + 512 * b + P * t : W8_AT + 512 * b + P * (t + 1)],
-                                    rhs=v2_w[a][:].bitcast(FP8X4), rhs_scale=planes[:, a, V2_AT : V2_AT + M], start=(a == 0), stop=(a == 1))
+                                    lhsT_scale=planes[a][:, W8_AT + 512 * b + P * t : W8_AT + 512 * b + P * (t + 1)],
+                                    rhs=v2_w[a][:].bitcast(FP8X4), rhs_scale=planes[a][:, V2_AT : V2_AT + M], start=(a == 0), stop=(a == 1))
 
         def pick(b, t, lo, hi):
-            picked[b, t, lo] = ring.tile([P, hi - lo], F32, name="picked", bufs=3)
+            picked[b, t, lo] = ring.tile([P, hi - lo], F32, name="picked", bufs=4)
             nc.vector.tensor_copy(picked[b, t, lo][:], x_pre[b, t][:].indirect(pos_t[:, lo // 16 : hi // 16]))
 
         def subtract(b, t, lo, hi):
@@ -250,12 +250,17 @@ def tile_list_excess_delay_causes_kernel(tc, tab_words, tab_scales, offs, pos1, 
             if n == 0:
                 reorder(w8_p[0][:], w8_raw[:], 0, 8)
                 reorder(w8_p[1][:], w8_raw[:], 1, 8)
-                load_w1(1, 1, "slot_a")
+                load_w1(1, 1, "slot_b")
             if n > 0:
                 subtract(*tiles[n - 1], 0, M)
             if n in (1, 2):
                 for tt in range(2, 4):
                     cast_w1(n - 1, 1, tt)
+            if n == 1:
+                wo_raw = slot("wo_raw", [P, 2, 4, N], F32, "slot_c")
+                for bb in range(2):
+                    for tt in range(4):
+                        load(wo_raw[:, bb, tt, :], wo[512 * bb : 512 * (bb + 1), :].rearrange("(q t i) n -> t q i n", t=4, i=8)[tt])
             if n in (2, 3):
                 quantize_w1(n - 2, 1, 0, 4)
             if n == 4:
@@ -265,32 +270,42 @@ def tile_list_excess_delay_causes_kernel(tc, tab_words, tab_scales, offs, pos1, 
             if n == 5:
                 quantize_h(0, 0, M)
 
-        half = M // 2
         callee_product(1, 3)
         quantize_wo()
-        pick(1, 3, 0, half)
-        pick(1, 3, half, M)
-        subtract(1, 3, 0, half)
-        relu_scalar(1, 0, half)
-        subtract(1, 3, half, M)
-        scores = {}
-        for hf in range(2):
+        chunks = ((0, 256), (256, 384), (384, 512))
+        pick(1, 3, *chunks[0])
+        pick(1, 3, *chunks[1])
+        subtract(1, 3, *chunks[0])
+        relu_scalar(1, *chunks[0])
+        pick(1, 3, *chunks[2])
+        subtract(1, 3, *chunks[1])
+        relu_scalar(1, *chunks[1])
+        subtract(1, 3, *chunks[2])
+        relu_vector(1, *chunks[2])
+
+        def score_pass(dst, b, c3, lo, hi):
+            cols = slice(N * b + P * c3, N * b + P * (c3 + 1))
+            codes, scales = (h_c[0, 0][:, lo:hi], h_s[0, 0][:, lo:hi]) if b == 0 else (h_c[1, lo][:], h_s[1, lo][:])
+            nc.tensor.matmul_mx(out=dst, lhsT=wo_c[:, cols].bitcast(FP8X4), lhsT_scale=wo_s[:, cols],
+                                rhs=codes.bitcast(FP8X4), rhs_scale=scales, start=(b == 0), stop=(b == 1))
+
+        out_rows = out.rearrange("(c p) m -> p c m", p=P)
+        wide = [psum.tile([P, BANK], F32, name="wide", tag="p1") for c3 in range(3)]
+        for c3 in range(3):
+            score_pass(wide[c3][:, 0:256], 0, c3, *chunks[0])
+        quantize_h(1, *chunks[0])
+        staged = held("staged0", [P, 3, 256], F32)
+        for c3 in range(3):
+            score_pass(wide[c3][:, 0:256], 1, c3, *chunks[0])
+            nc.scalar.copy(staged[:, c3, :], wide[c3][:, 0:256])
+        nc.sync.dma_start(out_rows[:, :, 0:256], staged[:])
+        for lo, hi in (chunks[2], chunks[1]):
+            quantize_h(1, lo, hi)
+        for lo, hi in (chunks[2], chunks[1]):
+            narrow = psum.tile([P, BANK], F32, name="narrow", tag="p4")
             for c3 in range(3):
-                scores[hf, c3] = psum.tile([P, BANK], F32, name="scores", tag="p1" if hf == 0 else "p4")
-                nc.tensor.matmul_mx(out=scores[hf, c3][:, 0:half], lhsT=wo_c[:, P * c3 : P * (c3 + 1)].bitcast(FP8X4), lhsT_scale=wo_s[:, P * c3 : P * (c3 + 1)],
-                                    rhs=h_c[0, 0][:, half * hf : half * (hf + 1)].bitcast(FP8X4), rhs_scale=h_s[0, 0][:, half * hf : half * (hf + 1)],
-                                    start=True, stop=False)
-        relu_vector(1, half, M)
-        quantize_h(1, 0, half)
-        quantize_h(1, half, M)
-        for hf in range(2):
-            staged = held("staged%d" % hf, [P, 3, half], F32)
-            for c3 in range(3):
-                cols = slice(N + P * c3, N + P * (c3 + 1))
-                nc.tensor.matmul_mx(out=scores[hf, c3][:, 0:half], lhsT=wo_c[:, cols].bitcast(FP8X4), lhsT_scale=wo_s[:, cols],
-                                    rhs=h_c[1, half * hf][:].bitcast(FP8X4), rhs_scale=h_s[1, half * hf][:], start=False, stop=True)
-                if hf == 1 and c3 == 1:
-                    nc.vector.tensor_copy(staged[:, c3, :], scores[hf, c3][:, 0:half])
-                else:
-                    nc.scalar.copy(staged[:, c3, :], scores[hf, c3][:, 0:half])
-            nc.sync.dma_start(out.rearrange("(c p) m -> p c m", p=P)[:, :, half * hf : half * (hf + 1)], staged[:])
+                for b in range(2):
+                    score_pass(narrow[:, P * c3 : P * (c3 + 1)], b, c3, lo, hi)
+            staged = held("staged%d" % lo, [P, 3, P], F32)
+            nc.vector.tensor_copy(staged[:].rearrange("p c m -> p (c m)"), narrow[:, 0 : 3 * P])
+            nc.sync.dma_start(out_rows[:, :, lo:hi], staged[:])

@@ -43,7 +43,6 @@ def tile_list_excess_delay_causes_kernel(tc, tab_words, tab_scales, offs, pos1, 
         tab_s = held("tab_s", [P, T], U8)
         tab2_w = slot("tab2_w", [P, 2, T2], I32, "slot_d")
         tab2_s = held("tab2_s", [P, T2], U8)
-        w4_raw = slot("w4_raw", [P, 2, 2 * H], U8, "slot_b")
         w4s_raw = held("w4s_raw", [32, H], U8)
         w8s_raw = held("w8s_raw", [32, H], U8)
         planes = {0: held("plane0", [P, ROW], U8)}
@@ -73,6 +72,12 @@ def tile_list_excess_delay_causes_kernel(tc, tab_words, tab_scales, offs, pos1, 
             tab_w[a] = slot("tab_w", [P, T], I32, "slot_c")
             load(tab_w[a][:], tab_words[a].rearrange("p t i -> p (t i)").bitcast(I32))
 
+        w4_raw = {}
+
+        def load_w4(b, tag):
+            w4_raw[b] = slot("w4_raw", [P, 2, H], U8, tag)
+            load(w4_raw[b][:].bitcast(I32), w4_words[:, :, H * b : H * (b + 1)].rearrange("a p e -> p a e").bitcast(I32))
+
         w1_raw = {}
 
         def load_w1(a, b, tag):
@@ -85,7 +90,7 @@ def tile_list_excess_delay_causes_kernel(tc, tab_words, tab_scales, offs, pos1, 
         load_scale_rows(tab2_s, tab2_scales)
         load_scale_rows(w4s_raw, w4_scales)
         load_scale_rows(w8s_raw, w8_scales)
-        load(w4_raw[:].bitcast(I32), w4_words.rearrange("a p e -> p a e").bitcast(I32))
+        load_w4(0, "slot_b")
         load(tab2_w[:], tab2_words.rearrange("a p t i -> p a (t i)").bitcast(I32))
         for b in range(2):
             load(bias_rows[4 * b : 4 * b + 4, :], b1[512 * b : 512 * (b + 1)].rearrange("(q t i) -> t q i", t=4, i=8))
@@ -118,10 +123,9 @@ def tile_list_excess_delay_causes_kernel(tc, tab_words, tab_scales, offs, pos1, 
                                   src[:, :, b * width : (b + 1) * width].rearrange("p a (q t i) -> p a t q i", t=4, i=run))
 
         def reorder_w4(b):
-            reorder(w4_p[b][:].bitcast(I32), w4_raw[:].bitcast(I32), b, 4)
+            reorder(w4_p[b][:].bitcast(I32), w4_raw[b][:].bitcast(I32), 0, 4)
 
         reorder_w4(0)
-        reorder_w4(1)
         load_w1(1, 0, "slot_b")
         v2_w = [held("v2_w%d" % a, [P, M], U32) for a in range(2)]
         for a in range(2):
@@ -173,6 +177,7 @@ def tile_list_excess_delay_causes_kernel(tc, tab_words, tab_scales, offs, pos1, 
             for t in range(4):
                 cast_w1(a, 0, t)
             quantize_w1(a, 0, 0, 4)
+        load_w4(1, "slot_a")
         gather_words(1, 0)
         gather_words(1, 1)
 
@@ -196,11 +201,16 @@ def tile_list_excess_delay_causes_kernel(tc, tab_words, tab_scales, offs, pos1, 
             for a in range(2):
                 nc.tensor.matmul_mx(out=p4[:], lhsT=w4_p[b][:, a, 2 * P * t : 2 * P * (t + 1)].bitcast(FP4X4), lhsT_scale=planes[a][:, W4_AT + 512 * b + P * t : W4_AT + 512 * b + P * (t + 1)],
                                     rhs=v_w[a, hf][:].bitcast(FP8X4), rhs_scale=planes[a][:, V_AT + BANK * hf : V_AT + BANK * (hf + 1)], start=(a == 0), stop=(a == 1))
-            c = ring.tile([P, BANK], F32, name="c", bufs=3)
+            c = ring.tile([P, BANK], F32, name="c", bufs=4)
             nc.scalar.activation(c[:], p1[:], RELU, bias=bias[:, 4 * b + t : 4 * b + t + 1])
             if hf == 0:
-                x_pre[b, t] = ring.tile([P, S], F32, name="x_pre", bufs=2)
-            nc.vector.tensor_tensor(x_pre[b, t][:, jc], p4[:], c[:], ALU.add)
+                x_pre[b, t] = ring.tile([P, S], F32, name="x_pre", bufs=3)
+            if hf == 0 and (b, t) in ((0, 0), (0, 1), (0, 3), (1, 2)):
+                y = ring.tile([P, BANK], F32, name="y", bufs=2)
+                nc.scalar.copy(y[:], p4[:])
+                nc.gpsimd.tensor_tensor(x_pre[b, t][:, jc], y[:], c[:], ALU.add)
+            else:
+                nc.vector.tensor_tensor(x_pre[b, t][:, jc], p4[:], c[:], ALU.add)
 
         def callee_product(b, t):
             own[b, t] = psum.tile([P, BANK], F32, name="own", tag="pb", bufs=2)
@@ -261,17 +271,20 @@ def tile_list_excess_delay_causes_kernel(tc, tab_words, tab_scales, offs, pos1, 
                 for bb in range(2):
                     for tt in range(4):
                         load(wo_raw[:, bb, tt, :], wo[512 * bb : 512 * (bb + 1), :].rearrange("(q t i) n -> t q i n", t=4, i=8)[tt])
+            if n == 2:
+                reorder_w4(1)
             if n in (2, 3):
                 quantize_w1(n - 2, 1, 0, 4)
-            if n == 4:
+            if n == 6:
                 relu_scalar(0, 0, M)
-            if n in (5, 6):
-                cast_wo(n - 5)
-            if n == 5:
+            if n in (4, 5):
+                cast_wo(n - 4)
+            if n == 6:
+                quantize_wo()
+            if n == 7:
                 quantize_h(0, 0, M)
 
         callee_product(1, 3)
-        quantize_wo()
         chunks = ((0, 256), (256, 384), (384, 512))
         pick(1, 3, *chunks[0])
         pick(1, 3, *chunks[1])
@@ -279,8 +292,8 @@ def tile_list_excess_delay_causes_kernel(tc, tab_words, tab_scales, offs, pos1, 
         relu_scalar(1, *chunks[0])
         pick(1, 3, *chunks[2])
         subtract(1, 3, *chunks[1])
-        relu_scalar(1, *chunks[1])
         subtract(1, 3, *chunks[2])
+        relu_vector(1, *chunks[1])
         relu_vector(1, *chunks[2])
 
         def score_pass(dst, b, c3, lo, hi):
@@ -299,13 +312,14 @@ def tile_list_excess_delay_causes_kernel(tc, tab_words, tab_scales, offs, pos1, 
             score_pass(wide[c3][:, 0:256], 1, c3, *chunks[0])
             nc.scalar.copy(staged[:, c3, :], wide[c3][:, 0:256])
         nc.sync.dma_start(out_rows[:, :, 0:256], staged[:])
-        for lo, hi in (chunks[2], chunks[1]):
+        for lo, hi in chunks[1:]:
             quantize_h(1, lo, hi)
-        for lo, hi in (chunks[2], chunks[1]):
+        for lo, hi in chunks[1:]:
             narrow = psum.tile([P, BANK], F32, name="narrow", tag="p4")
             for c3 in range(3):
                 for b in range(2):
                     score_pass(narrow[:, P * c3 : P * (c3 + 1)], b, c3, lo, hi)
             staged = held("staged%d" % lo, [P, 3, P], F32)
-            nc.vector.tensor_copy(staged[:].rearrange("p c m -> p (c m)"), narrow[:, 0 : 3 * P])
+            copy = nc.vector.tensor_copy if hi == M else nc.scalar.copy
+            copy(staged[:].rearrange("p c m -> p (c m)"), narrow[:, 0 : 3 * P])
             nc.sync.dma_start(out_rows[:, :, lo:hi], staged[:])

@@ -27,6 +27,7 @@ def tile_list_excess_delay_causes_kernel(tc, tab_words, tab_scales, offs, pos1, 
     nc = tc.nc
     with ExitStack() as ctx:
         keep = ctx.enter_context(tc.tile_pool(name="keep", bufs=1))
+        late = ctx.enter_context(tc.tile_pool(name="late", bufs=1))
         ring = ctx.enter_context(tc.tile_pool(name="ring", bufs=2))
         psum = ctx.enter_context(tc.psum_pool(name="psum", bufs=3))
 
@@ -40,12 +41,14 @@ def tile_list_excess_delay_causes_kernel(tc, tab_words, tab_scales, offs, pos1, 
         def slot(name, shape, dtype, tag):
             return keep.tile(shape, dtype, name=name, tag=tag, align_bytes=64)
 
+        def placed(name, shape, dtype, kib):
+            return late.tile(shape, dtype, name=name, offset=int(1024 * kib), align_bytes=64)
+
         tab_s = held("tab_s", [P, T], U8)
-        tab2_w = slot("tab2_w", [P, 2, T2], I32, "slot_d")
         tab2_s = held("tab2_s", [P, T2], U8)
         w4s_raw = held("w4s_raw", [32, H], U8)
         w8s_raw = held("w8s_raw", [32, H], U8)
-        planes = {0: held("plane0", [P, ROW], U8)}
+        planes = [held("plane%d" % a, [P, ROW], U8) for a in range(2)]
         bias_rows = held("bias_rows", [P, P], F32)
         ident = held("ident", [P, P], F32)
         bias = held("bias", [P, 8], F32)
@@ -56,7 +59,8 @@ def tile_list_excess_delay_causes_kernel(tc, tab_words, tab_scales, offs, pos1, 
             nc.vector.memset(window[64:128, :].bitcast(I32), 0)
         nc.gpsimd.memset(bias_rows[:], 0.0)
         nc.gpsimd.memset(warm[:], 0.0)
-        nc.gpsimd.memset(planes[0][:].bitcast(I32), 0)
+        for a in range(2):
+            nc.gpsimd.memset(planes[a][:].bitcast(I32), 0)
         make_identity(nc, ident[:])
         nc.scalar.activation(warm[:, 4:8], warm[:, 0:4], RELU)
 
@@ -69,38 +73,40 @@ def tile_list_excess_delay_causes_kernel(tc, tab_words, tab_scales, offs, pos1, 
         tab_w = {}
 
         def load_tab_words(a):
-            tab_w[a] = slot("tab_w", [P, T], I32, "slot_c")
+            tab_w[a] = placed("tab_w%d" % a, [P, T], I32, 3.5)
             load(tab_w[a][:], tab_words[a].rearrange("p t i -> p (t i)").bitcast(I32))
 
         w4_raw = {}
 
-        def load_w4(b, tag):
-            w4_raw[b] = slot("w4_raw", [P, 2, H], U8, tag)
+        def load_w4(b, tile):
+            w4_raw[b] = tile
             load(w4_raw[b][:].bitcast(I32), w4_words[:, :, H * b : H * (b + 1)].rearrange("a p e -> p a e").bitcast(I32))
 
         w1_raw = {}
 
-        def load_w1(a, b, tag):
-            w1_raw[a, b] = slot("w1_raw", [P, 4, 512], F32, tag)
+        def load_w1(a, b, tile):
+            w1_raw[a, b] = tile
             load(w1_raw[a, b][:], w1[512 * a : 512 * (a + 1), 512 * b : 512 * (b + 1)].rearrange("(p j) c -> p j c", j=4))
+
+        def load_bias(b):
+            load(bias_rows[4 * b : 4 * b + 4, :], b1[512 * b : 512 * (b + 1)].rearrange("(q t i) -> t q i", t=4, i=8))
 
         load(offs_t[:], offs)
         load_scale_rows(tab_s, tab_scales)
+        load_scale_rows(w4s_raw, w4_scales)
         load(offs2_t[:], offs2)
         load_scale_rows(tab2_s, tab2_scales)
-        load_scale_rows(w4s_raw, w4_scales)
         load_scale_rows(w8s_raw, w8_scales)
-        load_w4(0, "slot_b")
-        load(tab2_w[:], tab2_words.rearrange("a p t i -> p a (t i)").bitcast(I32))
-        for b in range(2):
-            load(bias_rows[4 * b : 4 * b + 4, :], b1[512 * b : 512 * (b + 1)].rearrange("(q t i) -> t q i", t=4, i=8))
+        load_w4(0, held("w4_raw0", [P, 2, H], U8))
         load_tab_words(0)
+        load_bias(0)
+        load_w1(0, 0, held("w1_raw00", [P, 4, 512], F32))
+        load_bias(1)
         load(pos_t[:], pos1)
-        load_w1(0, 0, "slot_a")
 
-        stage = held("stage", [32, ROW], U8)
+        stage = placed("stage", [32, ROW], U8, 35)
         v_s = held("v_s", [P, S], U8)
-        v2_s = held("v2_s", [P, M], U8)
+        v2_s = placed("v2_s", [P, M], U8, 20)
         nc.vector.tensor_copy(v_s[:], tab_s[:].indirect(offs_t[:]))
         nc.vector.tensor_copy(v2_s[:], tab2_s[:].indirect(offs2_t[:]))
         for raw, at in ((w4s_raw, W4_AT), (w8s_raw, W8_AT)):
@@ -111,28 +117,28 @@ def tile_list_excess_delay_causes_kernel(tc, tab_words, tab_scales, offs, pos1, 
 
         def move_scale_rows(a):
             for r in range(4):
-                nc.scalar.dma_start(planes[a][r:P:32, :].bitcast(I32), stage[16 * a + r : 16 * a + 16 : 4, :].bitcast(I32))
+                nc.sync.dma_start(planes[a][r:P:32, :].bitcast(I32), stage[16 * a + r : 16 * a + 16 : 4, :].bitcast(I32))
 
         move_scale_rows(0)
-        w4_p = [held("w4_p%d" % b, [P, 2, H], U8) for b in range(2)]
-        w8_p = [held("w8_p%d" % b, [P, 2, H // 2], I32) for b in range(2)]
+        load_w1(1, 0, placed("w1_raw10", [P, 4, 512], F32, 20))
+        move_scale_rows(1)
+        w4_p = {}
+        w8_p = {}
 
         def reorder(dst, src, b, run):
             width = 64 * run
             nc.vector.tensor_copy(dst.rearrange("p a (t q i) -> p a t q i", t=4, i=run),
                                   src[:, :, b * width : (b + 1) * width].rearrange("p a (q t i) -> p a t q i", t=4, i=run))
 
-        def reorder_w4(b):
+        def reorder_w4(b, tag):
+            w4_p[b] = slot("w4_p%d" % b, [P, 2, H], U8, tag)
             reorder(w4_p[b][:].bitcast(I32), w4_raw[b][:].bitcast(I32), 0, 4)
 
-        reorder_w4(0)
-        load_w1(1, 0, "slot_b")
-        v2_w = [held("v2_w%d" % a, [P, M], U32) for a in range(2)]
-        for a in range(2):
-            nc.vector.tensor_copy(v2_w[a][:], tab2_w[:, a, :].bitcast(U32).indirect(offs2_t[:]))
-        planes[1] = slot("plane1", [P, ROW], U8, "slot_d")
-        nc.gpsimd.memset(planes[1][:].bitcast(I32), 0)
-        move_scale_rows(1)
+        def reorder_w8(b):
+            w8_p[b] = slot("w8_p%d" % b, [P, 2, H // 2], I32, ("c00", "c21")[b])
+            reorder(w8_p[b][:], w8_raw[:], b, 8)
+
+        reorder_w4(0, "w4_p0")
 
         v_w = {(a, hf): held("v_w%d%d" % (a, hf), [P, BANK], U32) for a in range(2) for hf in range(2)}
 
@@ -142,6 +148,12 @@ def tile_list_excess_delay_causes_kernel(tc, tab_words, tab_scales, offs, pos1, 
         gather_words(0, 0)
         gather_words(0, 1)
         load_tab_words(1)
+        tab2_w = placed("tab2_w", [P, 2, T2], I32, 28)
+        load(tab2_w[:], tab2_words.rearrange("a p t i -> p a (t i)").bitcast(I32))
+        load_w4(1, placed("w4_raw1", [P, 2, H], U8, 37))
+
+        def gather_callees(a):
+            nc.vector.tensor_copy(v2_w[:, a, :], tab2_w[:, a, :].bitcast(U32).indirect(offs2_t[:]))
 
         bias_ps = psum.tile([P, BANK], F32, name="bias_ps", tag="pb", bufs=2)
         nc.tensor.transpose(bias_ps[:, 0:P], bias_rows[:], ident[:])
@@ -152,38 +164,55 @@ def tile_list_excess_delay_causes_kernel(tc, tab_words, tab_scales, offs, pos1, 
         w1_g = {}
 
         def cast_w1(a, b, t):
-            if t == 0:
-                w1_g[a, b] = ring.tile([P, 2048], BF16, name="w1_g", bufs=2, align_bytes=64)
-            nc.scalar.copy(w1_g[a, b][:, 512 * t : 512 * (t + 1)].rearrange("p (q u i j) -> p q u j i", u=2, i=4, j=4),
-                 w1_raw[a, b][:].rearrange("p j (q t u i) -> p t q u j i", t=4, u=2, i=4)[:, t])
+            if b == 0:
+                if t == 0:
+                    w1_g[a, b] = ring.tile([P, 2048], BF16, name="w1_g", bufs=2, align_bytes=64)
+                nc.scalar.copy(w1_g[a, b][:, 512 * t : 512 * (t + 1)].rearrange("p (q u i j) -> p q u j i", u=2, i=4, j=4),
+                               w1_raw[a, b][:].rearrange("p j (q t u i) -> p t q u j i", t=4, u=2, i=4)[:, t])
+            else:
+                if t % 2 == 0:
+                    w1_g[a, b, t // 2] = slot("w1_late", [P, 1024], BF16, ("c10", "c11", "c20", "c30")[a + t])
+                nc.scalar.copy(w1_g[a, b, t // 2][:, 512 * (t % 2) : 512 * (t % 2 + 1)].rearrange("p (q u i j) -> p q u j i", u=2, i=4, j=4),
+                               w1_raw[a, b][:].rearrange("p j (q t u i) -> p t q u j i", t=4, u=2, i=4)[:, t])
 
         def quantize_w1(a, b, lo, hi):
             cols = slice(P * lo, P * hi)
-            nc.vector.quantize_mx(out=w1_c[a, b][:, cols].bitcast(FP8X4), scales=w1_s[a, b][:, cols], in_=w1_g[a, b][:, 512 * lo : 512 * hi])
+            rounded = w1_g[a, b][:] if b == 0 else w1_g[a, b, lo // 2][:]
+            nc.vector.quantize_mx(out=w1_c[a, b][:, cols].bitcast(FP8X4), scales=w1_s[a, b][:, cols], in_=rounded)
 
-        wo_g = held("wo_g", [P, 2, N, 4], BF16)
+        wo_g = {}
+        wo_raw = {}
         wo_c = held("wo_c", [P, 2 * N], U32)
         wo_s = held("wo_s", [P, 2 * N], U8)
 
         def cast_wo(b):
-            nc.scalar.copy(wo_g[:, b].rearrange("p (c i) t -> p c t i", i=4), wo_raw[:, b].rearrange("p t (c i) -> p c t i", i=4))
+            wo_g[b] = slot("wo_g%d" % b, [P, N, 4], BF16, ("c31", "c40")[b])
+            nc.gpsimd.tensor_scalar(wo_g[b][:], wo_raw[b][:].rearrange("p t n -> p n t"), 1.0, 0.0, ALU.mult, ALU.add)
 
-        def quantize_wo():
-            flat = wo_g[:].rearrange("p b n t -> p (b n t)")
-            for lo, hi in ((0, 512), (512, 768)):
-                nc.vector.quantize_mx(out=wo_c[:, lo:hi].bitcast(FP8X4), scales=wo_s[:, lo:hi], in_=flat[:, 4 * lo : 4 * hi])
+        def quantize_wo(b):
+            flat = wo_g[b][:].rearrange("p n t -> p (n t)")
+            for lo, hi in ((0, 256), (256, 384)):
+                nc.vector.quantize_mx(out=wo_c[:, N * b + lo : N * b + hi].bitcast(FP8X4), scales=wo_s[:, N * b + lo : N * b + hi], in_=flat[:, 4 * lo : 4 * hi])
+
+        def load_wo(b, kib):
+            wo_raw[b] = placed("wo_raw%d" % b, [P, 4, N], F32, kib)
+            for t in range(4):
+                load(wo_raw[b][:, t, :], wo[512 * b : 512 * (b + 1), :].rearrange("(q t i) n -> t q i n", t=4, i=8)[t])
 
         for a in range(2):
             for t in range(4):
                 cast_w1(a, 0, t)
             quantize_w1(a, 0, 0, 4)
-        load_w4(1, "slot_a")
+        w8_raw = placed("w8_raw", [P, 2, H], I32, 20)
+        load(w8_raw[:], w8_words.rearrange("a p e i -> p a (e i)").bitcast(I32))
         gather_words(1, 0)
         gather_words(1, 1)
-
-        w8_raw = slot("w8_raw", [P, 2, H], I32, "slot_b")
-        load(w8_raw[:], w8_words.rearrange("a p e i -> p a (e i)").bitcast(I32))
-        load_w1(0, 1, "slot_c")
+        for a in range(2):
+            load_w1(a, 1, placed("w1_raw%d1" % a, [P, 4, 512], F32, 4 + 8 * a))
+        v2_w = placed("v2_w", [P, 2, M], U32, 0)
+        gather_callees(0)
+        gather_callees(1)
+        load_wo(0, 28)
 
         x_pre = {}
         picked = {}
@@ -201,12 +230,12 @@ def tile_list_excess_delay_causes_kernel(tc, tab_words, tab_scales, offs, pos1, 
             for a in range(2):
                 nc.tensor.matmul_mx(out=p4[:], lhsT=w4_p[b][:, a, 2 * P * t : 2 * P * (t + 1)].bitcast(FP4X4), lhsT_scale=planes[a][:, W4_AT + 512 * b + P * t : W4_AT + 512 * b + P * (t + 1)],
                                     rhs=v_w[a, hf][:].bitcast(FP8X4), rhs_scale=planes[a][:, V_AT + BANK * hf : V_AT + BANK * (hf + 1)], start=(a == 0), stop=(a == 1))
-            c = ring.tile([P, BANK], F32, name="c", bufs=4)
+            c = slot("c", [P, BANK], F32, "c%d%d" % (4 * b + t, hf))
             nc.scalar.activation(c[:], p1[:], RELU, bias=bias[:, 4 * b + t : 4 * b + t + 1])
             if hf == 0:
-                x_pre[b, t] = ring.tile([P, S], F32, name="x_pre", bufs=3)
-            if hf == 0 and (b, t) in ((0, 0), (0, 1), (0, 3), (1, 2)):
-                y = ring.tile([P, BANK], F32, name="y", bufs=2)
+                x_pre[b, t] = ring.tile([P, S], F32, name="x_pre", bufs=4)
+            if hf == 0 or 4 * b + t in (0, 1, 6):
+                y = ring.tile([P, BANK], F32, name="y", bufs=3)
                 nc.scalar.copy(y[:], p4[:])
                 nc.gpsimd.tensor_tensor(x_pre[b, t][:, jc], y[:], c[:], ALU.add)
             else:
@@ -217,7 +246,7 @@ def tile_list_excess_delay_causes_kernel(tc, tab_words, tab_scales, offs, pos1, 
             for a in range(2):
                 nc.tensor.matmul_mx(out=own[b, t][:], lhsT=w8_p[b][:, a, P * t : P * (t + 1)].bitcast(FP8X4),
                                     lhsT_scale=planes[a][:, W8_AT + 512 * b + P * t : W8_AT + 512 * b + P * (t + 1)],
-                                    rhs=v2_w[a][:].bitcast(FP8X4), rhs_scale=planes[a][:, V2_AT : V2_AT + M], start=(a == 0), stop=(a == 1))
+                                    rhs=v2_w[:, a, :].bitcast(FP8X4), rhs_scale=planes[a][:, V2_AT : V2_AT + M], start=(a == 0), stop=(a == 1))
 
         def pick(b, t, lo, hi):
             picked[b, t, lo] = ring.tile([P, hi - lo], F32, name="picked", bufs=4)
@@ -250,39 +279,33 @@ def tile_list_excess_delay_causes_kernel(tc, tab_words, tab_scales, offs, pos1, 
         tiles = [(b, t) for b in range(2) for t in range(4)]
         for n, (b, t) in enumerate(tiles):
             caller_half(b, t, 0)
+            if n == 1:
+                reorder_w8(0)
             if n > 0:
                 callee_product(*tiles[n - 1])
                 pick(*tiles[n - 1], 0, M)
-            if n in (1, 2):
-                for tt in range(2):
-                    cast_w1(n - 1, 1, tt)
             caller_half(b, t, 1)
+            if 1 <= n <= 4:
+                late_a, late_t = (n - 1) % 2, 2 * ((n - 1) // 2)
+                cast_w1(late_a, 1, late_t)
+                cast_w1(late_a, 1, late_t + 1)
+            if n in (3, 5):
+                cast_wo(n // 2 - 1)
             if n == 0:
-                reorder(w8_p[0][:], w8_raw[:], 0, 8)
-                reorder(w8_p[1][:], w8_raw[:], 1, 8)
-                load_w1(1, 1, "slot_b")
+                reorder_w4(1, "c01")
             if n > 0:
                 subtract(*tiles[n - 1], 0, M)
-            if n in (1, 2):
-                for tt in range(2, 4):
-                    cast_w1(n - 1, 1, tt)
-            if n == 1:
-                wo_raw = slot("wo_raw", [P, 2, 4, N], F32, "slot_c")
-                for bb in range(2):
-                    for tt in range(4):
-                        load(wo_raw[:, bb, tt, :], wo[512 * bb : 512 * (bb + 1), :].rearrange("(q t i) n -> t q i n", t=4, i=8)[tt])
             if n == 2:
-                reorder_w4(1)
-            if n in (2, 3):
-                quantize_w1(n - 2, 1, 0, 4)
-            if n == 6:
-                relu_scalar(0, 0, M)
-            if n in (4, 5):
-                cast_wo(n - 4)
-            if n == 6:
-                quantize_wo()
-            if n == 7:
-                quantize_h(0, 0, M)
+                reorder_w8(1)
+                load_wo(1, 20)
+            if 1 <= n <= 4:
+                quantize_w1(late_a, 1, late_t, late_t + 2)
+            if n in (5, 6):
+                relu_scalar(0, 256 * (n - 5), 256 * (n - 4))
+            if n in (5, 7):
+                quantize_wo(n // 2 - 2)
+            if n in (6, 7):
+                quantize_h(0, 256 * (n - 6), 256 * (n - 5))
 
         callee_product(1, 3)
         chunks = ((0, 256), (256, 384), (384, 512))
@@ -298,7 +321,7 @@ def tile_list_excess_delay_causes_kernel(tc, tab_words, tab_scales, offs, pos1, 
 
         def score_pass(dst, b, c3, lo, hi):
             cols = slice(N * b + P * c3, N * b + P * (c3 + 1))
-            codes, scales = (h_c[0, 0][:, lo:hi], h_s[0, 0][:, lo:hi]) if b == 0 else (h_c[1, lo][:], h_s[1, lo][:])
+            codes, scales = (h_c[0, lo - lo % 256][:, lo % 256 : lo % 256 + hi - lo], h_s[0, lo - lo % 256][:, lo % 256 : lo % 256 + hi - lo]) if b == 0 else (h_c[1, lo][:], h_s[1, lo][:])
             nc.tensor.matmul_mx(out=dst, lhsT=wo_c[:, cols].bitcast(FP8X4), lhsT_scale=wo_s[:, cols],
                                 rhs=codes.bitcast(FP8X4), rhs_scale=scales, start=(b == 0), stop=(b == 1))
 

@@ -15,11 +15,13 @@ U8 = mybir.dt.uint8
 FP8X4 = mybir.dt.float8_e4m3fn_x4
 FP4X4 = mybir.dt.float4_e2m1fn_x4
 ALU = mybir.AluOpType
+IDENTITY = mybir.ActivationFunctionType.Identity
 RELU = mybir.ActivationFunctionType.Relu
 
 P = 128
 BANK = 512
-V_AT, V2_AT, W4_AT, W8_AT, ROW = 0, 1024, 1536, 2560, 3584
+FUSED = (3, 4, 5, 6)
+V_AT, W4_AT, ROW = 0, 1024, 2048
 
 
 def tile_list_excess_delay_causes_kernel(tc, tab_words, tab_scales, offs, pos1, tab2_words, tab2_scales, offs2,
@@ -27,7 +29,7 @@ def tile_list_excess_delay_causes_kernel(tc, tab_words, tab_scales, offs, pos1, 
     nc = tc.nc
     with ExitStack() as ctx:
         keep = ctx.enter_context(tc.tile_pool(name="keep", bufs=1))
-        late = ctx.enter_context(tc.tile_pool(name="late", bufs=1))
+        spare = ctx.enter_context(tc.tile_pool(name="late", bufs=1))
         ring = ctx.enter_context(tc.tile_pool(name="ring", bufs=2))
         psum = ctx.enter_context(tc.psum_pool(name="psum", bufs=3))
 
@@ -42,22 +44,28 @@ def tile_list_excess_delay_causes_kernel(tc, tab_words, tab_scales, offs, pos1, 
             return keep.tile(shape, dtype, name=name, tag=tag, align_bytes=64)
 
         def placed(name, shape, dtype, kib):
-            return late.tile(shape, dtype, name=name, offset=int(1024 * kib), align_bytes=64)
+            return spare.tile(shape, dtype, name=name, offset=int(1024 * kib), align_bytes=64)
+
+        def tenant(name, shape, dtype, where):
+            return placed(name, shape, dtype, where[1]) if where[0] == "at" else slot(name, shape, dtype, where)
 
         tab_s = held("tab_s", [P, T], U8)
         tab2_s = held("tab2_s", [P, T2], U8)
         w4s_raw = held("w4s_raw", [32, H], U8)
-        w8s_raw = held("w8s_raw", [32, H], U8)
+        w8s_raw = held("w8s_raw", [P, H], U8)
         planes = [held("plane%d" % a, [P, ROW], U8) for a in range(2)]
-        bias_rows = held("bias_rows", [P, P], F32)
+        bias_rows = held("bias_rows", [P, 512], F32)
+        bias_dealt = held("bias_dealt", [P, 4, P], F32)
         ident = held("ident", [P, P], F32)
         bias = held("bias", [P, 8], F32)
+        minus_bias = held("minus_bias", [P, 8], F32)
         warm = held("warm", [P, 8], F32)
 
-        for window in (tab_s, tab2_s):
-            nc.vector.memset(window[32:64, :].bitcast(I32), 0)
-            nc.vector.memset(window[64:128, :].bitcast(I32), 0)
-        nc.gpsimd.memset(bias_rows[:], 0.0)
+        nc.vector.memset(bias_rows[:], 0.0)
+        nc.vector.memset(tab_s[32:64, :].bitcast(I32), 0)
+        nc.vector.memset(tab_s[64:128, :].bitcast(I32), 0)
+        for raw in (tab2_s, w8s_raw):
+            nc.gpsimd.memset(raw[:].bitcast(I32), 0)
         nc.gpsimd.memset(warm[:], 0.0)
         for a in range(2):
             nc.gpsimd.memset(planes[a][:].bitcast(I32), 0)
@@ -73,7 +81,7 @@ def tile_list_excess_delay_causes_kernel(tc, tab_words, tab_scales, offs, pos1, 
         tab_w = {}
 
         def load_tab_words(a):
-            tab_w[a] = placed("tab_w%d" % a, [P, T], I32, 3.5)
+            tab_w[a] = placed("tab_w%d" % a, [P, T], I32, 16 * a)
             load(tab_w[a][:], tab_words[a].rearrange("p t i -> p (t i)").bitcast(I32))
 
         w4_raw = {}
@@ -88,39 +96,41 @@ def tile_list_excess_delay_causes_kernel(tc, tab_words, tab_scales, offs, pos1, 
             w1_raw[a, b] = tile
             load(w1_raw[a, b][:], w1[512 * a : 512 * (a + 1), 512 * b : 512 * (b + 1)].rearrange("(p j) c -> p j c", j=4))
 
-        def load_bias(b):
-            load(bias_rows[4 * b : 4 * b + 4, :], b1[512 * b : 512 * (b + 1)].rearrange("(q t i) -> t q i", t=4, i=8))
+        def load_packed_planes(dst, scales, quadrant):
+            load(dst[32 * quadrant + 4 : 32 * quadrant + 12, :].bitcast(I32), scales[:, 4 * quadrant : 4 * quadrant + 4, :].bitcast(I32))
 
         load(offs_t[:], offs)
         load_scale_rows(tab_s, tab_scales)
         load_scale_rows(w4s_raw, w4_scales)
         load(offs2_t[:], offs2)
-        load_scale_rows(tab2_s, tab2_scales)
-        load_scale_rows(w8s_raw, w8_scales)
-        load_w4(0, held("w4_raw0", [P, 2, H], U8))
-        load_tab_words(0)
-        load_bias(0)
-        load_w1(0, 0, held("w1_raw00", [P, 4, 512], F32))
-        load_bias(1)
         load(pos_t[:], pos1)
+        load_w4(0, held("w4_raw0", [P, 2, H], U8))
+        load(bias_rows[0:2, :], b1.rearrange("(b c) -> b c", b=2))
+        load_tab_words(0)
+        for quadrant in range(4):
+            load_packed_planes(tab2_s, tab2_scales, quadrant)
+        for quadrant in range(2):
+            load_packed_planes(w8s_raw, w8_scales, quadrant)
+        load_w1(0, 0, held("w1_raw00", [P, 4, 512], F32))
+        for quadrant in range(2, 4):
+            load_packed_planes(w8s_raw, w8_scales, quadrant)
 
-        stage = placed("stage", [32, ROW], U8, 35)
-        v_s = held("v_s", [P, S], U8)
-        v2_s = placed("v2_s", [P, M], U8, 20)
+        def deal_scales(dst, raw):
+            nc.vector.tensor_copy(dst.bitcast(I32).rearrange("p (b t q i) -> p b t q i", b=2, t=4, i=2),
+                                  raw.bitcast(I32).rearrange("p (b q t i) -> p b t q i", b=2, t=4, i=2))
+
+        stage = placed("stage", [32, ROW], U8, 32)
+        v_s = placed("v_s", [P, S], U8, 16)
         nc.vector.tensor_copy(v_s[:], tab_s[:].indirect(offs_t[:]))
-        nc.vector.tensor_copy(v2_s[:], tab2_s[:].indirect(offs2_t[:]))
-        for raw, at in ((w4s_raw, W4_AT), (w8s_raw, W8_AT)):
-            nc.vector.tensor_copy(stage[:, at : at + H].bitcast(I32).rearrange("p (b t q i) -> p b t q i", b=2, t=4, i=2),
-                                  raw[:].bitcast(I32).rearrange("p (b q t i) -> p b t q i", b=2, t=4, i=2))
+        deal_scales(stage[:, W4_AT : W4_AT + H], w4s_raw[:])
         nc.vector.tensor_copy(stage[:, V_AT : V_AT + S].bitcast(I32), v_s[0:32, :].bitcast(I32))
-        nc.vector.tensor_copy(stage[:, V2_AT : V2_AT + M].bitcast(I32), v2_s[0:32, :].bitcast(I32))
 
         def move_scale_rows(a):
             for r in range(4):
                 nc.sync.dma_start(planes[a][r:P:32, :].bitcast(I32), stage[16 * a + r : 16 * a + 16 : 4, :].bitcast(I32))
 
         move_scale_rows(0)
-        load_w1(1, 0, placed("w1_raw10", [P, 4, 512], F32, 20))
+        load_tab_words(1)
         move_scale_rows(1)
         w4_p = {}
         w8_p = {}
@@ -130,15 +140,18 @@ def tile_list_excess_delay_causes_kernel(tc, tab_words, tab_scales, offs, pos1, 
             nc.vector.tensor_copy(dst.rearrange("p a (t q i) -> p a t q i", t=4, i=run),
                                   src[:, :, b * width : (b + 1) * width].rearrange("p a (q t i) -> p a t q i", t=4, i=run))
 
-        def reorder_w4(b, tag):
-            w4_p[b] = slot("w4_p%d" % b, [P, 2, H], U8, tag)
-            reorder(w4_p[b][:].bitcast(I32), w4_raw[b][:].bitcast(I32), 0, 4)
+        def reorder_w4(b, lo, hi, where):
+            dealt = tenant("w4_p%d%d" % (b, lo), [P, 2, 2 * P * (hi - lo)], U8, where)
+            nc.vector.tensor_copy(dealt[:].bitcast(I32).rearrange("p a (t q i) -> p a t q i", q=16, i=4),
+                                  w4_raw[b][:].bitcast(I32).rearrange("p a (q t i) -> p a t q i", t=4, i=4)[:, :, lo:hi])
+            for t in range(lo, hi):
+                w4_p[b, t] = dealt[:, :, 2 * P * (t - lo) : 2 * P * (t - lo + 1)]
 
         def reorder_w8(b):
-            w8_p[b] = slot("w8_p%d" % b, [P, 2, H // 2], I32, ("c00", "c21")[b])
+            w8_p[b] = tenant("w8_p%d" % b, [P, 2, H // 2], I32, ("y10", "y31")[b])
             reorder(w8_p[b][:], w8_raw[:], b, 8)
 
-        reorder_w4(0, "w4_p0")
+        reorder_w4(0, 0, 1, "w4_p00")
 
         v_w = {(a, hf): held("v_w%d%d" % (a, hf), [P, BANK], U32) for a in range(2) for hf in range(2)}
 
@@ -147,38 +160,44 @@ def tile_list_excess_delay_causes_kernel(tc, tab_words, tab_scales, offs, pos1, 
 
         gather_words(0, 0)
         gather_words(0, 1)
-        load_tab_words(1)
-        tab2_w = placed("tab2_w", [P, 2, T2], I32, 28)
+        load_w1(1, 0, placed("w1_raw10", [P, 4, 512], F32, 0))
+        tab2_w = placed("tab2_w", [P, 2, T2], I32, 8)
         load(tab2_w[:], tab2_words.rearrange("a p t i -> p a (t i)").bitcast(I32))
-        load_w4(1, placed("w4_raw1", [P, 2, H], U8, 37))
+        load_w4(1, placed("w4_raw1", [P, 2, H], U8, 32))
+        v2_s = held("v2_s", [P, M], U8)
+        w8_s = held("w8_s", [P, H], U8)
+        nc.vector.tensor_copy(v2_s[:], tab2_s[:].indirect(offs2_t[:]))
+        deal_scales(w8_s[:], w8s_raw[:])
 
         def gather_callees(a):
             nc.vector.tensor_copy(v2_w[:, a, :], tab2_w[:, a, :].bitcast(U32).indirect(offs2_t[:]))
 
         bias_ps = psum.tile([P, BANK], F32, name="bias_ps", tag="pb", bufs=2)
-        nc.tensor.transpose(bias_ps[:, 0:P], bias_rows[:], ident[:])
-        nc.scalar.copy(bias[:], bias_ps[:, 0:8])
+        nc.scalar.copy(bias_dealt[:].rearrange("p t (q i) -> p t q i", i=8), bias_rows[:].rearrange("p (q t i) -> p t q i", t=4, i=8))
+        for t in range(4):
+            nc.tensor.transpose(bias_ps[:, P * t : P * (t + 1)], bias_dealt[:, t, :], ident[:])
+        by_tile = bias_ps[:].rearrange("p (t b) -> p b t", t=4)[:, 0:2, :]
+        nc.scalar.copy(bias[:].rearrange("p (b t) -> p b t", b=2), by_tile)
+        nc.scalar.mul(minus_bias[:].rearrange("p (b t) -> p b t", b=2), by_tile, -1.0)
 
         w1_c = {(a, b): held("w1_c%d%d" % (a, b), [P, 512], U32) for a in range(2) for b in range(2)}
         w1_s = {(a, b): held("w1_s%d%d" % (a, b), [P, 512], U8) for a in range(2) for b in range(2)}
         w1_g = {}
 
-        def cast_w1(a, b, t):
-            if b == 0:
-                if t == 0:
-                    w1_g[a, b] = ring.tile([P, 2048], BF16, name="w1_g", bufs=2, align_bytes=64)
-                nc.scalar.copy(w1_g[a, b][:, 512 * t : 512 * (t + 1)].rearrange("p (q u i j) -> p q u j i", u=2, i=4, j=4),
-                               w1_raw[a, b][:].rearrange("p j (q t u i) -> p t q u j i", t=4, u=2, i=4)[:, t])
-            else:
-                if t % 2 == 0:
-                    w1_g[a, b, t // 2] = slot("w1_late", [P, 1024], BF16, ("c10", "c11", "c20", "c30")[a + t])
-                nc.scalar.copy(w1_g[a, b, t // 2][:, 512 * (t % 2) : 512 * (t % 2 + 1)].rearrange("p (q u i j) -> p q u j i", u=2, i=4, j=4),
-                               w1_raw[a, b][:].rearrange("p j (q t u i) -> p t q u j i", t=4, u=2, i=4)[:, t])
+        def cast_w1(a, b, t, first, count, tag):
+            if t == first:
+                w1_g[a, b, first] = tenant("w1_g%d%d%d" % (a, b, first), [P, 512 * count], BF16, tag)
+            copy = nc.vector.tensor_copy if (a, b, t) == (1, 0, 0) else nc.scalar.copy
+            copy(w1_g[a, b, first][:, 512 * (t - first) : 512 * (t - first + 1)].rearrange("p (q u i j) -> p q u j i", u=2, i=4, j=4),
+                 w1_raw[a, b][:].rearrange("p j (q t u i) -> p t q u j i", t=4, u=2, i=4)[:, t])
+
+        def round_w1(a, b, first, count, tag):
+            for t in range(first, first + count):
+                cast_w1(a, b, t, first, count, tag)
 
         def quantize_w1(a, b, lo, hi):
             cols = slice(P * lo, P * hi)
-            rounded = w1_g[a, b][:] if b == 0 else w1_g[a, b, lo // 2][:]
-            nc.vector.quantize_mx(out=w1_c[a, b][:, cols].bitcast(FP8X4), scales=w1_s[a, b][:, cols], in_=rounded)
+            nc.vector.quantize_mx(out=w1_c[a, b][:, cols].bitcast(FP8X4), scales=w1_s[a, b][:, cols], in_=w1_g[a, b, lo][:])
 
         wo_g = {}
         wo_raw = {}
@@ -186,8 +205,8 @@ def tile_list_excess_delay_causes_kernel(tc, tab_words, tab_scales, offs, pos1, 
         wo_s = held("wo_s", [P, 2 * N], U8)
 
         def cast_wo(b):
-            wo_g[b] = slot("wo_g%d" % b, [P, N, 4], BF16, ("c31", "c40")[b])
-            nc.gpsimd.tensor_scalar(wo_g[b][:], wo_raw[b][:].rearrange("p t n -> p n t"), 1.0, 0.0, ALU.mult, ALU.add)
+            wo_g[b] = slot("wo_g%d" % b, [P, N, 4], BF16, ("y21", "y61")[b])
+            nc.scalar.copy(wo_g[b][:].rearrange("p (c i) t -> p c t i", i=4), wo_raw[b][:].rearrange("p t (c i) -> p c t i", i=4))
 
         def quantize_wo(b):
             flat = wo_g[b][:].rearrange("p n t -> p (n t)")
@@ -199,60 +218,73 @@ def tile_list_excess_delay_causes_kernel(tc, tab_words, tab_scales, offs, pos1, 
             for t in range(4):
                 load(wo_raw[b][:, t, :], wo[512 * b : 512 * (b + 1), :].rearrange("(q t i) n -> t q i n", t=4, i=8)[t])
 
-        for a in range(2):
-            for t in range(4):
-                cast_w1(a, 0, t)
-            quantize_w1(a, 0, 0, 4)
-        w8_raw = placed("w8_raw", [P, 2, H], I32, 20)
-        load(w8_raw[:], w8_words.rearrange("a p e i -> p a (e i)").bitcast(I32))
+        round_w1(0, 0, 0, 4, "w1_g00")
+        quantize_w1(0, 0, 0, 4)
         gather_words(1, 0)
         gather_words(1, 1)
-        for a in range(2):
-            load_w1(a, 1, placed("w1_raw%d1" % a, [P, 4, 512], F32, 4 + 8 * a))
-        v2_w = placed("v2_w", [P, 2, M], U32, 0)
-        gather_callees(0)
-        gather_callees(1)
-        load_wo(0, 28)
+        w8_raw = placed("w8_raw", [P, 2, H], I32, 16)
+        load(w8_raw[:], w8_words.rearrange("a p e i -> p a (e i)").bitcast(I32))
+        load_w1(0, 1, placed("w1_raw01", [P, 4, 512], F32, 24))
 
         x_pre = {}
         picked = {}
         own = {}
+        own_sb = {}
         diff = [held("diff%d" % b, [P, 4, M], F32) for b in range(2)]
+
+        y = {}
+        summed = {}
+
+        def moving(a, hf):
+            return dict(rhs=v_w[a, hf][:].bitcast(FP8X4), rhs_scale=planes[a][:, V_AT + BANK * hf : V_AT + BANK * (hf + 1)], start=(a == 0), stop=(a == 1))
+
+        def fp4_half(b, t, hf):
+            n = 4 * b + t
+            p4 = psum.tile([P, BANK], F32, name="p4", tag="p4")
+            for a in range(2):
+                nc.tensor.matmul_mx(out=p4[:], lhsT=w4_p[b, t][:, a, :].bitcast(FP4X4), lhsT_scale=planes[a][:, W4_AT + P * n : W4_AT + P * (n + 1)], **moving(a, hf))
+            y[n, hf] = tenant("y_%d%d" % (n, hf), [P, BANK], F32, ("at", 44) if n + hf == 0 else "y%d%d" % (n, hf))
+            nc.scalar.activation(y[n, hf][:], p4[:], IDENTITY, bias=bias[:, n : n + 1])
 
         def caller_half(b, t, hf):
             cols = slice(P * t, P * (t + 1))
-            jc = slice(BANK * hf, BANK * (hf + 1))
+            n = 4 * b + t
             p1 = psum.tile([P, BANK], F32, name="p1", tag="p1")
-            p4 = psum.tile([P, BANK], F32, name="p4", tag="p4")
             for a in range(2):
-                nc.tensor.matmul_mx(out=p1[:], lhsT=w1_c[a, b][:, cols].bitcast(FP8X4), lhsT_scale=w1_s[a, b][:, cols],
-                                    rhs=v_w[a, hf][:].bitcast(FP8X4), rhs_scale=planes[a][:, V_AT + BANK * hf : V_AT + BANK * (hf + 1)], start=(a == 0), stop=(a == 1))
-            for a in range(2):
-                nc.tensor.matmul_mx(out=p4[:], lhsT=w4_p[b][:, a, 2 * P * t : 2 * P * (t + 1)].bitcast(FP4X4), lhsT_scale=planes[a][:, W4_AT + 512 * b + P * t : W4_AT + 512 * b + P * (t + 1)],
-                                    rhs=v_w[a, hf][:].bitcast(FP8X4), rhs_scale=planes[a][:, V_AT + BANK * hf : V_AT + BANK * (hf + 1)], start=(a == 0), stop=(a == 1))
-            c = slot("c", [P, BANK], F32, "c%d%d" % (4 * b + t, hf))
-            nc.scalar.activation(c[:], p1[:], RELU, bias=bias[:, 4 * b + t : 4 * b + t + 1])
+                nc.tensor.matmul_mx(out=p1[:], lhsT=w1_c[a, b][:, cols].bitcast(FP8X4), lhsT_scale=w1_s[a, b][:, cols], **moving(a, hf))
             if hf == 0:
-                x_pre[b, t] = ring.tile([P, S], F32, name="x_pre", bufs=4)
-            if hf == 0 or 4 * b + t in (0, 1, 6):
-                y = ring.tile([P, BANK], F32, name="y", bufs=3)
-                nc.scalar.copy(y[:], p4[:])
-                nc.gpsimd.tensor_tensor(x_pre[b, t][:, jc], y[:], c[:], ALU.add)
+                x_pre[b, t] = ring.tile([P, S], F32, name="x_pre", bufs=3)
+            if n in FUSED:
+                summed[n, hf] = ring.tile([P, BANK], F32, name="summed", bufs=3)
+                target = summed[n, hf][:]
             else:
-                nc.vector.tensor_tensor(x_pre[b, t][:, jc], p4[:], c[:], ALU.add)
+                target = x_pre[b, t][:, BANK * hf : BANK * (hf + 1)]
+            nc.vector.scalar_tensor_tensor(target, p1[:], minus_bias[:, n : n + 1], y[n, hf][:], ALU.max, ALU.add)
+
+        def second_relu(b, t, hf):
+            if 4 * b + t in FUSED:
+                nc.scalar.activation(x_pre[b, t][:, BANK * hf : BANK * (hf + 1)], summed[4 * b + t, hf][:], RELU)
 
         def callee_product(b, t):
             own[b, t] = psum.tile([P, BANK], F32, name="own", tag="pb", bufs=2)
             for a in range(2):
                 nc.tensor.matmul_mx(out=own[b, t][:], lhsT=w8_p[b][:, a, P * t : P * (t + 1)].bitcast(FP8X4),
-                                    lhsT_scale=planes[a][:, W8_AT + 512 * b + P * t : W8_AT + 512 * b + P * (t + 1)],
-                                    rhs=v2_w[:, a, :].bitcast(FP8X4), rhs_scale=planes[a][:, V2_AT : V2_AT + M], start=(a == 0), stop=(a == 1))
+                                    lhsT_scale=w8_s[4 + 4 * a : P, 512 * b + P * t : 512 * b + P * (t + 1)],
+                                    rhs=v2_w[:, a, :].bitcast(FP8X4), rhs_scale=v2_s[4 + 4 * a : P, :], start=(a == 0), stop=(a == 1))
+            if 4 * b + t in FUSED:
+                own_sb[b, t] = ring.tile([P, M], F32, name="own_sb", bufs=2)
+                nc.scalar.copy(own_sb[b, t][:], own[b, t][:])
 
         def pick(b, t, lo, hi):
+            if 4 * b + t in FUSED:
+                return
             picked[b, t, lo] = ring.tile([P, hi - lo], F32, name="picked", bufs=4)
             nc.vector.tensor_copy(picked[b, t, lo][:], x_pre[b, t][:].indirect(pos_t[:, lo // 16 : hi // 16]))
 
         def subtract(b, t, lo, hi):
+            if 4 * b + t in FUSED:
+                nc.vector.tensor_tensor(diff[b][:, t, lo:hi], x_pre[b, t][:].indirect(pos_t[:, lo // 16 : hi // 16]), own_sb[b, t][:, lo:hi], ALU.subtract)
+                return
             nc.vector.scalar_tensor_tensor(diff[b][:, t, lo:hi], picked[b, t, lo][:], 0.0, own[b, t][:, lo:hi], ALU.max, ALU.subtract)
 
         h_g = {}
@@ -277,33 +309,61 @@ def tile_list_excess_delay_causes_kernel(tc, tab_words, tab_scales, offs, pos1, 
             nc.vector.quantize_mx(out=h_c[b, lo][:].bitcast(FP8X4), scales=h_s[b, lo][:], in_=h_g[b, lo][:].rearrange("p m t -> p (m t)"))
 
         tiles = [(b, t) for b in range(2) for t in range(4)]
+        late = {1: ((0, 0, "y11"),), 2: ((1, 0, "y20"), (0, 2, "y21")), 3: ((1, 2, "y30"),)}
+        fp4_half(0, 0, 0)
+        fp4_half(0, 0, 1)
+        fp4_ahead = [(1, 2, 3), (4,), (5,), (6,), (7,), (), (), ()]
+        round_w1(1, 0, 0, 1, ("at", 40))
+        quantize_w1(1, 0, 0, 1)
+        reorder_w4(0, 1, 4, ("at", 40))
         for n, (b, t) in enumerate(tiles):
             caller_half(b, t, 0)
-            if n == 1:
-                reorder_w8(0)
+            for ahead in fp4_ahead[n][:1]:
+                fp4_half(*tiles[ahead], 0)
+                fp4_half(*tiles[ahead], 1)
             if n > 0:
+                second_relu(*tiles[n - 1], 1)
+            if n > 1:
                 callee_product(*tiles[n - 1])
-                pick(*tiles[n - 1], 0, M)
-            caller_half(b, t, 1)
-            if 1 <= n <= 4:
-                late_a, late_t = (n - 1) % 2, 2 * ((n - 1) // 2)
-                cast_w1(late_a, 1, late_t)
-                cast_w1(late_a, 1, late_t + 1)
-            if n in (3, 5):
-                cast_wo(n // 2 - 1)
-            if n == 0:
-                reorder_w4(1, "c01")
             if n > 0:
-                subtract(*tiles[n - 1], 0, M)
+                pick(*tiles[n - 1], 0, M)
             if n == 2:
+                subtract(*tiles[0], 0, M)
+            caller_half(b, t, 1)
+            for ahead in fp4_ahead[n][1:]:
+                fp4_half(*tiles[ahead], 0)
+                fp4_half(*tiles[ahead], 1)
+            second_relu(b, t, 0)
+            if n == 0:
+                round_w1(1, 0, 1, 1, ("at", 45))
+                quantize_w1(1, 0, 1, 2)
+                reorder_w4(1, 0, 4, ("at", 45.5))
+                v2_w = placed("v2_w", [P, 2, M], U32, 41.5)
+                gather_callees(0)
+                gather_callees(1)
+                load_w1(1, 1, placed("w1_raw11", [P, 4, 512], F32, 8))
+            if n == 1:
+                for tt, tag in ((2, "y01"), (3, "y10")):
+                    round_w1(1, 0, tt, 1, tag)
+                    quantize_w1(1, 0, tt, tt + 1)
+                load_wo(0, 0)
+                reorder_w8(0)
+                callee_product(*tiles[0])
+            for late_a, late_t, tag in late.get(n, ()):
+                round_w1(late_a, 1, late_t, 2, tag)
+            if n in (3, 7):
+                cast_wo(n // 7)
+            if n > 1:
+                subtract(*tiles[n - 1], 0, M)
+            if n == 3:
                 reorder_w8(1)
-                load_wo(1, 20)
-            if 1 <= n <= 4:
+                load_wo(1, 16)
+            for late_a, late_t, tag in late.get(n, ()):
                 quantize_w1(late_a, 1, late_t, late_t + 2)
             if n in (5, 6):
                 relu_scalar(0, 256 * (n - 5), 256 * (n - 4))
             if n in (5, 7):
-                quantize_wo(n // 2 - 2)
+                quantize_wo(n // 7)
             if n in (6, 7):
                 quantize_h(0, 256 * (n - 6), 256 * (n - 5))
 

@@ -20,8 +20,29 @@ RELU = mybir.ActivationFunctionType.Relu
 
 P = 128
 BANK = 512
-FUSED = (3, 4, 5, 6)
-V_AT, W4_AT, ROW = 0, 1024, 2048
+PIECE = M // 2
+TILES = 8
+CALLER_ROWS = 112
+CALLEE_ROWS = 48
+V_AT, W4_AT, CALLER_WIDTH = 0, S, S + H
+V2_AT, W8_AT, CALLEE_WIDTH = 0, M, M + H
+FUSED = range(3, 7)
+AHEAD = 3
+
+AT_V2_SCALES = 0.5
+AT_TABLE = (1, 18.5)
+AT_W1_PASS1 = 1.5
+AT_TABLE2 = 9.5
+AT_W8 = 18
+AT_V_SCALES = 19
+AT_W1_PASS0 = 26
+AT_FIRST_ROUNDED = 34
+AT_STAGE = 36
+AT_V2_WORDS = 41.5
+AT_FIRST_Y = 44
+AT_SECOND_ROUNDED = 45
+AT_W4_DEALT = 45.5
+AT_LAST_PICKS = 48
 
 
 def tile_list_excess_delay_causes_kernel(tc, tab_words, tab_scales, offs, pos1, tab2_words, tab2_scales, offs2,
@@ -29,380 +50,330 @@ def tile_list_excess_delay_causes_kernel(tc, tab_words, tab_scales, offs, pos1, 
     nc = tc.nc
     with ExitStack() as ctx:
         keep = ctx.enter_context(tc.tile_pool(name="keep", bufs=1))
-        spare = ctx.enter_context(tc.tile_pool(name="late", bufs=1))
+        shared = ctx.enter_context(tc.tile_pool(name="shared", bufs=1))
         ring = ctx.enter_context(tc.tile_pool(name="ring", bufs=2))
         psum = ctx.enter_context(tc.psum_pool(name="psum", bufs=3))
 
         def held(name, shape, dtype):
             return keep.tile(shape, dtype, name=name, align_bytes=64)
 
+        def placed(name, shape, dtype, kib):
+            return shared.tile(shape, dtype, name=name, offset=int(1024 * kib), align_bytes=64)
+
+        def after_y(n, hf, name, shape, dtype):
+            return keep.tile(shape, dtype, name=name, tag="y%d%d" % (n, hf), align_bytes=64)
+
         offs_t = keep.tile([P, S // 16], U16, name="offs_t")
         pos_t = keep.tile([P, M // 16], U16, name="pos_t")
         offs2_t = keep.tile([P, M // 16], U16, name="offs2_t")
 
-        def slot(name, shape, dtype, tag):
-            return keep.tile(shape, dtype, name=name, tag=tag, align_bytes=64)
-
-        def placed(name, shape, dtype, kib):
-            return spare.tile(shape, dtype, name=name, offset=int(1024 * kib), align_bytes=64)
-
-        def tenant(name, shape, dtype, where):
-            return placed(name, shape, dtype, where[1]) if where[0] == "at" else slot(name, shape, dtype, where)
-
-        tab_s = held("tab_s", [P, T], U8)
-        tab2_s = held("tab2_s", [P, T2], U8)
-        w4s_raw = held("w4s_raw", [32, H], U8)
-        w8s_raw = held("w8s_raw", [P, H], U8)
-        planes = [held("plane%d" % a, [P, ROW], U8) for a in range(2)]
+        tab_s = held("tab_s", [P, 2, T], U8)
+        tab2_s = held("tab2_s", [P, 2, T2], U8)
+        w4s_raw = held("w4s_raw", [P, 2, H], U8)
+        w8s_raw = held("w8s_raw", [P, 2, H], U8)
+        callee_s = held("callee_s", [P, 2, CALLEE_WIDTH], U8)
+        caller_s = held("caller_s", [P, 2, CALLER_WIDTH], U8)
         bias_rows = held("bias_rows", [P, 512], F32)
         bias_dealt = held("bias_dealt", [P, 4, P], F32)
         ident = held("ident", [P, P], F32)
-        bias = held("bias", [P, 8], F32)
-        minus_bias = held("minus_bias", [P, 8], F32)
-        warm = held("warm", [P, 8], F32)
+        bias = held("bias", [P, TILES], F32)
+        minus_bias = held("minus_bias", [P, TILES], F32)
 
-        nc.vector.memset(bias_rows[:], 0.0)
-        nc.vector.memset(tab_s[32:64, :].bitcast(I32), 0)
-        nc.vector.memset(tab_s[64:128, :].bitcast(I32), 0)
-        for raw in (tab2_s, w8s_raw):
-            nc.gpsimd.memset(raw[:].bitcast(I32), 0)
-        nc.gpsimd.memset(warm[:], 0.0)
-        for a in range(2):
-            nc.gpsimd.memset(planes[a][:].bitcast(I32), 0)
+        nc.vector.memset(tab_s[0:CALLER_ROWS].bitcast(I32), 0)
+        nc.gpsimd.memset(bias_rows[:], 0.0)
+        nc.gpsimd.memset(w4s_raw[96:CALLER_ROWS].bitcast(I32), 0)
+        nc.gpsimd.memset(caller_s[:].bitcast(I32), 0)
         make_identity(nc, ident[:])
-        nc.scalar.activation(warm[:, 4:8], warm[:, 0:4], RELU)
+        nc.gpsimd.memset(tab2_s[0:CALLEE_ROWS].bitcast(I32), 0)
+        nc.gpsimd.memset(tab2_s[64:P].bitcast(I32), 0)
+        nc.gpsimd.memset(w8s_raw[32:CALLEE_ROWS].bitcast(I32), 0)
+        nc.gpsimd.memset(callee_s[:].bitcast(I32), 0)
 
         def load(dst, src):
             nc.sync.dma_start(dst, src)
 
-        def load_scale_rows(dst, scales):
-            load(dst[0:32, :].bitcast(I32), scales.rearrange("a q n -> (a q) n").bitcast(I32))
+        def load_scale_rows(dst, first, scales):
+            load(dst[first : first + 16].bitcast(I32), scales.rearrange("a q n -> q a n").bitcast(I32))
 
         tab_w = {}
+        w4_raw = {}
+        w1_raw = {}
+        wo_raw = {}
 
         def load_tab_words(a):
-            tab_w[a] = placed("tab_w%d" % a, [P, T], I32, 16 * a)
+            tab_w[a] = placed("tab_w%d" % a, [P, T], I32, AT_TABLE[a])
             load(tab_w[a][:], tab_words[a].rearrange("p t i -> p (t i)").bitcast(I32))
-
-        w4_raw = {}
 
         def load_w4(b, tile):
             w4_raw[b] = tile
-            load(w4_raw[b][:].bitcast(I32), w4_words[:, :, H * b : H * (b + 1)].rearrange("a p e -> p a e").bitcast(I32))
-
-        w1_raw = {}
+            load(tile[:].bitcast(I32), w4_words[:, :, H * b : H * (b + 1)].rearrange("a p e -> p a e").bitcast(I32))
 
         def load_w1(a, b, tile):
             w1_raw[a, b] = tile
-            load(w1_raw[a, b][:], w1[512 * a : 512 * (a + 1), 512 * b : 512 * (b + 1)].rearrange("(p j) c -> p j c", j=4))
+            load(tile[:], w1[512 * a : 512 * (a + 1), 512 * b : 512 * (b + 1)].rearrange("(p j) c -> p j c", j=4))
 
-        def load_packed_planes(dst, scales, quadrant):
-            load(dst[32 * quadrant + 4 : 32 * quadrant + 12, :].bitcast(I32), scales[:, 4 * quadrant : 4 * quadrant + 4, :].bitcast(I32))
+        def load_wo(b, kib):
+            wo_raw[b] = placed("wo_raw%d" % b, [P, 4, N], F32, kib)
+            for t in range(4):
+                load(wo_raw[b][:, t, :], wo[512 * b : 512 * (b + 1), :].rearrange("(q t e) n -> t q e n", t=4, e=8)[t])
 
         load(offs_t[:], offs)
-        load_scale_rows(tab_s, tab_scales)
-        load_scale_rows(w4s_raw, w4_scales)
+        load_scale_rows(tab_s, CALLER_ROWS, tab_scales)
+        load_scale_rows(w4s_raw, CALLER_ROWS, w4_scales)
         load(offs2_t[:], offs2)
         load(pos_t[:], pos1)
         load_w4(0, held("w4_raw0", [P, 2, H], U8))
         load(bias_rows[0:2, :], b1.rearrange("(b c) -> b c", b=2))
         load_tab_words(0)
-        for quadrant in range(4):
-            load_packed_planes(tab2_s, tab2_scales, quadrant)
-        for quadrant in range(2):
-            load_packed_planes(w8s_raw, w8_scales, quadrant)
+        load_scale_rows(tab2_s, CALLEE_ROWS, tab2_scales)
+        load_scale_rows(w8s_raw, CALLEE_ROWS, w8_scales)
         load_w1(0, 0, held("w1_raw00", [P, 4, 512], F32))
-        for quadrant in range(2, 4):
-            load_packed_planes(w8s_raw, w8_scales, quadrant)
 
         def deal_scales(dst, raw):
-            nc.vector.tensor_copy(dst.bitcast(I32).rearrange("p (b t q i) -> p b t q i", b=2, t=4, i=2),
-                                  raw.bitcast(I32).rearrange("p (b q t i) -> p b t q i", b=2, t=4, i=2))
+            nc.vector.tensor_copy(dst.bitcast(I32).rearrange("p (b t q i) -> p b t q i", t=4, q=16, i=2),
+                                  raw.bitcast(I32).rearrange("p (b q t i) -> p b t q i", t=4, q=16, i=2))
 
-        stage = placed("stage", [32, ROW], U8, 32)
-        v_s = placed("v_s", [P, S], U8, 16)
-        nc.vector.tensor_copy(v_s[:], tab_s[:].indirect(offs_t[:]))
-        deal_scales(stage[:, W4_AT : W4_AT + H], w4s_raw[:])
-        nc.vector.tensor_copy(stage[:, V_AT : V_AT + S].bitcast(I32), v_s[0:32, :].bitcast(I32))
-
-        def move_scale_rows(a):
-            for r in range(4):
-                nc.sync.dma_start(planes[a][r:P:32, :].bitcast(I32), stage[16 * a + r : 16 * a + 16 : 4, :].bitcast(I32))
-
-        move_scale_rows(0)
+        stage = placed("stage", [P, 2, CALLER_WIDTH], U8, AT_STAGE)
+        v_s = placed("v_s", [P, 2, S], U8, AT_V_SCALES)
+        for a in range(2):
+            nc.vector.tensor_copy(v_s[:, a, :], tab_s[:, a, :].indirect(offs_t[:]))
+            deal_scales(stage[96:P, a, W4_AT : W4_AT + H], w4s_raw[96:P, a, :])
+        nc.vector.tensor_copy(stage[96:P, :, V_AT : V_AT + S].bitcast(I32), v_s[96:P].bitcast(I32))
+        for s in range(4):
+            load(caller_s[s:P:32].bitcast(I32), stage[CALLER_ROWS + s : P : 4].bitcast(I32))
         load_tab_words(1)
-        move_scale_rows(1)
-        w4_p = {}
-        w8_p = {}
 
-        def reorder(dst, src, b, run):
-            width = 64 * run
-            nc.vector.tensor_copy(dst.rearrange("p a (t q i) -> p a t q i", t=4, i=run),
-                                  src[:, :, b * width : (b + 1) * width].rearrange("p a (q t i) -> p a t q i", t=4, i=run))
+        w4_dealt = {}
+        w8_dealt = {}
 
-        def reorder_w4(b, lo, hi, where):
-            dealt = tenant("w4_p%d%d" % (b, lo), [P, 2, 2 * P * (hi - lo)], U8, where)
+        def deal_w4(b, lo, hi, dealt):
             nc.vector.tensor_copy(dealt[:].bitcast(I32).rearrange("p a (t q i) -> p a t q i", q=16, i=4),
                                   w4_raw[b][:].bitcast(I32).rearrange("p a (q t i) -> p a t q i", t=4, i=4)[:, :, lo:hi])
             for t in range(lo, hi):
-                w4_p[b, t] = dealt[:, :, 2 * P * (t - lo) : 2 * P * (t - lo + 1)]
+                w4_dealt[4 * b + t] = dealt[:, :, 2 * P * (t - lo) : 2 * P * (t - lo + 1)]
 
-        def reorder_w8(b):
-            w8_p[b] = tenant("w8_p%d" % b, [P, 2, H // 2], I32, ("y10", "y31")[b])
-            reorder(w8_p[b][:], w8_raw[:], b, 8)
+        def deal_w8(b, dealt):
+            w8_dealt[b] = dealt
+            nc.vector.tensor_copy(dealt[:].rearrange("p a (t q e) -> p a t q e", t=4, e=8),
+                                  w8_raw[:, :, 512 * b : 512 * (b + 1)].rearrange("p a (q t e) -> p a t q e", t=4, e=8))
 
-        reorder_w4(0, 0, 1, "w4_p00")
+        deal_w4(0, 0, 1, held("w4_first", [P, 2, 2 * P], U8))
 
         v_w = {(a, hf): held("v_w%d%d" % (a, hf), [P, BANK], U32) for a in range(2) for hf in range(2)}
 
-        def gather_words(a, hf):
-            nc.vector.tensor_copy(v_w[a, hf][:], tab_w[a][:].bitcast(U32).indirect(offs_t[:, 32 * hf : 32 * (hf + 1)]))
+        def gather_callers(a):
+            for hf in range(2):
+                nc.vector.tensor_copy(v_w[a, hf][:], tab_w[a][:].bitcast(U32).indirect(offs_t[:, 32 * hf : 32 * (hf + 1)]))
 
-        gather_words(0, 0)
-        gather_words(0, 1)
-        load_w1(1, 0, placed("w1_raw10", [P, 4, 512], F32, 0))
-        tab2_w = placed("tab2_w", [P, 2, T2], I32, 8)
+        gather_callers(0)
+        load_w1(1, 0, placed("w1_raw10", [P, 4, 512], F32, AT_W1_PASS1))
+        tab2_w = placed("tab2_w", [P, 2, T2], I32, AT_TABLE2)
         load(tab2_w[:], tab2_words.rearrange("a p t i -> p a (t i)").bitcast(I32))
-        load_w4(1, placed("w4_raw1", [P, 2, H], U8, 32))
-        v2_s = held("v2_s", [P, M], U8)
-        w8_s = held("w8_s", [P, H], U8)
-        nc.vector.tensor_copy(v2_s[:], tab2_s[:].indirect(offs2_t[:]))
-        deal_scales(w8_s[:], w8s_raw[:])
+        load_w4(1, placed("w4_raw1", [P, 2, H], U8, AT_STAGE))
 
-        def gather_callees(a):
-            nc.vector.tensor_copy(v2_w[:, a, :], tab2_w[:, a, :].bitcast(U32).indirect(offs2_t[:]))
+        v2_s = placed("v2_s", [P, 2, M], U8, AT_V2_SCALES)
+        stage2 = held("stage2", [P, 2, CALLEE_WIDTH], U8)
+        for a in range(2):
+            nc.vector.tensor_copy(v2_s[:, a, :], tab2_s[:, a, :].indirect(offs2_t[:]))
+            deal_scales(stage2[32:64, a, W8_AT : W8_AT + H], w8s_raw[32:64, a, :])
+        nc.vector.tensor_copy(stage2[32:64, :, V2_AT : V2_AT + M].bitcast(I32), v2_s[32:64].bitcast(I32))
+        for s in range(4):
+            load(callee_s[4 + s : P : 32].bitcast(I32), stage2[CALLEE_ROWS + s : 64 : 4].bitcast(I32))
 
-        bias_ps = psum.tile([P, BANK], F32, name="bias_ps", tag="pb", bufs=2)
-        nc.scalar.copy(bias_dealt[:].rearrange("p t (q i) -> p t q i", i=8), bias_rows[:].rearrange("p (q t i) -> p t q i", t=4, i=8))
+        bias_ps = psum.tile([P, BANK], F32, name="bias_ps", tag="callee", bufs=2)
+        nc.scalar.copy(bias_dealt[:].rearrange("p t (q e) -> p t q e", e=8), bias_rows[:].rearrange("p (q t e) -> p t q e", t=4, e=8))
         for t in range(4):
             nc.tensor.transpose(bias_ps[:, P * t : P * (t + 1)], bias_dealt[:, t, :], ident[:])
         by_tile = bias_ps[:].rearrange("p (t b) -> p b t", t=4)[:, 0:2, :]
         nc.scalar.copy(bias[:].rearrange("p (b t) -> p b t", b=2), by_tile)
-        nc.scalar.mul(minus_bias[:].rearrange("p (b t) -> p b t", b=2), by_tile, -1.0)
+        nc.scalar.activation(minus_bias[:].rearrange("p (b t) -> p b t", b=2), by_tile, IDENTITY, scale=-1.0)
 
         w1_c = {(a, b): held("w1_c%d%d" % (a, b), [P, 512], U32) for a in range(2) for b in range(2)}
         w1_s = {(a, b): held("w1_s%d%d" % (a, b), [P, 512], U8) for a in range(2) for b in range(2)}
-        w1_g = {}
+        w1_rounded = {}
 
-        def cast_w1(a, b, t, first, count, tag):
-            if t == first:
-                w1_g[a, b, first] = tenant("w1_g%d%d%d" % (a, b, first), [P, 512 * count], BF16, tag)
-            copy = nc.vector.tensor_copy if (a, b, t) == (1, 0, 0) else nc.scalar.copy
-            copy(w1_g[a, b, first][:, 512 * (t - first) : 512 * (t - first + 1)].rearrange("p (q u i j) -> p q u j i", u=2, i=4, j=4),
-                 w1_raw[a, b][:].rearrange("p j (q t u i) -> p t q u j i", t=4, u=2, i=4)[:, t])
-
-        def round_w1(a, b, first, count, tag):
-            for t in range(first, first + count):
-                cast_w1(a, b, t, first, count, tag)
+        def round_w1(a, b, lo, hi, rounded, copy=nc.scalar.copy):
+            w1_rounded[a, b, lo] = rounded
+            copy(rounded[:].rearrange("p (t q e j) -> p t q j e", q=16, e=8, j=4),
+                 w1_raw[a, b][:].rearrange("p j (q t e) -> p t q j e", t=4, e=8)[:, lo:hi])
 
         def quantize_w1(a, b, lo, hi):
             cols = slice(P * lo, P * hi)
-            nc.vector.quantize_mx(out=w1_c[a, b][:, cols].bitcast(FP8X4), scales=w1_s[a, b][:, cols], in_=w1_g[a, b, lo][:])
+            nc.vector.quantize_mx(out=w1_c[a, b][:, cols].bitcast(FP8X4), scales=w1_s[a, b][:, cols], in_=w1_rounded[a, b, lo][:])
 
-        wo_g = {}
-        wo_raw = {}
-        wo_c = held("wo_c", [P, 2 * N], U32)
+        wo_rounded = {}
         wo_s = held("wo_s", [P, 2 * N], U8)
 
-        def cast_wo(b):
-            wo_g[b] = slot("wo_g%d" % b, [P, N, 4], BF16, ("y21", "y61")[b])
-            nc.scalar.copy(wo_g[b][:].rearrange("p (c i) t -> p c t i", i=4), wo_raw[b][:].rearrange("p t (c i) -> p c t i", i=4))
+        def round_wo(b, rounded):
+            wo_rounded[b] = rounded
+            nc.scalar.copy(rounded[:].rearrange("p (c i) t -> p c t i", i=4), wo_raw[b][:].rearrange("p t (c i) -> p c t i", i=4))
 
         def quantize_wo(b):
-            flat = wo_g[b][:].rearrange("p n t -> p (n t)")
-            for lo, hi in ((0, 256), (256, 384)):
+            flat = wo_rounded[b][:].rearrange("p n t -> p (n t)")
+            for lo, hi in ((0, 256), (256, N)):
                 nc.vector.quantize_mx(out=wo_c[:, N * b + lo : N * b + hi].bitcast(FP8X4), scales=wo_s[:, N * b + lo : N * b + hi], in_=flat[:, 4 * lo : 4 * hi])
 
-        def load_wo(b, kib):
-            wo_raw[b] = placed("wo_raw%d" % b, [P, 4, N], F32, kib)
-            for t in range(4):
-                load(wo_raw[b][:, t, :], wo[512 * b : 512 * (b + 1), :].rearrange("(q t i) n -> t q i n", t=4, i=8)[t])
-
-        round_w1(0, 0, 0, 4, "w1_g00")
+        round_w1(0, 0, 0, 4, held("w1_rounded00", [P, 2048], BF16))
         quantize_w1(0, 0, 0, 4)
-        gather_words(1, 0)
-        gather_words(1, 1)
-        w8_raw = placed("w8_raw", [P, 2, H], I32, 16)
+        gather_callers(1)
+        w8_raw = placed("w8_raw", [P, 2, H], I32, AT_W8)
         load(w8_raw[:], w8_words.rearrange("a p e i -> p a (e i)").bitcast(I32))
-        load_w1(0, 1, placed("w1_raw01", [P, 4, 512], F32, 24))
-
-        x_pre = {}
-        picked = {}
-        own = {}
-        own_sb = {}
-        diff = [held("diff%d" % b, [P, 4, M], F32) for b in range(2)]
+        load_w1(0, 1, placed("w1_raw01", [P, 4, 512], F32, AT_W1_PASS0))
 
         y = {}
         summed = {}
+        window = {}
+        picked = {}
+        own = {}
+        own_copy = {}
+        minus_excess = [held("minus_excess%d" % b, [P, 4, M], F32) for b in range(2)]
 
-        def moving(a, hf):
-            return dict(rhs=v_w[a, hf][:].bitcast(FP8X4), rhs_scale=planes[a][:, V_AT + BANK * hf : V_AT + BANK * (hf + 1)], start=(a == 0), stop=(a == 1))
+        def callers(a, hf):
+            return dict(rhs=v_w[a, hf][:].bitcast(FP8X4), rhs_scale=caller_s[:, a, V_AT + BANK * hf : V_AT + BANK * (hf + 1)], start=(a == 0), stop=(a == 1))
 
-        def fp4_half(b, t, hf):
-            n = 4 * b + t
-            p4 = psum.tile([P, BANK], F32, name="p4", tag="p4")
-            for a in range(2):
-                nc.tensor.matmul_mx(out=p4[:], lhsT=w4_p[b, t][:, a, :].bitcast(FP4X4), lhsT_scale=planes[a][:, W4_AT + P * n : W4_AT + P * (n + 1)], **moving(a, hf))
-            y[n, hf] = tenant("y_%d%d" % (n, hf), [P, BANK], F32, ("at", 44) if n + hf == 0 else "y%d%d" % (n, hf))
-            nc.scalar.activation(y[n, hf][:], p4[:], IDENTITY, bias=bias[:, n : n + 1])
+        def w4_product(n):
+            for hf in range(2):
+                p4 = psum.tile([P, BANK], F32, name="p4", tag="p4")
+                for a in range(2):
+                    nc.tensor.matmul_mx(out=p4[:], lhsT=w4_dealt[n][:, a, :].bitcast(FP4X4), lhsT_scale=caller_s[:, a, W4_AT + P * n : W4_AT + P * (n + 1)], **callers(a, hf))
+                y[n, hf] = placed("y_first", [P, BANK], F32, AT_FIRST_Y) if (n, hf) == (0, 0) else after_y(n, hf, "y", [P, BANK], F32)
+                nc.scalar.activation(y[n, hf][:], p4[:], IDENTITY, bias=bias[:, n : n + 1])
 
-        def caller_half(b, t, hf):
+        def w1_product(n, hf):
+            b, t = divmod(n, 4)
             cols = slice(P * t, P * (t + 1))
-            n = 4 * b + t
             p1 = psum.tile([P, BANK], F32, name="p1", tag="p1")
             for a in range(2):
-                nc.tensor.matmul_mx(out=p1[:], lhsT=w1_c[a, b][:, cols].bitcast(FP8X4), lhsT_scale=w1_s[a, b][:, cols], **moving(a, hf))
+                nc.tensor.matmul_mx(out=p1[:], lhsT=w1_c[a, b][:, cols].bitcast(FP8X4), lhsT_scale=w1_s[a, b][:, cols], **callers(a, hf))
             if hf == 0:
-                x_pre[b, t] = ring.tile([P, S], F32, name="x_pre", bufs=3)
-            if n in FUSED:
-                summed[n, hf] = ring.tile([P, BANK], F32, name="summed", bufs=3)
-                target = summed[n, hf][:]
-            else:
-                target = x_pre[b, t][:, BANK * hf : BANK * (hf + 1)]
+                window[n] = ring.tile([P, S], F32, name="window", bufs=3)
+                if n in FUSED:
+                    summed[n] = ring.tile([P, S], F32, name="summed", bufs=2)
+            target = (summed[n] if n in FUSED else window[n])[:, BANK * hf : BANK * (hf + 1)]
             nc.vector.scalar_tensor_tensor(target, p1[:], minus_bias[:, n : n + 1], y[n, hf][:], ALU.max, ALU.add)
 
-        def second_relu(b, t, hf):
-            if 4 * b + t in FUSED:
-                nc.scalar.activation(x_pre[b, t][:, BANK * hf : BANK * (hf + 1)], summed[4 * b + t, hf][:], RELU)
-
-        def callee_product(b, t):
-            own[b, t] = psum.tile([P, BANK], F32, name="own", tag="pb", bufs=2)
+        def w8_product(n):
+            b, t = divmod(n, 4)
+            own[n] = psum.tile([P, BANK], F32, name="own", tag="callee", bufs=2)
             for a in range(2):
-                nc.tensor.matmul_mx(out=own[b, t][:], lhsT=w8_p[b][:, a, P * t : P * (t + 1)].bitcast(FP8X4),
-                                    lhsT_scale=w8_s[4 + 4 * a : P, 512 * b + P * t : 512 * b + P * (t + 1)],
-                                    rhs=v2_w[:, a, :].bitcast(FP8X4), rhs_scale=v2_s[4 + 4 * a : P, :], start=(a == 0), stop=(a == 1))
-            if 4 * b + t in FUSED:
-                own_sb[b, t] = ring.tile([P, M], F32, name="own_sb", bufs=2)
-                nc.scalar.copy(own_sb[b, t][:], own[b, t][:])
+                nc.tensor.matmul_mx(out=own[n][:], lhsT=w8_dealt[b][:, a, P * t : P * (t + 1)].bitcast(FP8X4),
+                                    lhsT_scale=callee_s[4:P, a, W8_AT + P * n : W8_AT + P * (n + 1)],
+                                    rhs=v2_w[:, a, :].bitcast(FP8X4), rhs_scale=callee_s[4:P, a, V2_AT : V2_AT + M], start=(a == 0), stop=(a == 1))
+            if n in FUSED:
+                own_copy[n] = ring.tile([P, M], F32, name="own_copy", bufs=2)
+                nc.scalar.copy(own_copy[n][:], own[n][:])
 
-        def pick(b, t, lo, hi):
-            if 4 * b + t in FUSED:
-                return
-            picked[b, t, lo] = ring.tile([P, hi - lo], F32, name="picked", bufs=4)
-            nc.vector.tensor_copy(picked[b, t, lo][:], x_pre[b, t][:].indirect(pos_t[:, lo // 16 : hi // 16]))
+        def pick(n, lo, hi, tile):
+            picked[n, lo] = tile
+            nc.vector.tensor_copy(tile[:], window[n][:].indirect(pos_t[:, lo // 16 : hi // 16]))
 
-        def subtract(b, t, lo, hi):
-            if 4 * b + t in FUSED:
-                nc.vector.tensor_tensor(diff[b][:, t, lo:hi], x_pre[b, t][:].indirect(pos_t[:, lo // 16 : hi // 16]), own_sb[b, t][:, lo:hi], ALU.subtract)
-                return
-            nc.vector.scalar_tensor_tensor(diff[b][:, t, lo:hi], picked[b, t, lo][:], 0.0, own[b, t][:, lo:hi], ALU.max, ALU.subtract)
+        def subtract(n, lo, hi):
+            b, t = divmod(n, 4)
+            if n in FUSED:
+                nc.vector.tensor_tensor(minus_excess[b][:, t, lo:hi], window[n][:].indirect(pos_t[:, lo // 16 : hi // 16]), own_copy[n][:, lo:hi], ALU.subtract)
+            else:
+                nc.vector.scalar_tensor_tensor(minus_excess[b][:, t, lo:hi], picked[n, lo][:], 0.0, own[n][:, lo:hi], ALU.max, ALU.subtract)
 
-        h_g = {}
+        h_rounded = {}
         h_c = {}
         h_s = {}
 
-        def views(b, lo, hi):
-            h_g[b, lo] = held("h_g%d_%d" % (b, lo), [P, hi - lo, 4], BF16)
-            return (h_g[b, lo][:].rearrange("p (c i) t -> p c t i", i=4), diff[b][:, :, lo:hi].rearrange("p t (c i) -> p c t i", i=4))
+        def h_views(b, lo):
+            h_rounded[b, lo] = held("h_rounded%d_%d" % (b, lo), [P, PIECE, 4], BF16)
+            return (h_rounded[b, lo][:].rearrange("p (c i) t -> p c t i", i=4),
+                    minus_excess[b][:, :, lo : lo + PIECE].rearrange("p t (c i) -> p c t i", i=4))
 
-        def relu_scalar(b, lo, hi):
-            dst, src = views(b, lo, hi)
+        def round_h(b, lo):
+            dst, src = h_views(b, lo)
             nc.scalar.activation(dst, src, RELU, scale=-1.0)
 
-        def relu_vector(b, lo, hi):
-            dst, src = views(b, lo, hi)
-            nc.vector.tensor_scalar(dst, src, -1.0, 0.0, ALU.mult, ALU.max)
+        def quantize_h(b, lo):
+            h_c[b, lo] = held("h_c%d_%d" % (b, lo), [P, PIECE], U32)
+            h_s[b, lo] = held("h_s%d_%d" % (b, lo), [P, PIECE], U8)
+            nc.vector.quantize_mx(out=h_c[b, lo][:].bitcast(FP8X4), scales=h_s[b, lo][:], in_=h_rounded[b, lo][:].rearrange("p m t -> p (m t)"))
 
-        def quantize_h(b, lo, hi):
-            h_c[b, lo] = held("h_c%d_%d" % (b, lo), [P, hi - lo], U32)
-            h_s[b, lo] = held("h_s%d_%d" % (b, lo), [P, hi - lo], U8)
-            nc.vector.quantize_mx(out=h_c[b, lo][:].bitcast(FP8X4), scales=h_s[b, lo][:], in_=h_g[b, lo][:].rearrange("p m t -> p (m t)"))
+        def late_pieces(n):
+            return [(i % 2, 2 * (i // 2), (3 + i) % 2) for i in range(4) if (3 + i) // 2 == n]
 
-        tiles = [(b, t) for b in range(2) for t in range(4)]
-        late = {1: ((0, 0, "y11"),), 2: ((1, 0, "y20"), (0, 2, "y21")), 3: ((1, 2, "y30"),)}
-        fp4_half(0, 0, 0)
-        fp4_half(0, 0, 1)
-        fp4_ahead = [(1, 2, 3), (4,), (5,), (6,), (7,), (), (), ()]
-        round_w1(1, 0, 0, 1, ("at", 40))
+        w4_product(0)
+        round_w1(1, 0, 0, 1, placed("w1_rounded100", [P, 512], BF16, AT_FIRST_ROUNDED), copy=nc.vector.tensor_copy)
         quantize_w1(1, 0, 0, 1)
-        reorder_w4(0, 1, 4, ("at", 40))
-        for n, (b, t) in enumerate(tiles):
-            caller_half(b, t, 0)
-            for ahead in fp4_ahead[n][:1]:
-                fp4_half(*tiles[ahead], 0)
-                fp4_half(*tiles[ahead], 1)
-            if n > 0:
-                second_relu(*tiles[n - 1], 1)
+        deal_w4(0, 1, 4, placed("w4_rest", [P, 2, 6 * P], U8, AT_FIRST_ROUNDED))
+
+        for n in range(TILES):
+            ahead = range(1, AHEAD + 1) if n == 0 else range(n + AHEAD, min(n + AHEAD + 1, TILES))
+            w1_product(n, 0)
+            for later in ahead[:1]:
+                w4_product(later)
             if n > 1:
-                callee_product(*tiles[n - 1])
-            if n > 0:
-                pick(*tiles[n - 1], 0, M)
+                w8_product(n - 1)
+            if n > 0 and n - 1 not in FUSED:
+                pick(n - 1, 0, M, ring.tile([P, M], F32, name="picked", bufs=4))
             if n == 2:
-                subtract(*tiles[0], 0, M)
-            caller_half(b, t, 1)
-            for ahead in fp4_ahead[n][1:]:
-                fp4_half(*tiles[ahead], 0)
-                fp4_half(*tiles[ahead], 1)
-            second_relu(b, t, 0)
+                subtract(0, 0, M)
+            w1_product(n, 1)
+            for later in ahead[1:]:
+                w4_product(later)
+            if n in FUSED:
+                nc.scalar.activation(window[n][:], summed[n][:], RELU)
             if n == 0:
-                round_w1(1, 0, 1, 1, ("at", 45))
+                round_w1(1, 0, 1, 2, placed("w1_rounded101", [P, 512], BF16, AT_SECOND_ROUNDED))
                 quantize_w1(1, 0, 1, 2)
-                reorder_w4(1, 0, 4, ("at", 45.5))
-                v2_w = placed("v2_w", [P, 2, M], U32, 41.5)
-                gather_callees(0)
-                gather_callees(1)
-                load_w1(1, 1, placed("w1_raw11", [P, 4, 512], F32, 8))
+                deal_w4(1, 0, 4, placed("w4_second", [P, 2, H], U8, AT_W4_DEALT))
+                v2_w = placed("v2_w", [P, 2, M], U32, AT_V2_WORDS)
+                for a in range(2):
+                    nc.vector.tensor_copy(v2_w[:, a, :], tab2_w[:, a, :].bitcast(U32).indirect(offs2_t[:]))
+                load_w1(1, 1, placed("w1_raw11", [P, 4, 512], F32, AT_TABLE2))
             if n == 1:
-                for tt, tag in ((2, "y01"), (3, "y10")):
-                    round_w1(1, 0, tt, 1, tag)
-                    quantize_w1(1, 0, tt, tt + 1)
-                load_wo(0, 0)
-                reorder_w8(0)
-                callee_product(*tiles[0])
-            for late_a, late_t, tag in late.get(n, ()):
-                round_w1(late_a, 1, late_t, 2, tag)
-            if n in (3, 7):
-                cast_wo(n // 7)
+                for t in (2, 3):
+                    round_w1(1, 0, t, t + 1, after_y(*divmod(t - 1, 2), "w1_rounded", [P, 512], BF16))
+                    quantize_w1(1, 0, t, t + 1)
+                load_wo(0, AT_W1_PASS1)
+                deal_w8(0, after_y(1, 0, "w8_dealt", [P, 2, 512], I32))
+                w8_product(0)
+            for a, t, hf in late_pieces(n):
+                round_w1(a, 1, t, t + 2, after_y(n, hf, "w1_rounded", [P, 1024], BF16))
+            if n in (FUSED[0], TILES - 1):
+                round_wo(n // (TILES - 1), after_y(n - 1, 1, "wo_rounded", [P, N, 4], BF16))
             if n > 1:
-                subtract(*tiles[n - 1], 0, M)
+                subtract(n - 1, 0, M)
             if n == 3:
-                reorder_w8(1)
-                load_wo(1, 16)
-            for late_a, late_t, tag in late.get(n, ()):
-                quantize_w1(late_a, 1, late_t, late_t + 2)
+                deal_w8(1, after_y(3, 1, "w8_dealt", [P, 2, 512], I32))
+                load_wo(1, AT_W8)
+            for a, t, hf in late_pieces(n):
+                quantize_w1(a, 1, t, t + 2)
             if n in (5, 6):
-                relu_scalar(0, 256 * (n - 5), 256 * (n - 4))
-            if n in (5, 7):
-                quantize_wo(n // 7)
+                round_h(0, PIECE * (n - 5))
             if n in (6, 7):
-                quantize_h(0, 256 * (n - 6), 256 * (n - 5))
+                quantize_h(0, PIECE * (n - 6))
 
-        callee_product(1, 3)
-        chunks = ((0, 256), (256, 384), (384, 512))
-        pick(1, 3, *chunks[0])
-        pick(1, 3, *chunks[1])
-        subtract(1, 3, *chunks[0])
-        relu_scalar(1, *chunks[0])
-        pick(1, 3, *chunks[2])
-        subtract(1, 3, *chunks[1])
-        subtract(1, 3, *chunks[2])
-        relu_vector(1, *chunks[1])
-        relu_vector(1, *chunks[2])
+        last = TILES - 1
+        w8_product(last)
+        pick(last, 0, PIECE, placed("last_picks", [P, PIECE], F32, AT_LAST_PICKS))
+        subtract(last, 0, PIECE)
+        wo_c = placed("wo_c", [P, 2 * N], U32, AT_LAST_PICKS)
+        quantize_wo(0)
+        pick(last, PIECE, M, ring.tile([P, PIECE], F32, name="picked", bufs=4))
+        subtract(last, PIECE, M)
+        quantize_wo(1)
+        round_h(1, 0)
+        dst, src = h_views(1, PIECE)
+        nc.vector.tensor_scalar(dst[:, 0:32], src[:, 0:32], -1.0, 0.0, ALU.mult, ALU.max)
+        nc.scalar.activation(dst[:, 32:64], src[:, 32:64], RELU, scale=-1.0)
 
-        def score_pass(dst, b, c3, lo, hi):
-            cols = slice(N * b + P * c3, N * b + P * (c3 + 1))
-            codes, scales = (h_c[0, lo - lo % 256][:, lo % 256 : lo % 256 + hi - lo], h_s[0, lo - lo % 256][:, lo % 256 : lo % 256 + hi - lo]) if b == 0 else (h_c[1, lo][:], h_s[1, lo][:])
-            nc.tensor.matmul_mx(out=dst, lhsT=wo_c[:, cols].bitcast(FP8X4), lhsT_scale=wo_s[:, cols],
-                                rhs=codes.bitcast(FP8X4), rhs_scale=scales, start=(b == 0), stop=(b == 1))
+        def score_pass(b, lo, c):
+            cols = slice(N * b + P * c, N * b + P * (c + 1))
+            nc.tensor.matmul_mx(out=scores[lo, c][:, 0:PIECE], lhsT=wo_c[:, cols].bitcast(FP8X4), lhsT_scale=wo_s[:, cols],
+                                rhs=h_c[b, lo][:].bitcast(FP8X4), rhs_scale=h_s[b, lo][:], start=(b == 0), stop=(b == 1))
 
-        out_rows = out.rearrange("(c p) m -> p c m", p=P)
-        wide = [psum.tile([P, BANK], F32, name="wide", tag="p1") for c3 in range(3)]
-        for c3 in range(3):
-            score_pass(wide[c3][:, 0:256], 0, c3, *chunks[0])
-        quantize_h(1, *chunks[0])
-        staged = held("staged0", [P, 3, 256], F32)
-        for c3 in range(3):
-            score_pass(wide[c3][:, 0:256], 1, c3, *chunks[0])
-            nc.scalar.copy(staged[:, c3, :], wide[c3][:, 0:256])
-        nc.sync.dma_start(out_rows[:, :, 0:256], staged[:])
-        for lo, hi in chunks[1:]:
-            quantize_h(1, lo, hi)
-        for lo, hi in chunks[1:]:
-            narrow = psum.tile([P, BANK], F32, name="narrow", tag="p4")
-            for c3 in range(3):
-                for b in range(2):
-                    score_pass(narrow[:, P * c3 : P * (c3 + 1)], b, c3, lo, hi)
-            staged = held("staged%d" % lo, [P, 3, P], F32)
-            copy = nc.vector.tensor_copy if hi == M else nc.scalar.copy
-            copy(staged[:].rearrange("p c m -> p (c m)"), narrow[:, 0 : 3 * P])
-            nc.sync.dma_start(out_rows[:, :, lo:hi], staged[:])
+        scores = {(lo, c): psum.tile([P, BANK], F32, name="scores", tag=tag) for lo, tag in ((0, "p1"), (PIECE, "p4")) for c in range(3)}
+        for lo, c in scores:
+            score_pass(0, lo, c)
+        for lo in (0, PIECE):
+            quantize_h(1, lo)
+        copies = [nc.scalar.copy, nc.scalar.copy, nc.vector.tensor_copy, nc.vector.tensor_copy, nc.scalar.copy, nc.vector.tensor_copy]
+        for copy, (lo, c) in zip(copies, scores):
+            score_pass(1, lo, c)
+            staged = held("staged%d_%d" % (lo, c), [P, PIECE], F32)
+            copy(staged[:], scores[lo, c][:, 0:PIECE])
+            nc.sync.dma_start(out[P * c : P * (c + 1), lo : lo + PIECE], staged[:])

@@ -79,15 +79,11 @@ def tile_list_excess_delay_causes_kernel(tc, tab_words, tab_scales, offs, pos1, 
         bias = held("bias", [P, TILES], F32)
         minus_bias = held("minus_bias", [P, TILES], F32)
 
-        nc.vector.memset(tab_s[0:CALLER_ROWS].bitcast(I32), 0)
         nc.gpsimd.memset(bias_rows[:], 0.0)
-        nc.gpsimd.memset(w4s_raw[96:CALLER_ROWS].bitcast(I32), 0)
-        nc.gpsimd.memset(caller_s[:].bitcast(I32), 0)
         make_identity(nc, ident[:])
-        nc.gpsimd.memset(tab2_s[0:CALLEE_ROWS].bitcast(I32), 0)
-        nc.gpsimd.memset(tab2_s[64:P].bitcast(I32), 0)
-        nc.gpsimd.memset(w8s_raw[32:CALLEE_ROWS].bitcast(I32), 0)
-        nc.gpsimd.memset(callee_s[:].bitcast(I32), 0)
+        nc.vector.memset(tab_s[0:CALLER_ROWS].bitcast(I32), 0)
+        nc.vector.memset(w4s_raw[96:CALLER_ROWS].bitcast(I32), 0)
+        nc.vector.memset(caller_s[:].bitcast(I32), 0)
 
         def load(dst, src):
             nc.sync.dma_start(dst, src)
@@ -171,6 +167,10 @@ def tile_list_excess_delay_causes_kernel(tc, tab_words, tab_scales, offs, pos1, 
         load(tab2_w[:], tab2_words.rearrange("a p t i -> p a (t i)").bitcast(I32))
         load_w4(1, placed("w4_raw1", [P, 2, H], U8, AT_STAGE))
 
+        nc.vector.memset(tab2_s[0:CALLEE_ROWS].bitcast(I32), 0)
+        nc.vector.memset(tab2_s[64:P].bitcast(I32), 0)
+        nc.vector.memset(w8s_raw[32:CALLEE_ROWS].bitcast(I32), 0)
+        nc.vector.memset(callee_s[:].bitcast(I32), 0)
         v2_s = placed("v2_s", [P, 2, M], U8, AT_V2_SCALES)
         stage2 = held("stage2", [P, 2, CALLEE_WIDTH], U8)
         for a in range(2):

@@ -22,27 +22,26 @@ P = 128
 BANK = 512
 PIECE = M // 2
 TILES = 8
-CALLER_ROWS = 112
-CALLEE_ROWS = 48
+RAW_ROWS = 112
 V_AT, W4_AT, CALLER_WIDTH = 0, S, S + H
 V2_AT, W8_AT, CALLEE_WIDTH = 0, M, M + H
 FUSED = range(3, 7)
 AHEAD = 3
 
-AT_V2_SCALES = 0.5
-AT_TABLE = (1, 18.5)
-AT_W1_PASS1 = 1.5
-AT_TABLE2 = 9.5
-AT_W8 = 18
-AT_V_SCALES = 19
-AT_W1_PASS0 = 26
-AT_FIRST_ROUNDED = 34
-AT_STAGE = 36
-AT_V2_WORDS = 41.5
-AT_FIRST_Y = 44
-AT_SECOND_ROUNDED = 45
-AT_W4_DEALT = 45.5
-AT_LAST_PICKS = 48
+AT_V2_SCALES = 3.0625
+AT_TABLE = (3, 21.5)
+AT_W1_PASS1 = 4.0625
+AT_TABLE2 = 12.0625
+AT_W8 = 21
+AT_V_SCALES = 22
+AT_W1_PASS0 = 29
+AT_FIRST_ROUNDED = 38
+AT_W4_RAW = 1.0625
+AT_V2_WORDS = 44.5
+AT_FIRST_Y = 47
+AT_SECOND_ROUNDED = 48
+AT_W4_DEALT = 48.5
+AT_LAST_PICKS = 51
 
 
 def tile_list_excess_delay_causes_kernel(tc, tab_words, tab_scales, offs, pos1, tab2_words, tab2_scales, offs2,
@@ -81,15 +80,16 @@ def tile_list_excess_delay_causes_kernel(tc, tab_words, tab_scales, offs, pos1, 
 
         nc.gpsimd.memset(bias_rows[:], 0.0)
         make_identity(nc, ident[:])
-        nc.vector.memset(tab_s[0:CALLER_ROWS].bitcast(I32), 0)
-        nc.vector.memset(w4s_raw[96:CALLER_ROWS].bitcast(I32), 0)
-        nc.vector.memset(caller_s[:].bitcast(I32), 0)
+        for raw in (tab_s, w4s_raw):
+            nc.vector.memset(raw[0:RAW_ROWS].bitcast(I32), 0)
+        for raw in (tab2_s, w8s_raw):
+            nc.gpsimd.memset(raw[0:RAW_ROWS].bitcast(I32), 0)
 
         def load(dst, src):
             nc.sync.dma_start(dst, src)
 
-        def load_scale_rows(dst, first, scales):
-            load(dst[first : first + 16].bitcast(I32), scales.rearrange("a q n -> q a n").bitcast(I32))
+        def load_scale_rows(dst, scales):
+            load(dst[RAW_ROWS:P].bitcast(I32), scales.rearrange("a q n -> q a n").bitcast(I32))
 
         tab_w = {}
         w4_raw = {}
@@ -114,29 +114,28 @@ def tile_list_excess_delay_causes_kernel(tc, tab_words, tab_scales, offs, pos1, 
                 load(wo_raw[b][:, t, :], wo[512 * b : 512 * (b + 1), :].rearrange("(q t e) n -> t q e n", t=4, e=8)[t])
 
         load(offs_t[:], offs)
-        load_scale_rows(tab_s, CALLER_ROWS, tab_scales)
-        load_scale_rows(w4s_raw, CALLER_ROWS, w4_scales)
+        load_scale_rows(tab_s, tab_scales)
+        load_scale_rows(w4s_raw, w4_scales)
         load(offs2_t[:], offs2)
         load(pos_t[:], pos1)
         load_w4(0, held("w4_raw0", [P, 2, H], U8))
         load(bias_rows[0:2, :], b1.rearrange("(b c) -> b c", b=2))
         load_tab_words(0)
-        load_scale_rows(tab2_s, CALLEE_ROWS, tab2_scales)
-        load_scale_rows(w8s_raw, CALLEE_ROWS, w8_scales)
+        load_scale_rows(tab2_s, tab2_scales)
+        load_scale_rows(w8s_raw, w8_scales)
         load_w1(0, 0, held("w1_raw00", [P, 4, 512], F32))
 
         def deal_scales(dst, raw):
             nc.vector.tensor_copy(dst.bitcast(I32).rearrange("p (b t q i) -> p b t q i", t=4, q=16, i=2),
                                   raw.bitcast(I32).rearrange("p (b q t i) -> p b t q i", t=4, q=16, i=2))
 
-        stage = placed("stage", [P, 2, CALLER_WIDTH], U8, AT_STAGE)
         v_s = placed("v_s", [P, 2, S], U8, AT_V_SCALES)
         for a in range(2):
             nc.vector.tensor_copy(v_s[:, a, :], tab_s[:, a, :].indirect(offs_t[:]))
-            deal_scales(stage[96:P, a, W4_AT : W4_AT + H], w4s_raw[96:P, a, :])
-        nc.vector.tensor_copy(stage[96:P, :, V_AT : V_AT + S].bitcast(I32), v_s[96:P].bitcast(I32))
+            deal_scales(caller_s[:, a, W4_AT : W4_AT + H], w4s_raw[:, a, :])
+        nc.vector.tensor_copy(caller_s[:, :, V_AT : V_AT + S].bitcast(I32), v_s[:].bitcast(I32))
         for s in range(4):
-            load(caller_s[s:P:32].bitcast(I32), stage[CALLER_ROWS + s : P : 4].bitcast(I32))
+            load(caller_s[s:P:32].bitcast(I32), caller_s[RAW_ROWS + s : P : 4].bitcast(I32))
         load_tab_words(1)
 
         w4_dealt = {}
@@ -165,20 +164,15 @@ def tile_list_excess_delay_causes_kernel(tc, tab_words, tab_scales, offs, pos1, 
         load_w1(1, 0, placed("w1_raw10", [P, 4, 512], F32, AT_W1_PASS1))
         tab2_w = placed("tab2_w", [P, 2, T2], I32, AT_TABLE2)
         load(tab2_w[:], tab2_words.rearrange("a p t i -> p a (t i)").bitcast(I32))
-        load_w4(1, placed("w4_raw1", [P, 2, H], U8, AT_STAGE))
+        load_w4(1, placed("w4_raw1", [P, 2, H], U8, AT_W4_RAW))
 
-        nc.vector.memset(tab2_s[0:CALLEE_ROWS].bitcast(I32), 0)
-        nc.vector.memset(tab2_s[64:P].bitcast(I32), 0)
-        nc.vector.memset(w8s_raw[32:CALLEE_ROWS].bitcast(I32), 0)
-        nc.vector.memset(callee_s[:].bitcast(I32), 0)
         v2_s = placed("v2_s", [P, 2, M], U8, AT_V2_SCALES)
-        stage2 = held("stage2", [P, 2, CALLEE_WIDTH], U8)
         for a in range(2):
             nc.vector.tensor_copy(v2_s[:, a, :], tab2_s[:, a, :].indirect(offs2_t[:]))
-            deal_scales(stage2[32:64, a, W8_AT : W8_AT + H], w8s_raw[32:64, a, :])
-        nc.vector.tensor_copy(stage2[32:64, :, V2_AT : V2_AT + M].bitcast(I32), v2_s[32:64].bitcast(I32))
+            deal_scales(callee_s[:, a, W8_AT : W8_AT + H], w8s_raw[:, a, :])
+        nc.vector.tensor_copy(callee_s[:, :, V2_AT : V2_AT + M].bitcast(I32), v2_s[:].bitcast(I32))
         for s in range(4):
-            load(callee_s[4 + s : P : 32].bitcast(I32), stage2[CALLEE_ROWS + s : 64 : 4].bitcast(I32))
+            load(callee_s[4 + s : P : 32].bitcast(I32), callee_s[RAW_ROWS + s : P : 4].bitcast(I32))
 
         bias_ps = psum.tile([P, BANK], F32, name="bias_ps", tag="callee", bufs=2)
         nc.scalar.copy(bias_dealt[:].rearrange("p t (q e) -> p t q e", e=8), bias_rows[:].rearrange("p (q t e) -> p t q e", t=4, e=8))

@@ -30,12 +30,12 @@ AHEAD = 3
 
 AT_V2_SCALES = 3.0625
 AT_TABLE = (3, 21.5)
-AT_W1_PASS1 = 4.0625
+AT_W1_PASS1 = 55.9375
 AT_TABLE2 = 12.0625
 AT_W8 = 21
-AT_V_SCALES = 22
+AT_V_SCALES = 54
 AT_W1_PASS0 = 29
-AT_FIRST_ROUNDED = 38
+AT_FIRST_ROUNDED = 37
 AT_W4_RAW = 1.0625
 AT_V2_WORDS = 44.5
 AT_FIRST_Y = 47
@@ -117,13 +117,14 @@ def tile_list_excess_delay_causes_kernel(tc, tab_words, tab_scales, offs, pos1, 
         load_scale_rows(tab_s, tab_scales)
         load_scale_rows(w4s_raw, w4_scales)
         load(offs2_t[:], offs2)
-        load(pos_t[:], pos1)
-        load_w4(0, held("w4_raw0", [P, 2, H], U8))
-        load(bias_rows[0:2, :], b1.rearrange("(b c) -> b c", b=2))
         load_tab_words(0)
         load_scale_rows(tab2_s, tab2_scales)
         load_scale_rows(w8s_raw, w8_scales)
+        load(bias_rows[0:2, :], b1.rearrange("(b c) -> b c", b=2))
+        load_w4(0, held("w4_raw0", [P, 2, H], U8))
         load_w1(0, 0, held("w1_raw00", [P, 4, 512], F32))
+        load_tab_words(1)
+        load(pos_t[:], pos1)
 
         def deal_scales(dst, raw):
             nc.vector.tensor_copy(dst.bitcast(I32).rearrange("p (b t q i) -> p b t q i", t=4, q=16, i=2),
@@ -136,7 +137,7 @@ def tile_list_excess_delay_causes_kernel(tc, tab_words, tab_scales, offs, pos1, 
         nc.vector.tensor_copy(caller_s[:, :, V_AT : V_AT + S].bitcast(I32), v_s[:].bitcast(I32))
         for s in range(4):
             load(caller_s[s:P:32].bitcast(I32), caller_s[RAW_ROWS + s : P : 4].bitcast(I32))
-        load_tab_words(1)
+        load_w1(1, 0, placed("w1_raw10", [P, 4, 512], F32, AT_W1_PASS1))
 
         w4_dealt = {}
         w8_dealt = {}
@@ -161,7 +162,6 @@ def tile_list_excess_delay_causes_kernel(tc, tab_words, tab_scales, offs, pos1, 
                 nc.vector.tensor_copy(v_w[a, hf][:], tab_w[a][:].bitcast(U32).indirect(offs_t[:, 32 * hf : 32 * (hf + 1)]))
 
         gather_callers(0)
-        load_w1(1, 0, placed("w1_raw10", [P, 4, 512], F32, AT_W1_PASS1))
         tab2_w = placed("tab2_w", [P, 2, T2], I32, AT_TABLE2)
         load(tab2_w[:], tab2_words.rearrange("a p t i -> p a (t i)").bitcast(I32))
         load_w4(1, placed("w4_raw1", [P, 2, H], U8, AT_W4_RAW))
@@ -225,26 +225,38 @@ def tile_list_excess_delay_causes_kernel(tc, tab_words, tab_scales, offs, pos1, 
         def callers(a, hf):
             return dict(rhs=v_w[a, hf][:].bitcast(FP8X4), rhs_scale=caller_s[:, a, V_AT + BANK * hf : V_AT + BANK * (hf + 1)], start=(a == 0), stop=(a == 1))
 
+        p4 = {}
+        p1 = {}
+
+        def w4_pass(n, hf, a):
+            if a == 0:
+                p4[n, hf] = psum.tile([P, BANK], F32, name="p4", tag="p4")
+            nc.tensor.matmul_mx(out=p4[n, hf][:], lhsT=w4_dealt[n][:, a, :].bitcast(FP4X4), lhsT_scale=caller_s[:, a, W4_AT + P * n : W4_AT + P * (n + 1)], **callers(a, hf))
+            if a == 1:
+                y[n, hf] = placed("y_first", [P, BANK], F32, AT_FIRST_Y) if (n, hf) == (0, 0) else after_y(n, hf, "y", [P, BANK], F32)
+                nc.scalar.activation(y[n, hf][:], p4[n, hf][:], IDENTITY, bias=bias[:, n : n + 1])
+
         def w4_product(n):
             for hf in range(2):
-                p4 = psum.tile([P, BANK], F32, name="p4", tag="p4")
                 for a in range(2):
-                    nc.tensor.matmul_mx(out=p4[:], lhsT=w4_dealt[n][:, a, :].bitcast(FP4X4), lhsT_scale=caller_s[:, a, W4_AT + P * n : W4_AT + P * (n + 1)], **callers(a, hf))
-                y[n, hf] = placed("y_first", [P, BANK], F32, AT_FIRST_Y) if (n, hf) == (0, 0) else after_y(n, hf, "y", [P, BANK], F32)
-                nc.scalar.activation(y[n, hf][:], p4[:], IDENTITY, bias=bias[:, n : n + 1])
+                    w4_pass(n, hf, a)
 
-        def w1_product(n, hf):
+        def w1_pass(n, hf, a):
             b, t = divmod(n, 4)
             cols = slice(P * t, P * (t + 1))
-            p1 = psum.tile([P, BANK], F32, name="p1", tag="p1")
-            for a in range(2):
-                nc.tensor.matmul_mx(out=p1[:], lhsT=w1_c[a, b][:, cols].bitcast(FP8X4), lhsT_scale=w1_s[a, b][:, cols], **callers(a, hf))
+            if a == 0:
+                p1[n, hf] = psum.tile([P, BANK], F32, name="p1", tag="p1")
+            nc.tensor.matmul_mx(out=p1[n, hf][:], lhsT=w1_c[a, b][:, cols].bitcast(FP8X4), lhsT_scale=w1_s[a, b][:, cols], **callers(a, hf))
+
+        def w1_product(n, hf):
+            for a in range(2) if n > 0 else (1,):
+                w1_pass(n, hf, a)
             if hf == 0:
                 window[n] = ring.tile([P, S], F32, name="window", bufs=3)
                 if n in FUSED:
                     summed[n] = ring.tile([P, S], F32, name="summed", bufs=2)
             target = (summed[n] if n in FUSED else window[n])[:, BANK * hf : BANK * (hf + 1)]
-            nc.vector.scalar_tensor_tensor(target, p1[:], minus_bias[:, n : n + 1], y[n, hf][:], ALU.max, ALU.add)
+            nc.vector.scalar_tensor_tensor(target, p1[n, hf][:], minus_bias[:, n : n + 1], y[n, hf][:], ALU.max, ALU.add)
 
         def w8_product(n):
             b, t = divmod(n, 4)
@@ -289,7 +301,11 @@ def tile_list_excess_delay_causes_kernel(tc, tab_words, tab_scales, offs, pos1, 
         def late_pieces(n):
             return [(i % 2, 2 * (i // 2), (3 + i) % 2) for i in range(4) if (3 + i) // 2 == n]
 
-        w4_product(0)
+        for hf in range(2):
+            w4_pass(0, hf, 0)
+            w1_pass(0, hf, 0)
+        for hf in range(2):
+            w4_pass(0, hf, 1)
         round_w1(1, 0, 0, 1, placed("w1_rounded100", [P, 512], BF16, AT_FIRST_ROUNDED), copy=nc.vector.tensor_copy)
         quantize_w1(1, 0, 0, 1)
         deal_w4(0, 1, 4, placed("w4_rest", [P, 2, 6 * P], U8, AT_FIRST_ROUNDED))

@@ -19,13 +19,14 @@ IDENTITY = mybir.ActivationFunctionType.Identity
 RELU = mybir.ActivationFunctionType.Relu
 
 P = 128
+FLOAT32_MAX = 3.4028234663852886e38
 BANK = 512
 PIECE = M // 2
 TILES = 8
 RAW_ROWS = 112
 V_AT, W4_AT, CALLER_WIDTH = 0, S, S + H
 V2_AT, W8_AT, CALLEE_WIDTH = 0, M, M + H
-FUSED = range(3, 7)
+FUSED = range(2, 7)
 AHEAD = 3
 
 AT_V2_SCALES = 3.0625
@@ -254,7 +255,7 @@ def tile_list_excess_delay_causes_kernel(tc, tab_words, tab_scales, offs, pos1, 
             if hf == 0:
                 window[n] = ring.tile([P, S], F32, name="window", bufs=3)
                 if n in FUSED:
-                    summed[n] = ring.tile([P, S], F32, name="summed", bufs=2)
+                    summed[n] = ring.tile([P, S], F32, name="summed", bufs=3)
             target = (summed[n] if n in FUSED else window[n])[:, BANK * hf : BANK * (hf + 1)]
             nc.vector.scalar_tensor_tensor(target, p1[n, hf][:], minus_bias[:, n : n + 1], y[n, hf][:], ALU.max, ALU.add)
 
@@ -313,19 +314,22 @@ def tile_list_excess_delay_causes_kernel(tc, tab_words, tab_scales, offs, pos1, 
         for n in range(TILES):
             ahead = range(1, AHEAD + 1) if n == 0 else range(n + AHEAD, min(n + AHEAD + 1, TILES))
             w1_product(n, 0)
+            if n in FUSED:
+                nc.gpsimd.tensor_scalar(window[n][:, 0:BANK], summed[n][:, 0:BANK], FLOAT32_MAX, 0.0, ALU.min, ALU.max)
             for later in ahead[:1]:
                 w4_product(later)
             if n > 1:
                 w8_product(n - 1)
-            if n > 0 and n - 1 not in FUSED:
-                pick(n - 1, 0, M, ring.tile([P, M], F32, name="picked", bufs=4))
-            if n == 2:
-                subtract(0, 0, M)
+            if n == 1:
+                pick(0, 0, M, ring.tile([P, M], F32, name="picked", bufs=4))
             w1_product(n, 1)
+            if n == 2:
+                pick(1, 0, M, ring.tile([P, M], F32, name="picked", bufs=4))
+                subtract(0, 0, M)
             for later in ahead[1:]:
                 w4_product(later)
             if n in FUSED:
-                nc.scalar.activation(window[n][:], summed[n][:], RELU)
+                nc.scalar.activation(window[n][:, BANK:S], summed[n][:, BANK:S], RELU)
             if n == 0:
                 round_w1(1, 0, 1, 2, placed("w1_rounded101", [P, 512], BF16, AT_SECOND_ROUNDED))
                 quantize_w1(1, 0, 1, 2)
@@ -343,7 +347,7 @@ def tile_list_excess_delay_causes_kernel(tc, tab_words, tab_scales, offs, pos1, 
                 w8_product(0)
             for a, t, hf in late_pieces(n):
                 round_w1(a, 1, t, t + 2, after_y(n, hf, "w1_rounded", [P, 1024], BF16))
-            if n in (FUSED[0], TILES - 1):
+            if n in (3, TILES - 1):
                 round_wo(n // (TILES - 1), after_y(n - 1, 1, "wo_rounded", [P, N, 4], BF16))
             if n > 1:
                 subtract(n - 1, 0, M)

@@ -24,25 +24,23 @@ BANK = 512
 PIECE = M // 2
 TILES = 8
 RAW_ROWS = 112
+CALLER_ROWS = 96
 V_AT, W4_AT, CALLER_WIDTH = 0, S, S + H
 V2_AT, W8_AT, CALLEE_WIDTH = 0, M, M + H
 FUSED = range(2, 7)
-AHEAD = 3
 
-AT_V2_SCALES = 3.0625
-AT_TABLE = (3, 21.5)
-AT_W1_PASS1 = 55.9375
-AT_TABLE2 = 12.0625
-AT_W8 = 21
-AT_V_SCALES = 54
-AT_W1_PASS0 = 29
-AT_FIRST_ROUNDED = 37
-AT_W4_RAW = 1.0625
-AT_V2_WORDS = 44.5
-AT_FIRST_Y = 47
-AT_SECOND_ROUNDED = 48
-AT_W4_DEALT = 48.5
-AT_LAST_PICKS = 51
+AT_TABLE = (1, 24)
+AT_W4_RAW = 0
+AT_V2_SCALES = 2
+AT_W1_REST = 7
+AT_TABLE2 = 15
+AT_V_SCALES = 23.0625
+AT_W8 = 23.5
+AT_W1_LATE = 31.5
+AT_WO = (7, 13)
+AT_LAST_PICKS = 47.5
+AT_W1_SECOND = 3
+AT_Y = 51
 
 
 def tile_list_excess_delay_causes_kernel(tc, tab_words, tab_scales, offs, pos1, tab2_words, tab2_scales, offs2,
@@ -67,12 +65,13 @@ def tile_list_excess_delay_causes_kernel(tc, tab_words, tab_scales, offs, pos1, 
         pos_t = keep.tile([P, M // 16], U16, name="pos_t")
         offs2_t = keep.tile([P, M // 16], U16, name="offs2_t")
 
-        tab_s = held("tab_s", [P, 2, T], U8)
+        tab_s = held("tab_s", [P, T], U8)
         tab2_s = held("tab2_s", [P, 2, T2], U8)
-        w4s_raw = held("w4s_raw", [P, 2, H], U8)
+        w4s_raw = held("w4s_raw", [P, 1, H], U8)
+        caller_staged = held("caller_staged", [P, 1, CALLER_WIDTH], U8)
         w8s_raw = held("w8s_raw", [P, 2, H], U8)
         callee_s = held("callee_s", [P, 2, CALLEE_WIDTH], U8)
-        caller_s = held("caller_s", [P, 2, CALLER_WIDTH], U8)
+        caller_s = [held("caller_s%d" % a, [P, CALLER_WIDTH], U8) for a in range(2)]
         bias_rows = held("bias_rows", [P, 512], F32)
         bias_dealt = held("bias_dealt", [P, 4, P], F32)
         ident = held("ident", [P, P], F32)
@@ -82,7 +81,9 @@ def tile_list_excess_delay_causes_kernel(tc, tab_words, tab_scales, offs, pos1, 
         nc.gpsimd.memset(bias_rows[:], 0.0)
         make_identity(nc, ident[:])
         for raw in (tab_s, w4s_raw):
-            nc.vector.memset(raw[0:RAW_ROWS].bitcast(I32), 0)
+            nc.vector.memset(raw[0:CALLER_ROWS].bitcast(I32), 0)
+        for plane in caller_s:
+            nc.vector.memset(plane[:].bitcast(I32), 0)
         for raw in (tab2_s, w8s_raw):
             nc.gpsimd.memset(raw[0:RAW_ROWS].bitcast(I32), 0)
 
@@ -105,40 +106,53 @@ def tile_list_excess_delay_causes_kernel(tc, tab_words, tab_scales, offs, pos1, 
             w4_raw[b] = tile
             load(tile[:].bitcast(I32), w4_words[:, :, H * b : H * (b + 1)].rearrange("a p e -> p a e").bitcast(I32))
 
-        def load_w1(a, b, tile):
-            w1_raw[a, b] = tile
-            load(tile[:], w1[512 * a : 512 * (a + 1), 512 * b : 512 * (b + 1)].rearrange("(p j) c -> p j c", j=4))
+        def load_wo(b):
+            wo_raw[b] = placed("wo_raw%d" % b, [P, 4, N], F32, AT_WO[b])
+            if b == 0:
+                load(wo_raw[b][:], wo[0:512, :].rearrange("(p t) n -> p t n", t=4))
+            else:
+                for t in range(4):
+                    load(wo_raw[b][:, t, :], wo[512:H, :].rearrange("(q t e) n -> t q e n", t=4, e=8)[t])
 
-        def load_wo(b, kib):
-            wo_raw[b] = placed("wo_raw%d" % b, [P, 4, N], F32, kib)
-            for t in range(4):
-                load(wo_raw[b][:, t, :], wo[512 * b : 512 * (b + 1), :].rearrange("(q t e) n -> t q e n", t=4, e=8)[t])
+        def load_w1_columns(tile, lo, hi):
+            for a in range(2):
+                load(tile[:, a], w1[512 * a : 512 * (a + 1), lo:hi].rearrange("(p j) c -> p j c", j=4))
 
         load(offs_t[:], offs)
-        load_scale_rows(tab_s, tab_scales)
-        load_scale_rows(w4s_raw, w4_scales)
+        load(tab_s[CALLER_ROWS:P].bitcast(I32), tab_scales.rearrange("a q n -> (a q) n").bitcast(I32))
+        load(w4s_raw[CALLER_ROWS:P, 0].bitcast(I32), w4_scales.rearrange("a q n -> (a q) n").bitcast(I32))
         load(offs2_t[:], offs2)
-        load_tab_words(0)
         load_scale_rows(tab2_s, tab2_scales)
         load_scale_rows(w8s_raw, w8_scales)
-        load(bias_rows[0:2, :], b1.rearrange("(b c) -> b c", b=2))
+        load_tab_words(0)
         load_w4(0, held("w4_raw0", [P, 2, H], U8))
-        load_w1(0, 0, held("w1_raw00", [P, 4, 512], F32))
-        load_tab_words(1)
+        load(bias_rows[0:2, :], b1.rearrange("(b c) -> b c", b=2))
+        w1_first = held("w1_first", [P, 2, 4, P], F32)
+        load_w1_columns(w1_first, 0, P)
         load(pos_t[:], pos1)
 
         def deal_scales(dst, raw):
-            nc.vector.tensor_copy(dst.bitcast(I32).rearrange("p (b t q i) -> p b t q i", t=4, q=16, i=2),
-                                  raw.bitcast(I32).rearrange("p (b q t i) -> p b t q i", t=4, q=16, i=2))
+            nc.vector.tensor_copy(dst[:, :, 0:512].bitcast(I32), raw[:, :, 0:512].bitcast(I32))
+            nc.vector.tensor_copy(dst[:, :, 512:H].bitcast(I32).rearrange("p a (t q i) -> p a t q i", t=4, i=2),
+                                  raw[:, :, 512:H].bitcast(I32).rearrange("p a (q t i) -> p a t q i", t=4, i=2))
 
-        v_s = placed("v_s", [P, 2, S], U8, AT_V_SCALES)
-        for a in range(2):
-            nc.vector.tensor_copy(v_s[:, a, :], tab_s[:, a, :].indirect(offs_t[:]))
-            deal_scales(caller_s[:, a, W4_AT : W4_AT + H], w4s_raw[:, a, :])
-        nc.vector.tensor_copy(caller_s[:, :, V_AT : V_AT + S].bitcast(I32), v_s[:].bitcast(I32))
-        for s in range(4):
-            load(caller_s[s:P:32].bitcast(I32), caller_s[RAW_ROWS + s : P : 4].bitcast(I32))
-        load_w1(1, 0, placed("w1_raw10", [P, 4, 512], F32, AT_W1_PASS1))
+        v_s = placed("v_s", [P, S], U8, AT_V_SCALES)
+        nc.vector.tensor_copy(v_s[:], tab_s[:].indirect(offs_t[:]))
+        deal_scales(caller_staged[:, :, W4_AT : W4_AT + H], w4s_raw[:])
+        nc.vector.tensor_copy(caller_staged[:, 0, V_AT : V_AT + S].bitcast(I32), v_s[:].bitcast(I32))
+
+        def move_caller_rows(a):
+            first = CALLER_ROWS + 16 * a
+            for s in range(4):
+                load(caller_s[a][s:P:32].bitcast(I32), caller_staged[first + s : first + 16 : 4, 0].bitcast(I32))
+
+        move_caller_rows(0)
+        load_tab_words(1)
+        move_caller_rows(1)
+        w1_second = placed("w1_second", [P, 2, 4, P], F32, AT_W1_SECOND)
+        load_w1_columns(w1_second, P, 2 * P)
+        w1_rest = placed("w1_rest", [P, 2, 4, 2 * P], F32, AT_W1_REST)
+        load_w1_columns(w1_rest, 2 * P, 4 * P)
 
         w4_dealt = {}
         w8_dealt = {}
@@ -154,7 +168,8 @@ def tile_list_excess_delay_causes_kernel(tc, tab_words, tab_scales, offs, pos1, 
             nc.vector.tensor_copy(dealt[:].rearrange("p a (t q e) -> p a t q e", t=4, e=8),
                                   w8_raw[:, :, 512 * b : 512 * (b + 1)].rearrange("p a (q t e) -> p a t q e", t=4, e=8))
 
-        deal_w4(0, 0, 1, held("w4_first", [P, 2, 2 * P], U8))
+        for n in range(4):
+            w4_dealt[n] = w4_raw[0][:, :, 2 * P * n : 2 * P * (n + 1)]
 
         v_w = {(a, hf): held("v_w%d%d" % (a, hf), [P, BANK], U32) for a in range(2) for hf in range(2)}
 
@@ -163,38 +178,40 @@ def tile_list_excess_delay_causes_kernel(tc, tab_words, tab_scales, offs, pos1, 
                 nc.vector.tensor_copy(v_w[a, hf][:], tab_w[a][:].bitcast(U32).indirect(offs_t[:, 32 * hf : 32 * (hf + 1)]))
 
         gather_callers(0)
+        load_w4(1, placed("w4_raw1", [P, 2, H], U8, AT_W4_RAW))
         tab2_w = placed("tab2_w", [P, 2, T2], I32, AT_TABLE2)
         load(tab2_w[:], tab2_words.rearrange("a p t i -> p a (t i)").bitcast(I32))
-        load_w4(1, placed("w4_raw1", [P, 2, H], U8, AT_W4_RAW))
 
         v2_s = placed("v2_s", [P, 2, M], U8, AT_V2_SCALES)
         for a in range(2):
             nc.vector.tensor_copy(v2_s[:, a, :], tab2_s[:, a, :].indirect(offs2_t[:]))
-            deal_scales(callee_s[:, a, W8_AT : W8_AT + H], w8s_raw[:, a, :])
+        deal_scales(callee_s[:, :, W8_AT : W8_AT + H], w8s_raw[:])
         nc.vector.tensor_copy(callee_s[:, :, V2_AT : V2_AT + M].bitcast(I32), v2_s[:].bitcast(I32))
         for s in range(4):
             load(callee_s[4 + s : P : 32].bitcast(I32), callee_s[RAW_ROWS + s : P : 4].bitcast(I32))
 
-        bias_ps = psum.tile([P, BANK], F32, name="bias_ps", tag="callee", bufs=2)
         nc.scalar.copy(bias_dealt[:].rearrange("p t (q e) -> p t q e", e=8), bias_rows[:].rearrange("p (q t e) -> p t q e", t=4, e=8))
-        for t in range(4):
-            nc.tensor.transpose(bias_ps[:, P * t : P * (t + 1)], bias_dealt[:, t, :], ident[:])
-        by_tile = bias_ps[:].rearrange("p (t b) -> p b t", t=4)[:, 0:2, :]
-        nc.scalar.copy(bias[:].rearrange("p (b t) -> p b t", b=2), by_tile)
-        nc.scalar.activation(minus_bias[:].rearrange("p (b t) -> p b t", b=2), by_tile, IDENTITY, scale=-1.0)
+        for b, rows in enumerate((bias_rows[:].rearrange("p (t c) -> p t c", t=4), bias_dealt[:])):
+            bias_ps = psum.tile([P, BANK], F32, name="bias_ps", tag="callee", bufs=2)
+            for t in range(4):
+                nc.tensor.transpose(bias_ps[:, P * t : P * (t + 1)], rows[:, t, :], ident[:])
+            nc.scalar.copy(bias[:, 4 * b : 4 * (b + 1)], bias_ps[:, b:BANK:P])
+        nc.scalar.activation(minus_bias[:], bias[:], IDENTITY, scale=-1.0)
 
-        w1_c = {(a, b): held("w1_c%d%d" % (a, b), [P, 512], U32) for a in range(2) for b in range(2)}
-        w1_s = {(a, b): held("w1_s%d%d" % (a, b), [P, 512], U8) for a in range(2) for b in range(2)}
         w1_rounded = {}
+        first_c = [held("first_c%d" % n, [P, 2, P], U32) for n in range(TILES)]
+        first_s = [held("first_s%d" % n, [P, 2, P], U8) for n in range(TILES)]
+        first_rounded = {}
 
-        def round_w1(a, b, lo, hi, rounded, copy=nc.scalar.copy):
-            w1_rounded[a, b, lo] = rounded
-            copy(rounded[:].rearrange("p (t q e j) -> p t q j e", q=16, e=8, j=4),
-                 w1_raw[a, b][:].rearrange("p j (q t e) -> p t q j e", t=4, e=8)[:, lo:hi])
+        def round_first(n, lo, hi):
+            raw = (w1_first, w1_second)[n][:] if n < 2 else w1_rest[:, :, :, P * (n - 2) : P * (n - 1)]
+            shape = [P, hi - lo, P, 4]
+            first_rounded[n, lo] = held("first_rounded%d" % n, shape, BF16) if n < 2 else after_y(n - 2, 1, "first_rounded", shape, BF16)
+            nc.scalar.copy(first_rounded[n, lo][:].rearrange("p a (c i) j -> p a c j i", i=4), raw[:, lo:hi].rearrange("p a j (c i) -> p a c j i", i=4))
 
-        def quantize_w1(a, b, lo, hi):
-            cols = slice(P * lo, P * hi)
-            nc.vector.quantize_mx(out=w1_c[a, b][:, cols].bitcast(FP8X4), scales=w1_s[a, b][:, cols], in_=w1_rounded[a, b, lo][:])
+        def quantize_first(n, lo, hi):
+            nc.vector.quantize_mx(out=first_c[n][:, lo:hi].rearrange("p a c -> p (a c)").bitcast(FP8X4), scales=first_s[n][:, lo:hi].rearrange("p a c -> p (a c)"),
+                                  in_=first_rounded[n, lo][:].rearrange("p a c j -> p (a c j)"))
 
         wo_rounded = {}
         wo_s = held("wo_s", [P, 2 * N], U8)
@@ -208,12 +225,14 @@ def tile_list_excess_delay_causes_kernel(tc, tab_words, tab_scales, offs, pos1, 
             for lo, hi in ((0, 256), (256, N)):
                 nc.vector.quantize_mx(out=wo_c[:, N * b + lo : N * b + hi].bitcast(FP8X4), scales=wo_s[:, N * b + lo : N * b + hi], in_=flat[:, 4 * lo : 4 * hi])
 
-        round_w1(0, 0, 0, 4, held("w1_rounded00", [P, 2048], BF16))
-        quantize_w1(0, 0, 0, 4)
+        round_first(0, 0, 2)
+        quantize_first(0, 0, 2)
         gather_callers(1)
         w8_raw = placed("w8_raw", [P, 2, H], I32, AT_W8)
         load(w8_raw[:], w8_words.rearrange("a p e i -> p a (e i)").bitcast(I32))
-        load_w1(0, 1, placed("w1_raw01", [P, 4, 512], F32, AT_W1_PASS0))
+        w8_dealt[0] = w8_raw
+        w1_late = placed("w1_late", [P, 2, 4, 512], F32, AT_W1_LATE)
+        load_w1_columns(w1_late, 512, H)
 
         y = {}
         summed = {}
@@ -221,10 +240,12 @@ def tile_list_excess_delay_causes_kernel(tc, tab_words, tab_scales, offs, pos1, 
         picked = {}
         own = {}
         own_copy = {}
-        minus_excess = [held("minus_excess%d" % b, [P, 4, M], F32) for b in range(2)]
+        minus_excess = [placed("minus_excess0", [P, 4, M], F32, AT_Y + 8), held("minus_excess1", [P, 4, M], F32)]
+
+        natural = {}
 
         def callers(a, hf):
-            return dict(rhs=v_w[a, hf][:].bitcast(FP8X4), rhs_scale=caller_s[:, a, V_AT + BANK * hf : V_AT + BANK * (hf + 1)], start=(a == 0), stop=(a == 1))
+            return dict(rhs=v_w[a, hf][:].bitcast(FP8X4), rhs_scale=caller_s[a][:, V_AT + BANK * hf : V_AT + BANK * (hf + 1)], start=(a == 0), stop=(a == 1))
 
         p4 = {}
         p1 = {}
@@ -232,9 +253,10 @@ def tile_list_excess_delay_causes_kernel(tc, tab_words, tab_scales, offs, pos1, 
         def w4_pass(n, hf, a):
             if a == 0:
                 p4[n, hf] = psum.tile([P, BANK], F32, name="p4", tag="p4")
-            nc.tensor.matmul_mx(out=p4[n, hf][:], lhsT=w4_dealt[n][:, a, :].bitcast(FP4X4), lhsT_scale=caller_s[:, a, W4_AT + P * n : W4_AT + P * (n + 1)], **callers(a, hf))
+            nc.tensor.matmul_mx(out=p4[n, hf][:], lhsT=w4_dealt[n][:, a, :].bitcast(FP4X4), lhsT_scale=caller_s[a][:, W4_AT + P * n : W4_AT + P * (n + 1)], **callers(a, hf))
             if a == 1:
-                y[n, hf] = placed("y_first", [P, BANK], F32, AT_FIRST_Y) if (n, hf) == (0, 0) else after_y(n, hf, "y", [P, BANK], F32)
+                tag = "late_rounded%d" % (2 * n + hf - 5) if (n, hf) in ((5, 0), (5, 1), (6, 0)) else "y%d%d" % (n, hf)
+                y[n, hf] = placed("y50", [P, BANK], F32, AT_Y + 3) if (n, hf) == (5, 0) else keep.tile([P, BANK], F32, name="y", tag=tag, align_bytes=64)
                 nc.scalar.activation(y[n, hf][:], p4[n, hf][:], IDENTITY, bias=bias[:, n : n + 1])
 
         def w4_product(n):
@@ -247,7 +269,8 @@ def tile_list_excess_delay_causes_kernel(tc, tab_words, tab_scales, offs, pos1, 
             cols = slice(P * t, P * (t + 1))
             if a == 0:
                 p1[n, hf] = psum.tile([P, BANK], F32, name="p1", tag="p1")
-            nc.tensor.matmul_mx(out=p1[n, hf][:], lhsT=w1_c[a, b][:, cols].bitcast(FP8X4), lhsT_scale=w1_s[a, b][:, cols], **callers(a, hf))
+            codes, scales = first_c[n][:, a], first_s[n][:, a]
+            nc.tensor.matmul_mx(out=p1[n, hf][:], lhsT=codes.bitcast(FP8X4), lhsT_scale=scales, **callers(a, hf))
 
         def w1_product(n, hf):
             for a in range(2) if n > 0 else (1,):
@@ -258,6 +281,8 @@ def tile_list_excess_delay_causes_kernel(tc, tab_words, tab_scales, offs, pos1, 
                     summed[n] = ring.tile([P, S], F32, name="summed", bufs=3)
             target = (summed[n] if n in FUSED else window[n])[:, BANK * hf : BANK * (hf + 1)]
             nc.vector.scalar_tensor_tensor(target, p1[n, hf][:], minus_bias[:, n : n + 1], y[n, hf][:], ALU.max, ALU.add)
+            if n in FUSED:
+                nc.gpsimd.tensor_scalar(window[n][:, BANK * hf : BANK * (hf + 1)], target, FLOAT32_MAX, 0.0, ALU.min, ALU.max)
 
         def w8_product(n):
             b, t = divmod(n, 4)
@@ -267,7 +292,7 @@ def tile_list_excess_delay_causes_kernel(tc, tab_words, tab_scales, offs, pos1, 
                                     lhsT_scale=callee_s[4:P, a, W8_AT + P * n : W8_AT + P * (n + 1)],
                                     rhs=v2_w[:, a, :].bitcast(FP8X4), rhs_scale=callee_s[4:P, a, V2_AT : V2_AT + M], start=(a == 0), stop=(a == 1))
             if n in FUSED:
-                own_copy[n] = ring.tile([P, M], F32, name="own_copy", bufs=2)
+                own_copy[n] = placed("own_copy%d" % n, [P, M], F32, AT_Y + (1, -1)[n % 2])
                 nc.scalar.copy(own_copy[n][:], own[n][:])
 
         def pick(n, lo, hi, tile):
@@ -276,17 +301,26 @@ def tile_list_excess_delay_causes_kernel(tc, tab_words, tab_scales, offs, pos1, 
 
         def subtract(n, lo, hi):
             b, t = divmod(n, 4)
+            if b == 0:
+                natural[n] = held("natural%d" % n, [P, M], F32)
+            target = natural[n][:, lo:hi] if b == 0 else minus_excess[b][:, t, lo:hi]
             if n in FUSED:
-                nc.vector.tensor_tensor(minus_excess[b][:, t, lo:hi], window[n][:].indirect(pos_t[:, lo // 16 : hi // 16]), own_copy[n][:, lo:hi], ALU.subtract)
+                nc.vector.tensor_tensor(target, window[n][:].indirect(pos_t[:, lo // 16 : hi // 16]), own_copy[n][:, lo:hi], ALU.subtract)
             else:
-                nc.vector.scalar_tensor_tensor(minus_excess[b][:, t, lo:hi], picked[n, lo][:], 0.0, own[n][:, lo:hi], ALU.max, ALU.subtract)
+                nc.vector.scalar_tensor_tensor(target, picked[n, lo][:], 0.0, own[n][:, lo:hi], ALU.max, ALU.subtract)
+            if b == 0:
+                for place in range(4):
+                    load(minus_excess[0][32 * n : 32 * (n + 1), place, :], natural[n][place:P:4, :])
 
         h_rounded = {}
         h_c = {}
         h_s = {}
 
         def h_views(b, lo):
-            h_rounded[b, lo] = held("h_rounded%d_%d" % (b, lo), [P, PIECE, 4], BF16)
+            if b == 0:
+                h_rounded[b, lo] = keep.tile([P, PIECE, 4], BF16, name="h_rounded", tag=("late_rounded7", "y61")[lo // PIECE], align_bytes=64)
+            else:
+                h_rounded[b, lo] = placed("h_rounded%d" % lo, [P, PIECE, 4], BF16, AT_Y + 8 + 2 * (lo // PIECE))
             return (h_rounded[b, lo][:].rearrange("p (c i) t -> p c t i", i=4),
                     minus_excess[b][:, :, lo : lo + PIECE].rearrange("p t (c i) -> p c t i", i=4))
 
@@ -299,67 +333,65 @@ def tile_list_excess_delay_causes_kernel(tc, tab_words, tab_scales, offs, pos1, 
             h_s[b, lo] = held("h_s%d_%d" % (b, lo), [P, PIECE], U8)
             nc.vector.quantize_mx(out=h_c[b, lo][:].bitcast(FP8X4), scales=h_s[b, lo][:], in_=h_rounded[b, lo][:].rearrange("p m t -> p (m t)"))
 
-        def late_pieces(n):
-            return [(i % 2, 2 * (i // 2), (3 + i) % 2) for i in range(4) if (3 + i) // 2 == n]
+        def late_piece(n):
+            rounded = placed("late_rounded%d" % n, [P, 2, P, 4], BF16, AT_Y + 4 * (n - 4)) if n < 6 else held("late_rounded%d" % n, [P, 2, P, 4], BF16)
+            first_rounded[n, 0] = rounded
+            nc.scalar.copy(rounded[:].rearrange("p a (q e) j -> p a q j e", e=8), w1_late[:].rearrange("p a j (q t e) -> p t a q j e", t=4, e=8)[:, n - 4])
+            quantize_first(n, 0, 2)
+
+        def picks(n):
+            pick(n, 0, M, ring.tile([P, M], F32, name="picked", bufs=2, align_bytes=64))
 
         for hf in range(2):
             w4_pass(0, hf, 0)
             w1_pass(0, hf, 0)
+        round_first(1, 0, 2)
+        quantize_first(1, 0, 2)
         for hf in range(2):
             w4_pass(0, hf, 1)
-        round_w1(1, 0, 0, 1, placed("w1_rounded100", [P, 512], BF16, AT_FIRST_ROUNDED), copy=nc.vector.tensor_copy)
-        quantize_w1(1, 0, 0, 1)
-        deal_w4(0, 1, 4, placed("w4_rest", [P, 2, 6 * P], U8, AT_FIRST_ROUNDED))
-
-        for n in range(TILES):
-            ahead = range(1, AHEAD + 1) if n == 0 else range(n + AHEAD, min(n + AHEAD + 1, TILES))
-            w1_product(n, 0)
-            if n in FUSED:
-                nc.gpsimd.tensor_scalar(window[n][:, 0:BANK], summed[n][:, 0:BANK], FLOAT32_MAX, 0.0, ALU.min, ALU.max)
-            for later in ahead[:1]:
-                w4_product(later)
-            if n > 1:
-                w8_product(n - 1)
-            if n == 1:
-                pick(0, 0, M, ring.tile([P, M], F32, name="picked", bufs=4))
-            w1_product(n, 1)
-            if n == 2:
-                pick(1, 0, M, ring.tile([P, M], F32, name="picked", bufs=4))
-                subtract(0, 0, M)
-            for later in ahead[1:]:
-                w4_product(later)
-            if n in FUSED:
-                nc.scalar.activation(window[n][:, BANK:S], summed[n][:, BANK:S], RELU)
-            if n == 0:
-                round_w1(1, 0, 1, 2, placed("w1_rounded101", [P, 512], BF16, AT_SECOND_ROUNDED))
-                quantize_w1(1, 0, 1, 2)
-                deal_w4(1, 0, 4, placed("w4_second", [P, 2, H], U8, AT_W4_DEALT))
-                v2_w = placed("v2_w", [P, 2, M], U32, AT_V2_WORDS)
-                for a in range(2):
-                    nc.vector.tensor_copy(v2_w[:, a, :], tab2_w[:, a, :].bitcast(U32).indirect(offs2_t[:]))
-                load_w1(1, 1, placed("w1_raw11", [P, 4, 512], F32, AT_TABLE2))
-            if n == 1:
-                for t in (2, 3):
-                    round_w1(1, 0, t, t + 1, after_y(*divmod(t - 1, 2), "w1_rounded", [P, 512], BF16))
-                    quantize_w1(1, 0, t, t + 1)
-                load_wo(0, AT_W1_PASS1)
-                deal_w8(0, after_y(1, 0, "w8_dealt", [P, 2, 512], I32))
-                w8_product(0)
-            for a, t, hf in late_pieces(n):
-                round_w1(a, 1, t, t + 2, after_y(n, hf, "w1_rounded", [P, 1024], BF16))
-            if n in (3, TILES - 1):
-                round_wo(n // (TILES - 1), after_y(n - 1, 1, "wo_rounded", [P, N, 4], BF16))
-            if n > 1:
-                subtract(n - 1, 0, M)
+            w1_product(0, hf)
+        w4_product(1)
+        for hf in range(2):
+            w1_product(1, hf)
+        round_first(2, 0, 2)
+        picks(0)
+        quantize_first(2, 0, 2)
+        picks(1)
+        deal_w4(1, 0, 4, after_y(1, 0, "w4_second", [P, 2, H], U8))
+        v2_w = after_y(0, 1, "v2_w", [P, 2, M], U32)
+        for a in range(2):
+            nc.vector.tensor_copy(v2_w[:, a, :], tab2_w[:, a, :].bitcast(U32).indirect(offs2_t[:]))
+        w4_product(2)
+        round_first(3, 0, 2)
+        load_wo(0)
+        load_wo(1)
+        for hf in range(2):
+            w1_product(2, hf)
+        quantize_first(3, 0, 2)
+        w4_product(3)
+        for n in range(2):
+            w8_product(n)
+            subtract(n, 0, M)
+        w4_product(4)
+        for n in range(4, TILES):
+            late_piece(n)
+        for n in range(3, TILES):
+            for hf in range(2):
+                w1_product(n, hf)
+            w8_product(n - 1)
+            subtract(n - 1, 0, M)
             if n == 3:
-                deal_w8(1, after_y(3, 1, "w8_dealt", [P, 2, 512], I32))
-                load_wo(1, AT_W8)
-            for a, t, hf in late_pieces(n):
-                quantize_w1(a, 1, t, t + 2)
-            if n in (5, 6):
-                round_h(0, PIECE * (n - 5))
-            if n in (6, 7):
-                quantize_h(0, PIECE * (n - 6))
+                deal_w8(1, ring.tile([P, 2, 512], I32, name="w8_dealt", tag="picked", bufs=2, align_bytes=64))
+            if n in (4, 5, 6):
+                w4_product(n + 1)
+            if n == 4:
+                round_wo(0, placed("wo_rounded", [P, N, 4], BF16, AT_Y + 5))
+            if n == 7:
+                round_wo(1, keep.tile([P, N, 4], BF16, name="wo_rounded", tag="late_rounded6", align_bytes=64))
+                for lo in (0, PIECE):
+                    round_h(0, lo)
+                for lo in (0, PIECE):
+                    quantize_h(0, lo)
 
         last = TILES - 1
         w8_product(last)
@@ -367,7 +399,7 @@ def tile_list_excess_delay_causes_kernel(tc, tab_words, tab_scales, offs, pos1, 
         subtract(last, 0, PIECE)
         wo_c = placed("wo_c", [P, 2 * N], U32, AT_LAST_PICKS)
         quantize_wo(0)
-        pick(last, PIECE, M, ring.tile([P, PIECE], F32, name="picked", bufs=4))
+        pick(last, PIECE, M, ring.tile([P, PIECE], F32, name="picked", bufs=2, align_bytes=64))
         subtract(last, PIECE, M)
         quantize_wo(1)
         round_h(1, 0)

@@ -206,7 +206,7 @@ def tile_list_excess_delay_causes_kernel(tc, tab_words, tab_scales, offs, pos1, 
         def round_first(n, lo, hi):
             raw = (w1_first, w1_second)[n][:] if n < 2 else w1_rest[:, :, :, P * (n - 2) : P * (n - 1)]
             shape = [P, hi - lo, P, 4]
-            first_rounded[n, lo] = held("first_rounded%d" % n, shape, BF16) if n < 2 else after_y(n - 2, 1, "first_rounded", shape, BF16)
+            first_rounded[n, lo] = held("first_rounded%d" % n, shape, BF16) if n < 2 else after_y(1, n - 2, "first_rounded", shape, BF16)
             nc.scalar.copy(first_rounded[n, lo][:].rearrange("p a (c i) j -> p a c j i", i=4), raw[:, lo:hi].rearrange("p a j (c i) -> p a c j i", i=4))
 
         def quantize_first(n, lo, hi):
@@ -290,7 +290,7 @@ def tile_list_excess_delay_causes_kernel(tc, tab_words, tab_scales, offs, pos1, 
             for a in range(2):
                 nc.tensor.matmul_mx(out=own[n][:], lhsT=w8_dealt[b][:, a, P * t : P * (t + 1)].bitcast(FP8X4),
                                     lhsT_scale=callee_s[4:P, a, W8_AT + P * n : W8_AT + P * (n + 1)],
-                                    rhs=v2_w[:, a, :].bitcast(FP8X4), rhs_scale=callee_s[4:P, a, V2_AT : V2_AT + M], start=(a == 0), stop=(a == 1))
+                                    rhs=v2_w[a][:].bitcast(FP8X4), rhs_scale=callee_s[4:P, a, V2_AT : V2_AT + M], start=(a == 0), stop=(a == 1))
             if n in FUSED:
                 own_copy[n] = placed("own_copy%d" % n, [P, M], F32, AT_Y + (1, -1)[n % 2])
                 nc.scalar.copy(own_copy[n][:], own[n][:])
@@ -339,6 +339,12 @@ def tile_list_excess_delay_causes_kernel(tc, tab_words, tab_scales, offs, pos1, 
             nc.scalar.copy(rounded[:].rearrange("p a (q e) j -> p a q j e", e=8), w1_late[:].rearrange("p a j (q t e) -> p t a q j e", t=4, e=8)[:, n - 4])
             quantize_first(n, 0, 2)
 
+        v2_w = {}
+
+        def gather_callees(a):
+            v2_w[a] = after_y(1, a, "v2_w", [P, M], U32)
+            nc.vector.tensor_copy(v2_w[a][:], tab2_w[:, a, :].bitcast(U32).indirect(offs2_t[:]))
+
         def picks(n):
             pick(n, 0, M, ring.tile([P, M], F32, name="picked", bufs=2, align_bytes=64))
 
@@ -355,12 +361,10 @@ def tile_list_excess_delay_causes_kernel(tc, tab_words, tab_scales, offs, pos1, 
             w1_product(1, hf)
         round_first(2, 0, 2)
         picks(0)
-        quantize_first(2, 0, 2)
+        deal_w4(1, 0, 4, after_y(0, 1, "w4_second", [P, 2, H], U8))
         picks(1)
-        deal_w4(1, 0, 4, after_y(1, 0, "w4_second", [P, 2, H], U8))
-        v2_w = after_y(0, 1, "v2_w", [P, 2, M], U32)
-        for a in range(2):
-            nc.vector.tensor_copy(v2_w[:, a, :], tab2_w[:, a, :].bitcast(U32).indirect(offs2_t[:]))
+        quantize_first(2, 0, 2)
+        gather_callees(0)
         w4_product(2)
         round_first(3, 0, 2)
         load_wo(0)
@@ -368,6 +372,7 @@ def tile_list_excess_delay_causes_kernel(tc, tab_words, tab_scales, offs, pos1, 
         for hf in range(2):
             w1_product(2, hf)
         quantize_first(3, 0, 2)
+        gather_callees(1)
         w4_product(3)
         for n in range(2):
             w8_product(n)
@@ -375,6 +380,7 @@ def tile_list_excess_delay_causes_kernel(tc, tab_words, tab_scales, offs, pos1, 
         w4_product(4)
         for n in range(4, TILES):
             late_piece(n)
+        round_wo(0, placed("wo_rounded0", [P, N, 4], BF16, AT_W1_LATE))
         for n in range(3, TILES):
             for hf in range(2):
                 w1_product(n, hf)
@@ -384,10 +390,9 @@ def tile_list_excess_delay_causes_kernel(tc, tab_words, tab_scales, offs, pos1, 
                 deal_w8(1, ring.tile([P, 2, 512], I32, name="w8_dealt", tag="picked", bufs=2, align_bytes=64))
             if n in (4, 5, 6):
                 w4_product(n + 1)
-            if n == 4:
-                round_wo(0, placed("wo_rounded", [P, N, 4], BF16, AT_Y + 5))
+            if n == 5:
+                round_wo(1, placed("wo_rounded1", [P, N, 4], BF16, AT_W1_LATE + 3))
             if n == 7:
-                round_wo(1, keep.tile([P, N, 4], BF16, name="wo_rounded", tag="late_rounded6", align_bytes=64))
                 for lo in (0, PIECE):
                     round_h(0, lo)
                 for lo in (0, PIECE):

@@ -38,9 +38,8 @@ AT_V_SCALES = 23.0625
 AT_W8 = 23.5
 AT_W1_LATE = 31.5
 AT_WO = (7, 13)
-AT_LAST_PICKS = 47.5
-AT_W1_SECOND = 3
-AT_Y = 51
+AT_LAST_PICKS = 23.5
+AT_Y = 51.5
 
 
 def tile_list_excess_delay_causes_kernel(tc, tab_words, tab_scales, offs, pos1, tab2_words, tab2_scales, offs2,
@@ -127,8 +126,8 @@ def tile_list_excess_delay_causes_kernel(tc, tab_words, tab_scales, offs, pos1, 
         load_tab_words(0)
         load_w4(0, held("w4_raw0", [P, 2, H], U8))
         load(bias_rows[0:2, :], b1.rearrange("(b c) -> b c", b=2))
-        w1_first = held("w1_first", [P, 2, 4, P], F32)
-        load_w1_columns(w1_first, 0, P)
+        w1_first = held("w1_first", [P, 2, 4, 2 * P], F32)
+        load_w1_columns(w1_first, 0, 2 * P)
         load(pos_t[:], pos1)
 
         def deal_scales(dst, raw):
@@ -149,8 +148,6 @@ def tile_list_excess_delay_causes_kernel(tc, tab_words, tab_scales, offs, pos1, 
         move_caller_rows(0)
         load_tab_words(1)
         move_caller_rows(1)
-        w1_second = placed("w1_second", [P, 2, 4, P], F32, AT_W1_SECOND)
-        load_w1_columns(w1_second, P, 2 * P)
         w1_rest = placed("w1_rest", [P, 2, 4, 2 * P], F32, AT_W1_REST)
         load_w1_columns(w1_rest, 2 * P, 4 * P)
 
@@ -204,7 +201,7 @@ def tile_list_excess_delay_causes_kernel(tc, tab_words, tab_scales, offs, pos1, 
         first_rounded = {}
 
         def round_first(n, lo, hi):
-            raw = (w1_first, w1_second)[n][:] if n < 2 else w1_rest[:, :, :, P * (n - 2) : P * (n - 1)]
+            raw = (w1_first, w1_rest)[n // 2][:, :, :, P * (n % 2) : P * (n % 2 + 1)]
             shape = [P, hi - lo, P, 4]
             first_rounded[n, lo] = held("first_rounded%d" % n, shape, BF16) if n < 2 else after_y(1, n - 2, "first_rounded", shape, BF16)
             nc.scalar.copy(first_rounded[n, lo][:].rearrange("p a (c i) j -> p a c j i", i=4), raw[:, lo:hi].rearrange("p a j (c i) -> p a c j i", i=4))
@@ -229,10 +226,10 @@ def tile_list_excess_delay_causes_kernel(tc, tab_words, tab_scales, offs, pos1, 
         quantize_first(0, 0, 2)
         gather_callers(1)
         w8_raw = placed("w8_raw", [P, 2, H], I32, AT_W8)
-        load(w8_raw[:], w8_words.rearrange("a p e i -> p a (e i)").bitcast(I32))
         w8_dealt[0] = w8_raw
         w1_late = placed("w1_late", [P, 2, 4, 512], F32, AT_W1_LATE)
         load_w1_columns(w1_late, 512, H)
+        load(w8_raw[:], w8_words.rearrange("a p e i -> p a (e i)").bitcast(I32))
 
         y = {}
         summed = {}
@@ -292,7 +289,7 @@ def tile_list_excess_delay_causes_kernel(tc, tab_words, tab_scales, offs, pos1, 
                                     lhsT_scale=callee_s[4:P, a, W8_AT + P * n : W8_AT + P * (n + 1)],
                                     rhs=v2_w[a][:].bitcast(FP8X4), rhs_scale=callee_s[4:P, a, V2_AT : V2_AT + M], start=(a == 0), stop=(a == 1))
             if n in FUSED:
-                own_copy[n] = placed("own_copy%d" % n, [P, M], F32, AT_Y + (1, -1)[n % 2])
+                own_copy[n] = placed("own_copy%d" % n, [P, M], F32, AT_Y + (1, 5)[n % 2])
                 nc.scalar.copy(own_copy[n][:], own[n][:])
 
         def pick(n, lo, hi, tile):
@@ -387,7 +384,7 @@ def tile_list_excess_delay_causes_kernel(tc, tab_words, tab_scales, offs, pos1, 
             w8_product(n - 1)
             subtract(n - 1, 0, M)
             if n == 3:
-                deal_w8(1, ring.tile([P, 2, 512], I32, name="w8_dealt", tag="picked", bufs=2, align_bytes=64))
+                deal_w8(1, placed("w8_dealt", [P, 2, 512], I32, AT_Y - 3.9375))
             if n in (4, 5, 6):
                 w4_product(n + 1)
             if n == 5:

@@ -23,23 +23,29 @@ FLOAT32_MAX = 3.4028234663852886e38
 BANK = 512
 PIECE = M // 2
 TILES = 8
-RAW_ROWS = 112
+NATURAL = 4
+HALF = H // 2
 CALLER_ROWS = 96
+CALLEE_ROWS = 112
 V_AT, W4_AT, CALLER_WIDTH = 0, S, S + H
 V2_AT, W8_AT, CALLEE_WIDTH = 0, M, M + H
 FUSED = range(2, 7)
 
 AT_TABLE = (1, 24)
-AT_W4_RAW = 0
+AT_W4_DEALT_RAW = 0
 AT_V2_SCALES = 2
-AT_W1_REST = 7
+AT_W1_NEXT = 7
 AT_TABLE2 = 15
+AT_WO = (7, 13)
 AT_V_SCALES = 23.0625
 AT_W8 = 23.5
 AT_W1_LATE = 31.5
-AT_WO = (7, 13)
-AT_LAST_PICKS = 23.5
-AT_Y = 51.5
+AT_WO_ROUNDED = (31.5, 34.5)
+AT_LATE_ROUNDED = {4: 51.5, 5: 55.5}
+AT_W8_DEALT = 47.5625
+AT_OWN_COPY = (52.5, 56.5)
+AT_Y_TILE5 = 54.5
+AT_EXCESS = 59.5
 
 
 def tile_list_excess_delay_causes_kernel(tc, tab_words, tab_scales, offs, pos1, tab2_words, tab2_scales, offs2,
@@ -57,8 +63,14 @@ def tile_list_excess_delay_causes_kernel(tc, tab_words, tab_scales, offs, pos1, 
         def placed(name, shape, dtype, kib):
             return shared.tile(shape, dtype, name=name, offset=int(1024 * kib), align_bytes=64)
 
+        def after(tag, name, shape, dtype):
+            return keep.tile(shape, dtype, name=name, tag=tag, align_bytes=64)
+
+        def y_tag(n, hf):
+            return {(5, 1): "late_rounded6", (6, 0): "late_rounded7"}.get((n, hf), "y%d%d" % (n, hf))
+
         def after_y(n, hf, name, shape, dtype):
-            return keep.tile(shape, dtype, name=name, tag="y%d%d" % (n, hf), align_bytes=64)
+            return after(y_tag(n, hf), name, shape, dtype)
 
         offs_t = keep.tile([P, S // 16], U16, name="offs_t")
         pos_t = keep.tile([P, M // 16], U16, name="pos_t")
@@ -71,7 +83,7 @@ def tile_list_excess_delay_causes_kernel(tc, tab_words, tab_scales, offs, pos1, 
         w8s_raw = held("w8s_raw", [P, 2, H], U8)
         callee_s = held("callee_s", [P, 2, CALLEE_WIDTH], U8)
         caller_s = [held("caller_s%d" % a, [P, CALLER_WIDTH], U8) for a in range(2)]
-        bias_rows = held("bias_rows", [P, 512], F32)
+        bias_rows = held("bias_rows", [P, HALF], F32)
         bias_dealt = held("bias_dealt", [P, 4, P], F32)
         ident = held("ident", [P, P], F32)
         bias = held("bias", [P, TILES], F32)
@@ -84,17 +96,18 @@ def tile_list_excess_delay_causes_kernel(tc, tab_words, tab_scales, offs, pos1, 
         for plane in caller_s:
             nc.vector.memset(plane[:].bitcast(I32), 0)
         for raw in (tab2_s, w8s_raw):
-            nc.gpsimd.memset(raw[0:RAW_ROWS].bitcast(I32), 0)
+            nc.gpsimd.memset(raw[0:CALLEE_ROWS].bitcast(I32), 0)
 
         def load(dst, src):
             nc.sync.dma_start(dst, src)
 
-        def load_scale_rows(dst, scales):
-            load(dst[RAW_ROWS:P].bitcast(I32), scales.rearrange("a q n -> q a n").bitcast(I32))
+        def load_caller_rows(dst, scales):
+            load(dst.bitcast(I32), scales.rearrange("a q n -> (a q) n").bitcast(I32))
+
+        def load_callee_rows(dst, scales):
+            load(dst.bitcast(I32), scales.rearrange("a q n -> q a n").bitcast(I32))
 
         tab_w = {}
-        w4_raw = {}
-        w1_raw = {}
         wo_raw = {}
 
         def load_tab_words(a):
@@ -102,38 +115,38 @@ def tile_list_excess_delay_causes_kernel(tc, tab_words, tab_scales, offs, pos1, 
             load(tab_w[a][:], tab_words[a].rearrange("p t i -> p (t i)").bitcast(I32))
 
         def load_w4(b, tile):
-            w4_raw[b] = tile
             load(tile[:].bitcast(I32), w4_words[:, :, H * b : H * (b + 1)].rearrange("a p e -> p a e").bitcast(I32))
 
         def load_wo(b):
             wo_raw[b] = placed("wo_raw%d" % b, [P, 4, N], F32, AT_WO[b])
             if b == 0:
-                load(wo_raw[b][:], wo[0:512, :].rearrange("(p t) n -> p t n", t=4))
+                load(wo_raw[b][:], wo[0:HALF, :].rearrange("(p t) n -> p t n", t=4))
             else:
                 for t in range(4):
-                    load(wo_raw[b][:, t, :], wo[512:H, :].rearrange("(q t e) n -> t q e n", t=4, e=8)[t])
+                    load(wo_raw[b][:, t, :], wo[HALF:H, :].rearrange("(q t e) n -> t q e n", t=4, e=8)[t])
 
         def load_w1_columns(tile, lo, hi):
             for a in range(2):
                 load(tile[:, a], w1[512 * a : 512 * (a + 1), lo:hi].rearrange("(p j) c -> p j c", j=4))
 
         load(offs_t[:], offs)
-        load(tab_s[CALLER_ROWS:P].bitcast(I32), tab_scales.rearrange("a q n -> (a q) n").bitcast(I32))
-        load(w4s_raw[CALLER_ROWS:P, 0].bitcast(I32), w4_scales.rearrange("a q n -> (a q) n").bitcast(I32))
+        load_caller_rows(tab_s[CALLER_ROWS:P], tab_scales)
+        load_caller_rows(w4s_raw[CALLER_ROWS:P, 0], w4_scales)
         load(offs2_t[:], offs2)
-        load_scale_rows(tab2_s, tab2_scales)
-        load_scale_rows(w8s_raw, w8_scales)
+        load_callee_rows(tab2_s[CALLEE_ROWS:P], tab2_scales)
+        load_callee_rows(w8s_raw[CALLEE_ROWS:P], w8_scales)
         load_tab_words(0)
-        load_w4(0, held("w4_raw0", [P, 2, H], U8))
+        w4_natural = held("w4_natural", [P, 2, H], U8)
+        load_w4(0, w4_natural)
         load(bias_rows[0:2, :], b1.rearrange("(b c) -> b c", b=2))
         w1_first = held("w1_first", [P, 2, 4, 2 * P], F32)
         load_w1_columns(w1_first, 0, 2 * P)
         load(pos_t[:], pos1)
 
         def deal_scales(dst, raw):
-            nc.vector.tensor_copy(dst[:, :, 0:512].bitcast(I32), raw[:, :, 0:512].bitcast(I32))
-            nc.vector.tensor_copy(dst[:, :, 512:H].bitcast(I32).rearrange("p a (t q i) -> p a t q i", t=4, i=2),
-                                  raw[:, :, 512:H].bitcast(I32).rearrange("p a (q t i) -> p a t q i", t=4, i=2))
+            nc.vector.tensor_copy(dst[:, :, 0:HALF].bitcast(I32), raw[:, :, 0:HALF].bitcast(I32))
+            nc.vector.tensor_copy(dst[:, :, HALF:H].bitcast(I32).rearrange("p a (t q i) -> p a t q i", t=4, i=2),
+                                  raw[:, :, HALF:H].bitcast(I32).rearrange("p a (q t i) -> p a t q i", t=4, i=2))
 
         v_s = placed("v_s", [P, S], U8, AT_V_SCALES)
         nc.vector.tensor_copy(v_s[:], tab_s[:].indirect(offs_t[:]))
@@ -148,25 +161,21 @@ def tile_list_excess_delay_causes_kernel(tc, tab_words, tab_scales, offs, pos1, 
         move_caller_rows(0)
         load_tab_words(1)
         move_caller_rows(1)
-        w1_rest = placed("w1_rest", [P, 2, 4, 2 * P], F32, AT_W1_REST)
-        load_w1_columns(w1_rest, 2 * P, 4 * P)
+        w1_next = placed("w1_next", [P, 2, 4, 2 * P], F32, AT_W1_NEXT)
+        load_w1_columns(w1_next, 2 * P, 4 * P)
 
-        w4_dealt = {}
-        w8_dealt = {}
+        w4_tile = {n: w4_natural[:, :, 2 * P * n : 2 * P * (n + 1)] for n in range(NATURAL)}
 
-        def deal_w4(b, lo, hi, dealt):
+        def deal_w4(dealt):
             nc.vector.tensor_copy(dealt[:].bitcast(I32).rearrange("p a (t q i) -> p a t q i", q=16, i=4),
-                                  w4_raw[b][:].bitcast(I32).rearrange("p a (q t i) -> p a t q i", t=4, i=4)[:, :, lo:hi])
-            for t in range(lo, hi):
-                w4_dealt[4 * b + t] = dealt[:, :, 2 * P * (t - lo) : 2 * P * (t - lo + 1)]
+                                  w4_raw[:].bitcast(I32).rearrange("p a (q t i) -> p a t q i", t=4, i=4))
+            for t in range(4):
+                w4_tile[NATURAL + t] = dealt[:, :, 2 * P * t : 2 * P * (t + 1)]
 
-        def deal_w8(b, dealt):
-            w8_dealt[b] = dealt
+        def deal_w8(dealt):
+            w8_half[1] = dealt
             nc.vector.tensor_copy(dealt[:].rearrange("p a (t q e) -> p a t q e", t=4, e=8),
-                                  w8_raw[:, :, 512 * b : 512 * (b + 1)].rearrange("p a (q t e) -> p a t q e", t=4, e=8))
-
-        for n in range(4):
-            w4_dealt[n] = w4_raw[0][:, :, 2 * P * n : 2 * P * (n + 1)]
+                                  w8_raw[:, :, HALF:H].rearrange("p a (q t e) -> p a t q e", t=4, e=8))
 
         v_w = {(a, hf): held("v_w%d%d" % (a, hf), [P, BANK], U32) for a in range(2) for hf in range(2)}
 
@@ -175,7 +184,8 @@ def tile_list_excess_delay_causes_kernel(tc, tab_words, tab_scales, offs, pos1, 
                 nc.vector.tensor_copy(v_w[a, hf][:], tab_w[a][:].bitcast(U32).indirect(offs_t[:, 32 * hf : 32 * (hf + 1)]))
 
         gather_callers(0)
-        load_w4(1, placed("w4_raw1", [P, 2, H], U8, AT_W4_RAW))
+        w4_raw = placed("w4_raw", [P, 2, H], U8, AT_W4_DEALT_RAW)
+        load_w4(1, w4_raw)
         tab2_w = placed("tab2_w", [P, 2, T2], I32, AT_TABLE2)
         load(tab2_w[:], tab2_words.rearrange("a p t i -> p a (t i)").bitcast(I32))
 
@@ -185,7 +195,7 @@ def tile_list_excess_delay_causes_kernel(tc, tab_words, tab_scales, offs, pos1, 
         deal_scales(callee_s[:, :, W8_AT : W8_AT + H], w8s_raw[:])
         nc.vector.tensor_copy(callee_s[:, :, V2_AT : V2_AT + M].bitcast(I32), v2_s[:].bitcast(I32))
         for s in range(4):
-            load(callee_s[4 + s : P : 32].bitcast(I32), callee_s[RAW_ROWS + s : P : 4].bitcast(I32))
+            load(callee_s[4 + s : P : 32].bitcast(I32), callee_s[CALLEE_ROWS + s : P : 4].bitcast(I32))
 
         nc.scalar.copy(bias_dealt[:].rearrange("p t (q e) -> p t q e", e=8), bias_rows[:].rearrange("p (q t e) -> p t q e", t=4, e=8))
         for b, rows in enumerate((bias_rows[:].rearrange("p (t c) -> p t c", t=4), bias_dealt[:])):
@@ -195,41 +205,44 @@ def tile_list_excess_delay_causes_kernel(tc, tab_words, tab_scales, offs, pos1, 
             nc.scalar.copy(bias[:, 4 * b : 4 * (b + 1)], bias_ps[:, b:BANK:P])
         nc.scalar.activation(minus_bias[:], bias[:], IDENTITY, scale=-1.0)
 
+        w1_c = [held("w1_c%d" % n, [P, 2, P], U32) for n in range(TILES)]
+        w1_s = [held("w1_s%d" % n, [P, 2, P], U8) for n in range(TILES)]
         w1_rounded = {}
-        first_c = [held("first_c%d" % n, [P, 2, P], U32) for n in range(TILES)]
-        first_s = [held("first_s%d" % n, [P, 2, P], U8) for n in range(TILES)]
-        first_rounded = {}
+        ROUNDED = [P, 2, P, 4]
 
-        def round_first(n, lo, hi):
-            raw = (w1_first, w1_rest)[n // 2][:, :, :, P * (n % 2) : P * (n % 2 + 1)]
-            shape = [P, hi - lo, P, 4]
-            first_rounded[n, lo] = held("first_rounded%d" % n, shape, BF16) if n < 2 else after_y(1, n - 2, "first_rounded", shape, BF16)
-            nc.scalar.copy(first_rounded[n, lo][:].rearrange("p a (c i) j -> p a c j i", i=4), raw[:, lo:hi].rearrange("p a j (c i) -> p a c j i", i=4))
+        def round_natural(n):
+            raw = (w1_first, w1_next)[n // 2][:, :, :, P * (n % 2) : P * (n % 2 + 1)]
+            w1_rounded[n] = held("first_rounded%d" % n, ROUNDED, BF16) if n < 2 else after_y(1, n - 2, "next_rounded", ROUNDED, BF16)
+            nc.scalar.copy(w1_rounded[n][:].rearrange("p a (c i) j -> p a c j i", i=4), raw.rearrange("p a j (c i) -> p a c j i", i=4))
 
-        def quantize_first(n, lo, hi):
-            nc.vector.quantize_mx(out=first_c[n][:, lo:hi].rearrange("p a c -> p (a c)").bitcast(FP8X4), scales=first_s[n][:, lo:hi].rearrange("p a c -> p (a c)"),
-                                  in_=first_rounded[n, lo][:].rearrange("p a c j -> p (a c j)"))
+        def round_dealt(n):
+            name = "late_rounded%d" % n
+            w1_rounded[n] = placed(name, ROUNDED, BF16, AT_LATE_ROUNDED[n]) if n in AT_LATE_ROUNDED else held(name, ROUNDED, BF16)
+            nc.scalar.copy(w1_rounded[n][:].rearrange("p a (q e) j -> p a q j e", e=8),
+                           w1_late[:].rearrange("p a j (q t e) -> p t a q j e", t=4, e=8)[:, n - NATURAL])
 
-        wo_rounded = {}
+        def quantize_w1(n):
+            nc.vector.quantize_mx(out=w1_c[n][:].rearrange("p a c -> p (a c)").bitcast(FP8X4), scales=w1_s[n][:].rearrange("p a c -> p (a c)"),
+                                  in_=w1_rounded[n][:].rearrange("p a c j -> p (a c j)"))
+
         wo_s = held("wo_s", [P, 2 * N], U8)
+        wo_c = held("wo_c", [P, 2 * N], U32)
 
-        def round_wo(b, rounded):
-            wo_rounded[b] = rounded
+        def round_and_quantize_wo(b):
+            rounded = placed("wo_rounded%d" % b, [P, N, 4], BF16, AT_WO_ROUNDED[b])
             nc.scalar.copy(rounded[:].rearrange("p (c i) t -> p c t i", i=4), wo_raw[b][:].rearrange("p t (c i) -> p c t i", i=4))
-
-        def quantize_wo(b):
-            flat = wo_rounded[b][:].rearrange("p n t -> p (n t)")
+            flat = rounded[:].rearrange("p n t -> p (n t)")
             for lo, hi in ((0, 256), (256, N)):
                 nc.vector.quantize_mx(out=wo_c[:, N * b + lo : N * b + hi].bitcast(FP8X4), scales=wo_s[:, N * b + lo : N * b + hi], in_=flat[:, 4 * lo : 4 * hi])
 
-        round_first(0, 0, 2)
-        quantize_first(0, 0, 2)
+        round_natural(0)
+        quantize_w1(0)
         gather_callers(1)
+        w1_late = placed("w1_late", [P, 2, 4, HALF], F32, AT_W1_LATE)
+        load_w1_columns(w1_late, HALF, H)
         w8_raw = placed("w8_raw", [P, 2, H], I32, AT_W8)
-        w8_dealt[0] = w8_raw
-        w1_late = placed("w1_late", [P, 2, 4, 512], F32, AT_W1_LATE)
-        load_w1_columns(w1_late, 512, H)
         load(w8_raw[:], w8_words.rearrange("a p e i -> p a (e i)").bitcast(I32))
+        w8_half = {0: w8_raw}
 
         y = {}
         summed = {}
@@ -237,9 +250,7 @@ def tile_list_excess_delay_causes_kernel(tc, tab_words, tab_scales, offs, pos1, 
         picked = {}
         own = {}
         own_copy = {}
-        minus_excess = [placed("minus_excess0", [P, 4, M], F32, AT_Y + 8), held("minus_excess1", [P, 4, M], F32)]
-
-        natural = {}
+        minus_excess = [placed("minus_excess0", [P, 4, M], F32, AT_EXCESS), held("minus_excess1", [P, 4, M], F32)]
 
         def callers(a, hf):
             return dict(rhs=v_w[a, hf][:].bitcast(FP8X4), rhs_scale=caller_s[a][:, V_AT + BANK * hf : V_AT + BANK * (hf + 1)], start=(a == 0), stop=(a == 1))
@@ -250,10 +261,9 @@ def tile_list_excess_delay_causes_kernel(tc, tab_words, tab_scales, offs, pos1, 
         def w4_pass(n, hf, a):
             if a == 0:
                 p4[n, hf] = psum.tile([P, BANK], F32, name="p4", tag="p4")
-            nc.tensor.matmul_mx(out=p4[n, hf][:], lhsT=w4_dealt[n][:, a, :].bitcast(FP4X4), lhsT_scale=caller_s[a][:, W4_AT + P * n : W4_AT + P * (n + 1)], **callers(a, hf))
+            nc.tensor.matmul_mx(out=p4[n, hf][:], lhsT=w4_tile[n][:, a, :].bitcast(FP4X4), lhsT_scale=caller_s[a][:, W4_AT + P * n : W4_AT + P * (n + 1)], **callers(a, hf))
             if a == 1:
-                tag = "late_rounded%d" % (2 * n + hf - 5) if (n, hf) in ((5, 0), (5, 1), (6, 0)) else "y%d%d" % (n, hf)
-                y[n, hf] = placed("y50", [P, BANK], F32, AT_Y + 3) if (n, hf) == (5, 0) else keep.tile([P, BANK], F32, name="y", tag=tag, align_bytes=64)
+                y[n, hf] = placed("y_tile5", [P, BANK], F32, AT_Y_TILE5) if (n, hf) == (5, 0) else after(y_tag(n, hf), "y", [P, BANK], F32)
                 nc.scalar.activation(y[n, hf][:], p4[n, hf][:], IDENTITY, bias=bias[:, n : n + 1])
 
         def w4_product(n):
@@ -262,15 +272,12 @@ def tile_list_excess_delay_causes_kernel(tc, tab_words, tab_scales, offs, pos1, 
                     w4_pass(n, hf, a)
 
         def w1_pass(n, hf, a):
-            b, t = divmod(n, 4)
-            cols = slice(P * t, P * (t + 1))
             if a == 0:
                 p1[n, hf] = psum.tile([P, BANK], F32, name="p1", tag="p1")
-            codes, scales = first_c[n][:, a], first_s[n][:, a]
-            nc.tensor.matmul_mx(out=p1[n, hf][:], lhsT=codes.bitcast(FP8X4), lhsT_scale=scales, **callers(a, hf))
+            nc.tensor.matmul_mx(out=p1[n, hf][:], lhsT=w1_c[n][:, a].bitcast(FP8X4), lhsT_scale=w1_s[n][:, a], **callers(a, hf))
 
-        def w1_product(n, hf):
-            for a in range(2) if n > 0 else (1,):
+        def w1_product_and_add(n, hf, passes=range(2)):
+            for a in passes:
                 w1_pass(n, hf, a)
             if hf == 0:
                 window[n] = ring.tile([P, S], F32, name="window", bufs=3)
@@ -285,29 +292,26 @@ def tile_list_excess_delay_causes_kernel(tc, tab_words, tab_scales, offs, pos1, 
             b, t = divmod(n, 4)
             own[n] = psum.tile([P, BANK], F32, name="own", tag="callee", bufs=2)
             for a in range(2):
-                nc.tensor.matmul_mx(out=own[n][:], lhsT=w8_dealt[b][:, a, P * t : P * (t + 1)].bitcast(FP8X4),
+                nc.tensor.matmul_mx(out=own[n][:], lhsT=w8_half[b][:, a, P * t : P * (t + 1)].bitcast(FP8X4),
                                     lhsT_scale=callee_s[4:P, a, W8_AT + P * n : W8_AT + P * (n + 1)],
                                     rhs=v2_w[a][:].bitcast(FP8X4), rhs_scale=callee_s[4:P, a, V2_AT : V2_AT + M], start=(a == 0), stop=(a == 1))
             if n in FUSED:
-                own_copy[n] = placed("own_copy%d" % n, [P, M], F32, AT_Y + (1, 5)[n % 2])
+                own_copy[n] = placed("own_copy%d" % n, [P, M], F32, AT_OWN_COPY[n % 2])
                 nc.scalar.copy(own_copy[n][:], own[n][:])
 
-        def pick(n, lo, hi, tile):
-            picked[n, lo] = tile
-            nc.vector.tensor_copy(tile[:], window[n][:].indirect(pos_t[:, lo // 16 : hi // 16]))
+        def pick(n, lo, hi):
+            picked[n, lo] = ring.tile([P, hi - lo], F32, name="picked", bufs=2, align_bytes=64)
+            nc.vector.tensor_copy(picked[n, lo][:], window[n][:].indirect(pos_t[:, lo // 16 : hi // 16]))
 
         def subtract(n, lo, hi):
-            b, t = divmod(n, 4)
-            if b == 0:
-                natural[n] = held("natural%d" % n, [P, M], F32)
-            target = natural[n][:, lo:hi] if b == 0 else minus_excess[b][:, t, lo:hi]
+            target = held("natural%d" % n, [P, M], F32)[:] if n < NATURAL else minus_excess[1][:, n - NATURAL, lo:hi]
             if n in FUSED:
                 nc.vector.tensor_tensor(target, window[n][:].indirect(pos_t[:, lo // 16 : hi // 16]), own_copy[n][:, lo:hi], ALU.subtract)
             else:
                 nc.vector.scalar_tensor_tensor(target, picked[n, lo][:], 0.0, own[n][:, lo:hi], ALU.max, ALU.subtract)
-            if b == 0:
-                for place in range(4):
-                    load(minus_excess[0][32 * n : 32 * (n + 1), place, :], natural[n][place:P:4, :])
+            if n < NATURAL:
+                for t in range(4):
+                    nc.sync.dma_start(minus_excess[0][32 * n : 32 * (n + 1), t, :], target[t:P:4, :])
 
         h_rounded = {}
         h_c = {}
@@ -315,9 +319,9 @@ def tile_list_excess_delay_causes_kernel(tc, tab_words, tab_scales, offs, pos1, 
 
         def h_views(b, lo):
             if b == 0:
-                h_rounded[b, lo] = keep.tile([P, PIECE, 4], BF16, name="h_rounded", tag=("late_rounded7", "y61")[lo // PIECE], align_bytes=64)
+                h_rounded[b, lo] = after_y(6, lo // PIECE, "h_rounded", [P, PIECE, 4], BF16)
             else:
-                h_rounded[b, lo] = placed("h_rounded%d" % lo, [P, PIECE, 4], BF16, AT_Y + 8 + 2 * (lo // PIECE))
+                h_rounded[b, lo] = placed("h_rounded%d" % lo, [P, PIECE, 4], BF16, AT_EXCESS + 2 * (lo // PIECE))
             return (h_rounded[b, lo][:].rearrange("p (c i) t -> p c t i", i=4),
                     minus_excess[b][:, :, lo : lo + PIECE].rearrange("p t (c i) -> p c t i", i=4))
 
@@ -330,84 +334,74 @@ def tile_list_excess_delay_causes_kernel(tc, tab_words, tab_scales, offs, pos1, 
             h_s[b, lo] = held("h_s%d_%d" % (b, lo), [P, PIECE], U8)
             nc.vector.quantize_mx(out=h_c[b, lo][:].bitcast(FP8X4), scales=h_s[b, lo][:], in_=h_rounded[b, lo][:].rearrange("p m t -> p (m t)"))
 
-        def late_piece(n):
-            rounded = placed("late_rounded%d" % n, [P, 2, P, 4], BF16, AT_Y + 4 * (n - 4)) if n < 6 else held("late_rounded%d" % n, [P, 2, P, 4], BF16)
-            first_rounded[n, 0] = rounded
-            nc.scalar.copy(rounded[:].rearrange("p a (q e) j -> p a q j e", e=8), w1_late[:].rearrange("p a j (q t e) -> p t a q j e", t=4, e=8)[:, n - 4])
-            quantize_first(n, 0, 2)
-
         v2_w = {}
 
         def gather_callees(a):
             v2_w[a] = after_y(1, a, "v2_w", [P, M], U32)
             nc.vector.tensor_copy(v2_w[a][:], tab2_w[:, a, :].bitcast(U32).indirect(offs2_t[:]))
 
-        def picks(n):
-            pick(n, 0, M, ring.tile([P, M], F32, name="picked", bufs=2, align_bytes=64))
-
         for hf in range(2):
             w4_pass(0, hf, 0)
             w1_pass(0, hf, 0)
-        round_first(1, 0, 2)
-        quantize_first(1, 0, 2)
+        round_natural(1)
+        quantize_w1(1)
         for hf in range(2):
             w4_pass(0, hf, 1)
-            w1_product(0, hf)
+            w1_product_and_add(0, hf, passes=(1,))
         w4_product(1)
         for hf in range(2):
-            w1_product(1, hf)
-        round_first(2, 0, 2)
-        picks(0)
-        deal_w4(1, 0, 4, after_y(0, 1, "w4_second", [P, 2, H], U8))
-        picks(1)
-        quantize_first(2, 0, 2)
+            w1_product_and_add(1, hf)
+        round_natural(2)
+        pick(0, 0, M)
+        deal_w4(after_y(0, 1, "w4_dealt", [P, 2, H], U8))
+        pick(1, 0, M)
+        quantize_w1(2)
         gather_callees(0)
+
         w4_product(2)
-        round_first(3, 0, 2)
-        load_wo(0)
-        load_wo(1)
+        round_natural(3)
+        for b in range(2):
+            load_wo(b)
         for hf in range(2):
-            w1_product(2, hf)
-        quantize_first(3, 0, 2)
+            w1_product_and_add(2, hf)
+        quantize_w1(3)
         gather_callees(1)
         w4_product(3)
         for n in range(2):
             w8_product(n)
             subtract(n, 0, M)
-        w4_product(4)
-        for n in range(4, TILES):
-            late_piece(n)
-        round_wo(0, placed("wo_rounded0", [P, N, 4], BF16, AT_W1_LATE))
-        for n in range(3, TILES):
+        w4_product(NATURAL)
+        for n in range(NATURAL, TILES):
+            round_dealt(n)
+            quantize_w1(n)
+        round_and_quantize_wo(0)
+
+        for n in range(NATURAL - 1, TILES):
             for hf in range(2):
-                w1_product(n, hf)
+                w1_product_and_add(n, hf)
             w8_product(n - 1)
             subtract(n - 1, 0, M)
-            if n == 3:
-                deal_w8(1, placed("w8_dealt", [P, 2, 512], I32, AT_Y - 3.9375))
-            if n in (4, 5, 6):
+            if n == NATURAL - 1:
+                deal_w8(placed("w8_dealt", [P, 2, HALF], I32, AT_W8_DEALT))
+            elif n + 1 < TILES:
                 w4_product(n + 1)
-            if n == 5:
-                round_wo(1, placed("wo_rounded1", [P, N, 4], BF16, AT_W1_LATE + 3))
-            if n == 7:
-                for lo in (0, PIECE):
-                    round_h(0, lo)
-                for lo in (0, PIECE):
-                    quantize_h(0, lo)
+            if n == NATURAL + 1:
+                round_and_quantize_wo(1)
+        for lo in (0, PIECE):
+            round_h(0, lo)
+        for lo in (0, PIECE):
+            quantize_h(0, lo)
 
         last = TILES - 1
         w8_product(last)
-        pick(last, 0, PIECE, placed("last_picks", [P, PIECE], F32, AT_LAST_PICKS))
-        subtract(last, 0, PIECE)
-        wo_c = placed("wo_c", [P, 2 * N], U32, AT_LAST_PICKS)
-        quantize_wo(0)
-        pick(last, PIECE, M, ring.tile([P, PIECE], F32, name="picked", bufs=2, align_bytes=64))
-        subtract(last, PIECE, M)
-        quantize_wo(1)
+        for lo in (0, PIECE):
+            pick(last, lo, lo + PIECE)
+            subtract(last, lo, lo + PIECE)
         round_h(1, 0)
         dst, src = h_views(1, PIECE)
-        nc.vector.tensor_scalar(dst[:, 0:32], src[:, 0:32], -1.0, 0.0, ALU.mult, ALU.max)
-        nc.scalar.activation(dst[:, 32:64], src[:, 32:64], RELU, scale=-1.0)
+        groups = PIECE // 4
+        nc.vector.tensor_scalar(dst[:, 0 : groups // 2], src[:, 0 : groups // 2], -1.0, 0.0, ALU.mult, ALU.max)
+        nc.scalar.activation(dst[:, groups // 2 : groups], src[:, groups // 2 : groups], RELU, scale=-1.0)
 
         def score_pass(b, lo, c):
             cols = slice(N * b + P * c, N * b + P * (c + 1))

@@ -29,7 +29,8 @@ CALLER_ROWS = 96
 CALLEE_ROWS = 112
 V_AT, W4_AT, CALLER_WIDTH = 0, S, S + H
 V2_AT, W8_AT, CALLEE_WIDTH = 0, M, M + H
-FUSED = range(2, 7)
+FUSED = range(2, 8)
+LAST = TILES - 1
 
 AT_TABLE = (1, 24)
 AT_W4_DEALT_RAW = 0
@@ -231,9 +232,7 @@ def tile_list_excess_delay_causes_kernel(tc, tab_words, tab_scales, offs, pos1, 
         def round_and_quantize_wo(b):
             rounded = placed("wo_rounded%d" % b, [P, N, 4], BF16, AT_WO_ROUNDED[b])
             nc.scalar.copy(rounded[:].rearrange("p (c i) t -> p c t i", i=4), wo_raw[b][:].rearrange("p t (c i) -> p c t i", i=4))
-            flat = rounded[:].rearrange("p n t -> p (n t)")
-            for lo, hi in ((0, 256), (256, N)):
-                nc.vector.quantize_mx(out=wo_c[:, N * b + lo : N * b + hi].bitcast(FP8X4), scales=wo_s[:, N * b + lo : N * b + hi], in_=flat[:, 4 * lo : 4 * hi])
+            nc.vector.quantize_mx(out=wo_c[:, N * b : N * (b + 1)].bitcast(FP8X4), scales=wo_s[:, N * b : N * (b + 1)], in_=rounded[:].rearrange("p n t -> p (n t)"))
 
         round_natural(0)
         quantize_w1(0)
@@ -260,11 +259,14 @@ def tile_list_excess_delay_causes_kernel(tc, tab_words, tab_scales, offs, pos1, 
 
         def w4_pass(n, hf, a):
             if a == 0:
-                p4[n, hf] = psum.tile([P, BANK], F32, name="p4", tag="p4")
+                p4[n, hf] = psum.tile([P, BANK], F32, name="p4", tag="callee", bufs=2) if (n, hf) == (1, 1) else psum.tile([P, BANK], F32, name="p4", tag="p4")
             nc.tensor.matmul_mx(out=p4[n, hf][:], lhsT=w4_tile[n][:, a, :].bitcast(FP4X4), lhsT_scale=caller_s[a][:, W4_AT + P * n : W4_AT + P * (n + 1)], **callers(a, hf))
             if a == 1:
                 y[n, hf] = placed("y_tile5", [P, BANK], F32, AT_Y_TILE5) if (n, hf) == (5, 0) else after(y_tag(n, hf), "y", [P, BANK], F32)
-                nc.scalar.activation(y[n, hf][:], p4[n, hf][:], IDENTITY, bias=bias[:, n : n + 1])
+                if n == LAST:
+                    nc.scalar.activation(y[n, hf][:], p4[n, hf][:], RELU)
+                else:
+                    nc.scalar.activation(y[n, hf][:], p4[n, hf][:], IDENTITY, bias=bias[:, n : n + 1])
 
         def w4_product(n):
             for hf in range(2):
@@ -273,16 +275,23 @@ def tile_list_excess_delay_causes_kernel(tc, tab_words, tab_scales, offs, pos1, 
 
         def w1_pass(n, hf, a):
             if a == 0:
-                p1[n, hf] = psum.tile([P, BANK], F32, name="p1", tag="p1")
+                p1[n, hf] = psum.tile([P, BANK], F32, name="p1", tag="callee", bufs=2) if (n, hf) == (1, 1) else psum.tile([P, BANK], F32, name="p1", tag="p1")
             nc.tensor.matmul_mx(out=p1[n, hf][:], lhsT=w1_c[n][:, a].bitcast(FP8X4), lhsT_scale=w1_s[n][:, a], **callers(a, hf))
+            if a == 0 and n == LAST:
+                for a4 in range(2):
+                    nc.tensor.matmul_mx(out=p1[n, hf][:], lhsT=w4_tile[n][:, a4, :].bitcast(FP4X4), lhsT_scale=caller_s[a4][:, W4_AT + P * n : W4_AT + P * (n + 1)],
+                                        **dict(callers(a4, hf), start=False, stop=False))
 
         def w1_product_and_add(n, hf, passes=range(2)):
             for a in passes:
                 w1_pass(n, hf, a)
             if hf == 0:
                 window[n] = ring.tile([P, S], F32, name="window", bufs=3)
-                if n in FUSED:
+                if n in FUSED and n < LAST:
                     summed[n] = ring.tile([P, S], F32, name="summed", bufs=3)
+            if n == LAST:
+                nc.vector.scalar_tensor_tensor(window[n][:, BANK * hf : BANK * (hf + 1)], p1[n, hf][:], bias[:, n : n + 1], y[n, hf][:], ALU.add, ALU.max)
+                return
             target = (summed[n] if n in FUSED else window[n])[:, BANK * hf : BANK * (hf + 1)]
             nc.vector.scalar_tensor_tensor(target, p1[n, hf][:], minus_bias[:, n : n + 1], y[n, hf][:], ALU.max, ALU.add)
             if n in FUSED:
@@ -310,8 +319,7 @@ def tile_list_excess_delay_causes_kernel(tc, tab_words, tab_scales, offs, pos1, 
             else:
                 nc.vector.scalar_tensor_tensor(target, picked[n, lo][:], 0.0, own[n][:, lo:hi], ALU.max, ALU.subtract)
             if n < NATURAL:
-                for t in range(4):
-                    nc.sync.dma_start(minus_excess[0][32 * n : 32 * (n + 1), t, :], target[t:P:4, :])
+                nc.sync.dma_start(minus_excess[0][32 * n : 32 * (n + 1)], target)
 
         h_rounded = {}
         h_c = {}
@@ -346,11 +354,12 @@ def tile_list_excess_delay_causes_kernel(tc, tab_words, tab_scales, offs, pos1, 
         round_natural(1)
         quantize_w1(1)
         for hf in range(2):
-            w4_pass(0, hf, 1)
-            w1_product_and_add(0, hf, passes=(1,))
-        w4_product(1)
+            w4_pass(1, hf, 0)
+            w1_pass(1, hf, 0)
         for hf in range(2):
-            w1_product_and_add(1, hf)
+            for n in range(2):
+                w4_pass(n, hf, 1)
+                w1_product_and_add(n, hf, passes=(1,))
         round_natural(2)
         pick(0, 0, M)
         deal_w4(after_y(0, 1, "w4_dealt", [P, 2, H], U8))
@@ -395,7 +404,6 @@ def tile_list_excess_delay_causes_kernel(tc, tab_words, tab_scales, offs, pos1, 
         last = TILES - 1
         w8_product(last)
         for lo in (0, PIECE):
-            pick(last, lo, lo + PIECE)
             subtract(last, lo, lo + PIECE)
         round_h(1, 0)
         dst, src = h_views(1, PIECE)

@@ -214,7 +214,8 @@ def tile_list_excess_delay_causes_kernel(tc, tab_words, tab_scales, offs, pos1, 
         def round_natural(n):
             raw = (w1_first, w1_next)[n // 2][:, :, :, P * (n % 2) : P * (n % 2 + 1)]
             w1_rounded[n] = held("first_rounded%d" % n, ROUNDED, BF16) if n < 2 else after_y(1, n - 2, "next_rounded", ROUNDED, BF16)
-            nc.scalar.copy(w1_rounded[n][:].rearrange("p a (c i) j -> p a c j i", i=4), raw.rearrange("p a j (c i) -> p a c j i", i=4))
+            copy = nc.vector.tensor_copy if n == 3 else nc.scalar.copy
+            copy(w1_rounded[n][:].rearrange("p a (c i) j -> p a c j i", i=4), raw.rearrange("p a j (c i) -> p a c j i", i=4))
 
         def round_dealt(n):
             name = "late_rounded%d" % n

@@ -29,8 +29,8 @@ CALLER_ROWS = 96
 CALLEE_ROWS = 112
 V_AT, W4_AT, CALLER_WIDTH = 0, S, S + H
 V2_AT, W8_AT, CALLEE_WIDTH = 0, M, M + H
-FUSED = range(2, 8)
 LAST = TILES - 1
+FUSED = range(2, TILES)
 
 AT_TABLE = (1, 24)
 AT_W4_DEALT_RAW = 0
@@ -213,9 +213,13 @@ def tile_list_excess_delay_causes_kernel(tc, tab_words, tab_scales, offs, pos1, 
 
         def round_natural(n):
             raw = (w1_first, w1_next)[n // 2][:, :, :, P * (n % 2) : P * (n % 2 + 1)]
-            w1_rounded[n] = held("first_rounded%d" % n, ROUNDED, BF16) if n < 2 else after_y(1, n - 2, "next_rounded", ROUNDED, BF16)
-            copy = nc.vector.tensor_copy if n == 3 else nc.scalar.copy
-            copy(w1_rounded[n][:].rearrange("p a (c i) j -> p a c j i", i=4), raw.rearrange("p a j (c i) -> p a c j i", i=4))
+            if n == 3:
+                w1_rounded[n] = held("next_rounded3", ROUNDED, BF16)
+                for a in range(2):
+                    nc.gpsimd.tensor_scalar(w1_rounded[n][:, a], raw[:, a].rearrange("p j c -> p c j"), 1.0, 0.0, ALU.mult, ALU.add)
+                return
+            w1_rounded[n] = held("first_rounded%d" % n, ROUNDED, BF16) if n < 2 else after_y(1, 0, "next_rounded", ROUNDED, BF16)
+            nc.scalar.copy(w1_rounded[n][:].rearrange("p a (c i) j -> p a c j i", i=4), raw.rearrange("p a j (c i) -> p a c j i", i=4))
 
         def round_dealt(n):
             name = "late_rounded%d" % n
@@ -253,15 +257,23 @@ def tile_list_excess_delay_causes_kernel(tc, tab_words, tab_scales, offs, pos1, 
         minus_excess = [placed("minus_excess0", [P, 4, M], F32, AT_EXCESS), held("minus_excess1", [P, 4, M], F32)]
 
         def callers(a, hf):
-            return dict(rhs=v_w[a, hf][:].bitcast(FP8X4), rhs_scale=caller_s[a][:, V_AT + BANK * hf : V_AT + BANK * (hf + 1)], start=(a == 0), stop=(a == 1))
+            return dict(rhs=v_w[a, hf][:].bitcast(FP8X4), rhs_scale=caller_s[a][:, V_AT + BANK * hf : V_AT + BANK * (hf + 1)])
 
         p4 = {}
         p1 = {}
 
+        def sum_bank(name, n, hf):
+            if (n, hf) == (1, 1):
+                return psum.tile([P, BANK], F32, name=name, tag="callee", bufs=2)
+            return psum.tile([P, BANK], F32, name=name, tag=name)
+
+        def w4_operand(n, a):
+            return dict(lhsT=w4_tile[n][:, a, :].bitcast(FP4X4), lhsT_scale=caller_s[a][:, W4_AT + P * n : W4_AT + P * (n + 1)])
+
         def w4_pass(n, hf, a):
             if a == 0:
-                p4[n, hf] = psum.tile([P, BANK], F32, name="p4", tag="callee", bufs=2) if (n, hf) == (1, 1) else psum.tile([P, BANK], F32, name="p4", tag="p4")
-            nc.tensor.matmul_mx(out=p4[n, hf][:], lhsT=w4_tile[n][:, a, :].bitcast(FP4X4), lhsT_scale=caller_s[a][:, W4_AT + P * n : W4_AT + P * (n + 1)], **callers(a, hf))
+                p4[n, hf] = sum_bank("p4", n, hf)
+            nc.tensor.matmul_mx(out=p4[n, hf][:], start=(a == 0), stop=(a == 1), **w4_operand(n, a), **callers(a, hf))
             if a == 1:
                 y[n, hf] = placed("y_tile5", [P, BANK], F32, AT_Y_TILE5) if (n, hf) == (5, 0) else after(y_tag(n, hf), "y", [P, BANK], F32)
                 if n == LAST:
@@ -276,27 +288,28 @@ def tile_list_excess_delay_causes_kernel(tc, tab_words, tab_scales, offs, pos1, 
 
         def w1_pass(n, hf, a):
             if a == 0:
-                p1[n, hf] = psum.tile([P, BANK], F32, name="p1", tag="callee", bufs=2) if (n, hf) == (1, 1) else psum.tile([P, BANK], F32, name="p1", tag="p1")
-            nc.tensor.matmul_mx(out=p1[n, hf][:], lhsT=w1_c[n][:, a].bitcast(FP8X4), lhsT_scale=w1_s[n][:, a], **callers(a, hf))
+                p1[n, hf] = sum_bank("p1", n, hf)
+            nc.tensor.matmul_mx(out=p1[n, hf][:], lhsT=w1_c[n][:, a].bitcast(FP8X4), lhsT_scale=w1_s[n][:, a], start=(a == 0), stop=(a == 1), **callers(a, hf))
             if a == 0 and n == LAST:
                 for a4 in range(2):
-                    nc.tensor.matmul_mx(out=p1[n, hf][:], lhsT=w4_tile[n][:, a4, :].bitcast(FP4X4), lhsT_scale=caller_s[a4][:, W4_AT + P * n : W4_AT + P * (n + 1)],
-                                        **dict(callers(a4, hf), start=False, stop=False))
+                    nc.tensor.matmul_mx(out=p1[n, hf][:], start=False, stop=False, **w4_operand(n, a4), **callers(a4, hf))
 
         def w1_product_and_add(n, hf, passes=range(2)):
             for a in passes:
                 w1_pass(n, hf, a)
+            by_gpsimd = n in FUSED and n < LAST
             if hf == 0:
                 window[n] = ring.tile([P, S], F32, name="window", bufs=3)
-                if n in FUSED and n < LAST:
+                if by_gpsimd:
                     summed[n] = ring.tile([P, S], F32, name="summed", bufs=3)
+            half = slice(BANK * hf, BANK * (hf + 1))
             if n == LAST:
-                nc.vector.scalar_tensor_tensor(window[n][:, BANK * hf : BANK * (hf + 1)], p1[n, hf][:], bias[:, n : n + 1], y[n, hf][:], ALU.add, ALU.max)
+                nc.vector.scalar_tensor_tensor(window[n][:, half], p1[n, hf][:], bias[:, n : n + 1], y[n, hf][:], ALU.add, ALU.max)
                 return
-            target = (summed[n] if n in FUSED else window[n])[:, BANK * hf : BANK * (hf + 1)]
+            target = (summed if by_gpsimd else window)[n][:, half]
             nc.vector.scalar_tensor_tensor(target, p1[n, hf][:], minus_bias[:, n : n + 1], y[n, hf][:], ALU.max, ALU.add)
-            if n in FUSED:
-                nc.gpsimd.tensor_scalar(window[n][:, BANK * hf : BANK * (hf + 1)], target, FLOAT32_MAX, 0.0, ALU.min, ALU.max)
+            if by_gpsimd:
+                nc.gpsimd.tensor_scalar(window[n][:, half], target, FLOAT32_MAX, 0.0, ALU.min, ALU.max)
 
         def w8_product(n):
             b, t = divmod(n, 4)
@@ -309,16 +322,16 @@ def tile_list_excess_delay_causes_kernel(tc, tab_words, tab_scales, offs, pos1, 
                 own_copy[n] = placed("own_copy%d" % n, [P, M], F32, AT_OWN_COPY[n % 2])
                 nc.scalar.copy(own_copy[n][:], own[n][:])
 
-        def pick(n, lo, hi):
-            picked[n, lo] = ring.tile([P, hi - lo], F32, name="picked", bufs=2, align_bytes=64)
-            nc.vector.tensor_copy(picked[n, lo][:], window[n][:].indirect(pos_t[:, lo // 16 : hi // 16]))
+        def pick(n):
+            picked[n] = ring.tile([P, M], F32, name="picked", bufs=2, align_bytes=64)
+            nc.vector.tensor_copy(picked[n][:], window[n][:].indirect(pos_t[:]))
 
         def subtract(n, lo, hi):
             target = held("natural%d" % n, [P, M], F32)[:] if n < NATURAL else minus_excess[1][:, n - NATURAL, lo:hi]
             if n in FUSED:
                 nc.vector.tensor_tensor(target, window[n][:].indirect(pos_t[:, lo // 16 : hi // 16]), own_copy[n][:, lo:hi], ALU.subtract)
             else:
-                nc.vector.scalar_tensor_tensor(target, picked[n, lo][:], 0.0, own[n][:, lo:hi], ALU.max, ALU.subtract)
+                nc.vector.scalar_tensor_tensor(target, picked[n][:], 0.0, own[n][:], ALU.max, ALU.subtract)
             if n < NATURAL:
                 nc.sync.dma_start(minus_excess[0][32 * n : 32 * (n + 1)], target)
 
@@ -346,7 +359,7 @@ def tile_list_excess_delay_causes_kernel(tc, tab_words, tab_scales, offs, pos1, 
         v2_w = {}
 
         def gather_callees(a):
-            v2_w[a] = after_y(1, a, "v2_w", [P, M], U32)
+            v2_w[a] = after((y_tag(1, 0), "next_rounded3")[a], "v2_w", [P, M], U32)
             nc.vector.tensor_copy(v2_w[a][:], tab2_w[:, a, :].bitcast(U32).indirect(offs2_t[:]))
 
         for hf in range(2):
@@ -362,9 +375,9 @@ def tile_list_excess_delay_causes_kernel(tc, tab_words, tab_scales, offs, pos1, 
                 w4_pass(n, hf, 1)
                 w1_product_and_add(n, hf, passes=(1,))
         round_natural(2)
-        pick(0, 0, M)
+        pick(0)
         deal_w4(after_y(0, 1, "w4_dealt", [P, 2, H], U8))
-        pick(1, 0, M)
+        pick(1)
         quantize_w1(2)
         gather_callees(0)
 
@@ -402,10 +415,9 @@ def tile_list_excess_delay_causes_kernel(tc, tab_words, tab_scales, offs, pos1, 
         for lo in (0, PIECE):
             quantize_h(0, lo)
 
-        last = TILES - 1
-        w8_product(last)
+        w8_product(LAST)
         for lo in (0, PIECE):
-            subtract(last, lo, lo + PIECE)
+            subtract(LAST, lo, lo + PIECE)
         round_h(1, 0)
         dst, src = h_views(1, PIECE)
         groups = PIECE // 4

from contextlib import ExitStack

import concourse.mybir as mybir
from concourse.masks import make_identity

K, T, S, T2, M, H, N = 1024, 4096, 1024, 1024, 512, 1024, 384
FLOPS = 2 * K * H * S * 2 + 2 * K * H * M + 2 * H * N * M

F32 = mybir.dt.float32
BF16 = mybir.dt.bfloat16
I32 = mybir.dt.int32
U32 = mybir.dt.uint32
U16 = mybir.dt.uint16
U8 = mybir.dt.uint8
FP8X4 = mybir.dt.float8_e4m3fn_x4
FP4X4 = mybir.dt.float4_e2m1fn_x4
ALU = mybir.AluOpType
IDENTITY = mybir.ActivationFunctionType.Identity
RELU = mybir.ActivationFunctionType.Relu

P = 128
FLOAT32_MAX = 3.4028234663852886e38
BANK = 512
PIECE = M // 2
TILES = 8
NATURAL = 4
HALF = H // 2
CALLER_ROWS = 96
CALLEE_ROWS = 112
V_AT, W4_AT, CALLER_WIDTH = 0, S, S + H
V2_AT, W8_AT, CALLEE_WIDTH = 0, M, M + H
LAST = TILES - 1
FUSED = range(2, TILES)

AT_TABLE = (1, 24)
AT_W4_DEALT_RAW = 0
AT_V2_SCALES = 2
AT_W1_NEXT = 7
AT_TABLE2 = 15
AT_WO = (7, 13)
AT_V_SCALES = 23.0625
AT_W8 = 23.5
AT_W1_LATE = 31.5
AT_WO_ROUNDED = (31.5, 34.5)
AT_LATE_ROUNDED = {4: 51.5, 5: 55.5}
AT_W8_DEALT = 47.5625
AT_OWN_COPY = (52.5, 56.5)
AT_Y_TILE5 = 54.5
AT_EXCESS = 59.5


def tile_list_excess_delay_causes_kernel(tc, tab_words, tab_scales, offs, pos1, tab2_words, tab2_scales, offs2,
                                                   w1, b1, w4_words, w4_scales, w8_words, w8_scales, wo, out):
    nc = tc.nc
    with ExitStack() as ctx:
        keep = ctx.enter_context(tc.tile_pool(name="keep", bufs=1))
        shared = ctx.enter_context(tc.tile_pool(name="shared", bufs=1))
        ring = ctx.enter_context(tc.tile_pool(name="ring", bufs=2))
        psum = ctx.enter_context(tc.psum_pool(name="psum", bufs=3))

        def held(name, shape, dtype):
            return keep.tile(shape, dtype, name=name, align_bytes=64)

        def placed(name, shape, dtype, kib):
            return shared.tile(shape, dtype, name=name, offset=int(1024 * kib), align_bytes=64)

        def after(tag, name, shape, dtype):
            return keep.tile(shape, dtype, name=name, tag=tag, align_bytes=64)

        def y_tag(n, hf):
            return {(5, 1): "late_rounded6", (6, 0): "late_rounded7"}.get((n, hf), "y%d%d" % (n, hf))

        def after_y(n, hf, name, shape, dtype):
            return after(y_tag(n, hf), name, shape, dtype)

        offs_t = keep.tile([P, S // 16], U16, name="offs_t")
        pos_t = keep.tile([P, M // 16], U16, name="pos_t")
        offs2_t = keep.tile([P, M // 16], U16, name="offs2_t")

        tab_s = held("tab_s", [P, T], U8)
        tab2_s = held("tab2_s", [P, 2, T2], U8)
        w4s_raw = held("w4s_raw", [P, 1, H], U8)
        caller_staged = held("caller_staged", [P, 1, CALLER_WIDTH], U8)
        w8s_raw = held("w8s_raw", [P, 2, H], U8)
        callee_s = held("callee_s", [P, 2, CALLEE_WIDTH], U8)
        caller_s = [held("caller_s%d" % a, [P, CALLER_WIDTH], U8) for a in range(2)]
        bias_rows = held("bias_rows", [P, HALF], F32)
        bias_dealt = held("bias_dealt", [P, 4, P], F32)
        ident = held("ident", [P, P], F32)
        bias = held("bias", [P, TILES], F32)
        minus_bias = held("minus_bias", [P, TILES], F32)

        nc.gpsimd.memset(bias_rows[:], 0.0)
        make_identity(nc, ident[:])
        for raw in (tab_s, w4s_raw):
            nc.vector.memset(raw[0:CALLER_ROWS].bitcast(I32), 0)
        for plane in caller_s:
            nc.vector.memset(plane[:].bitcast(I32), 0)
        for raw in (tab2_s, w8s_raw):
            nc.gpsimd.memset(raw[0:CALLEE_ROWS].bitcast(I32), 0)

        def load(dst, src):
            nc.sync.dma_start(dst, src)

        def load_caller_rows(dst, scales):
            load(dst.bitcast(I32), scales.rearrange("a q n -> (a q) n").bitcast(I32))

        def load_callee_rows(dst, scales):
            load(dst.bitcast(I32), scales.rearrange("a q n -> q a n").bitcast(I32))

        tab_w = {}
        wo_raw = {}

        def load_tab_words(a):
            tab_w[a] = placed("tab_w%d" % a, [P, T], I32, AT_TABLE[a])
            load(tab_w[a][:], tab_words[a].rearrange("p t i -> p (t i)").bitcast(I32))

        def load_w4(b, tile):
            load(tile[:].bitcast(I32), w4_words[:, :, H * b : H * (b + 1)].rearrange("a p e -> p a e").bitcast(I32))

        def load_wo(b):
            wo_raw[b] = placed("wo_raw%d" % b, [P, 4, N], F32, AT_WO[b])
            if b == 0:
                load(wo_raw[b][:], wo[0:HALF, :].rearrange("(p t) n -> p t n", t=4))
            else:
                for t in range(4):
                    load(wo_raw[b][:, t, :], wo[HALF:H, :].rearrange("(q t e) n -> t q e n", t=4, e=8)[t])

        def load_w1_columns(tile, lo, hi):
            for a in range(2):
                load(tile[:, a], w1[512 * a : 512 * (a + 1), lo:hi].rearrange("(p j) c -> p j c", j=4))

        load(offs_t[:], offs)
        load_caller_rows(tab_s[CALLER_ROWS:P], tab_scales)
        load_caller_rows(w4s_raw[CALLER_ROWS:P, 0], w4_scales)
        load(offs2_t[:], offs2)
        load_callee_rows(tab2_s[CALLEE_ROWS:P], tab2_scales)
        load_callee_rows(w8s_raw[CALLEE_ROWS:P], w8_scales)
        load_tab_words(0)
        w4_natural = held("w4_natural", [P, 2, H], U8)
        load_w4(0, w4_natural)
        load(bias_rows[0:2, :], b1.rearrange("(b c) -> b c", b=2))
        w1_first = held("w1_first", [P, 2, 4, 2 * P], F32)
        load_w1_columns(w1_first, 0, 2 * P)
        load(pos_t[:], pos1)

        def deal_scales(dst, raw):
            nc.vector.tensor_copy(dst[:, :, 0:HALF].bitcast(I32), raw[:, :, 0:HALF].bitcast(I32))
            nc.vector.tensor_copy(dst[:, :, HALF:H].bitcast(I32).rearrange("p a (t q i) -> p a t q i", t=4, i=2),
                                  raw[:, :, HALF:H].bitcast(I32).rearrange("p a (q t i) -> p a t q i", t=4, i=2))

        v_s = placed("v_s", [P, S], U8, AT_V_SCALES)
        nc.vector.tensor_copy(v_s[:], tab_s[:].indirect(offs_t[:]))
        deal_scales(caller_staged[:, :, W4_AT : W4_AT + H], w4s_raw[:])
        nc.vector.tensor_copy(caller_staged[:, 0, V_AT : V_AT + S].bitcast(I32), v_s[:].bitcast(I32))

        def move_caller_rows(a):
            first = CALLER_ROWS + 16 * a
            for s in range(4):
                load(caller_s[a][s:P:32].bitcast(I32), caller_staged[first + s : first + 16 : 4, 0].bitcast(I32))

        move_caller_rows(0)
        load_tab_words(1)
        move_caller_rows(1)
        w1_next = placed("w1_next", [P, 2, 4, 2 * P], F32, AT_W1_NEXT)
        load_w1_columns(w1_next, 2 * P, 4 * P)

        w4_tile = {n: w4_natural[:, :, 2 * P * n : 2 * P * (n + 1)] for n in range(NATURAL)}

        def deal_w4(dealt):
            nc.vector.tensor_copy(dealt[:].bitcast(I32).rearrange("p a (t q i) -> p a t q i", q=16, i=4),
                                  w4_raw[:].bitcast(I32).rearrange("p a (q t i) -> p a t q i", t=4, i=4))
            for t in range(4):
                w4_tile[NATURAL + t] = dealt[:, :, 2 * P * t : 2 * P * (t + 1)]

        def deal_w8(dealt):
            w8_half[1] = dealt
            nc.vector.tensor_copy(dealt[:].rearrange("p a (t q e) -> p a t q e", t=4, e=8),
                                  w8_raw[:, :, HALF:H].rearrange("p a (q t e) -> p a t q e", t=4, e=8))

        v_w = {(a, hf): held("v_w%d%d" % (a, hf), [P, BANK], U32) for a in range(2) for hf in range(2)}

        def gather_callers(a):
            for hf in range(2):
                nc.vector.tensor_copy(v_w[a, hf][:], tab_w[a][:].bitcast(U32).indirect(offs_t[:, 32 * hf : 32 * (hf + 1)]))

        gather_callers(0)
        w4_raw = placed("w4_raw", [P, 2, H], U8, AT_W4_DEALT_RAW)
        load_w4(1, w4_raw)
        tab2_w = placed("tab2_w", [P, 2, T2], I32, AT_TABLE2)
        load(tab2_w[:], tab2_words.rearrange("a p t i -> p a (t i)").bitcast(I32))

        v2_s = placed("v2_s", [P, 2, M], U8, AT_V2_SCALES)
        for a in range(2):
            nc.vector.tensor_copy(v2_s[:, a, :], tab2_s[:, a, :].indirect(offs2_t[:]))
        deal_scales(callee_s[:, :, W8_AT : W8_AT + H], w8s_raw[:])
        nc.vector.tensor_copy(callee_s[:, :, V2_AT : V2_AT + M].bitcast(I32), v2_s[:].bitcast(I32))
        for s in range(4):
            load(callee_s[4 + s : P : 32].bitcast(I32), callee_s[CALLEE_ROWS + s : P : 4].bitcast(I32))

        nc.scalar.copy(bias_dealt[:].rearrange("p t (q e) -> p t q e", e=8), bias_rows[:].rearrange("p (q t e) -> p t q e", t=4, e=8))
        for b, rows in enumerate((bias_rows[:].rearrange("p (t c) -> p t c", t=4), bias_dealt[:])):
            bias_ps = psum.tile([P, BANK], F32, name="bias_ps", tag="callee", bufs=2)
            for t in range(4):
                nc.tensor.transpose(bias_ps[:, P * t : P * (t + 1)], rows[:, t, :], ident[:])
            nc.scalar.copy(bias[:, 4 * b : 4 * (b + 1)], bias_ps[:, b:BANK:P])
        nc.scalar.activation(minus_bias[:], bias[:], IDENTITY, scale=-1.0)

        w1_c = [held("w1_c%d" % n, [P, 2, P], U32) for n in range(TILES)]
        w1_s = [held("w1_s%d" % n, [P, 2, P], U8) for n in range(TILES)]
        w1_rounded = {}
        ROUNDED = [P, 2, P, 4]

        def round_natural(n):
            raw = (w1_first, w1_next)[n // 2][:, :, :, P * (n % 2) : P * (n % 2 + 1)]
            if n == 3:
                w1_rounded[n] = held("next_rounded3", ROUNDED, BF16)
                for a in range(2):
                    nc.gpsimd.tensor_scalar(w1_rounded[n][:, a], raw[:, a].rearrange("p j c -> p c j"), 1.0, 0.0, ALU.mult, ALU.add)
                return
            w1_rounded[n] = held("first_rounded%d" % n, ROUNDED, BF16) if n < 2 else after_y(1, 0, "next_rounded", ROUNDED, BF16)
            nc.scalar.copy(w1_rounded[n][:].rearrange("p a (c i) j -> p a c j i", i=4), raw.rearrange("p a j (c i) -> p a c j i", i=4))

        def round_dealt(n):
            name = "late_rounded%d" % n
            w1_rounded[n] = placed(name, ROUNDED, BF16, AT_LATE_ROUNDED[n]) if n in AT_LATE_ROUNDED else held(name, ROUNDED, BF16)
            nc.scalar.copy(w1_rounded[n][:].rearrange("p a (q e) j -> p a q j e", e=8),
                           w1_late[:].rearrange("p a j (q t e) -> p t a q j e", t=4, e=8)[:, n - NATURAL])

        def quantize_w1(n):
            nc.vector.quantize_mx(out=w1_c[n][:].rearrange("p a c -> p (a c)").bitcast(FP8X4), scales=w1_s[n][:].rearrange("p a c -> p (a c)"),
                                  in_=w1_rounded[n][:].rearrange("p a c j -> p (a c j)"))

        wo_s = held("wo_s", [P, 2 * N], U8)
        wo_c = held("wo_c", [P, 2 * N], U32)

        def round_and_quantize_wo(b):
            rounded = placed("wo_rounded%d" % b, [P, N, 4], BF16, AT_WO_ROUNDED[b])
            nc.scalar.copy(rounded[:].rearrange("p (c i) t -> p c t i", i=4), wo_raw[b][:].rearrange("p t (c i) -> p c t i", i=4))
            nc.vector.quantize_mx(out=wo_c[:, N * b : N * (b + 1)].bitcast(FP8X4), scales=wo_s[:, N * b : N * (b + 1)], in_=rounded[:].rearrange("p n t -> p (n t)"))

        round_natural(0)
        quantize_w1(0)
        gather_callers(1)
        w1_late = placed("w1_late", [P, 2, 4, HALF], F32, AT_W1_LATE)
        load_w1_columns(w1_late, HALF, H)
        w8_raw = placed("w8_raw", [P, 2, H], I32, AT_W8)
        load(w8_raw[:], w8_words.rearrange("a p e i -> p a (e i)").bitcast(I32))
        w8_half = {0: w8_raw}

        y = {}
        summed = {}
        window = {}
        picked = {}
        own = {}
        own_copy = {}
        minus_excess = [placed("minus_excess0", [P, 4, M], F32, AT_EXCESS), held("minus_excess1", [P, 4, M], F32)]

        def callers(a, hf):
            return dict(rhs=v_w[a, hf][:].bitcast(FP8X4), rhs_scale=caller_s[a][:, V_AT + BANK * hf : V_AT + BANK * (hf + 1)])

        p4 = {}
        p1 = {}

        def sum_bank(name, n, hf):
            if (n, hf) == (1, 1):
                return psum.tile([P, BANK], F32, name=name, tag="callee", bufs=2)
            return psum.tile([P, BANK], F32, name=name, tag=name)

        def w4_operand(n, a):
            return dict(lhsT=w4_tile[n][:, a, :].bitcast(FP4X4), lhsT_scale=caller_s[a][:, W4_AT + P * n : W4_AT + P * (n + 1)])

        def w4_pass(n, hf, a):
            if a == 0:
                p4[n, hf] = sum_bank("p4", n, hf)
            nc.tensor.matmul_mx(out=p4[n, hf][:], start=(a == 0), stop=(a == 1), **w4_operand(n, a), **callers(a, hf))
            if a == 1:
                y[n, hf] = placed("y_tile5", [P, BANK], F32, AT_Y_TILE5) if (n, hf) == (5, 0) else after(y_tag(n, hf), "y", [P, BANK], F32)
                if n == LAST:
                    nc.scalar.activation(y[n, hf][:], p4[n, hf][:], RELU)
                else:
                    nc.scalar.activation(y[n, hf][:], p4[n, hf][:], IDENTITY, bias=bias[:, n : n + 1])

        def w4_product(n):
            for hf in range(2):
                for a in range(2):
                    w4_pass(n, hf, a)

        def w1_pass(n, hf, a):
            if a == 0:
                p1[n, hf] = sum_bank("p1", n, hf)
            nc.tensor.matmul_mx(out=p1[n, hf][:], lhsT=w1_c[n][:, a].bitcast(FP8X4), lhsT_scale=w1_s[n][:, a], start=(a == 0), stop=(a == 1), **callers(a, hf))
            if a == 0 and n == LAST:
                for a4 in range(2):
                    nc.tensor.matmul_mx(out=p1[n, hf][:], start=False, stop=False, **w4_operand(n, a4), **callers(a4, hf))

        def w1_product_and_add(n, hf, passes=range(2)):
            for a in passes:
                w1_pass(n, hf, a)
            by_gpsimd = n in FUSED and n < LAST
            if hf == 0:
                window[n] = ring.tile([P, S], F32, name="window", bufs=3)
                if by_gpsimd:
                    summed[n] = ring.tile([P, S], F32, name="summed", bufs=3)
            half = slice(BANK * hf, BANK * (hf + 1))
            if n == LAST:
                nc.vector.scalar_tensor_tensor(window[n][:, half], p1[n, hf][:], bias[:, n : n + 1], y[n, hf][:], ALU.add, ALU.max)
                return
            target = (summed if by_gpsimd else window)[n][:, half]
            nc.vector.scalar_tensor_tensor(target, p1[n, hf][:], minus_bias[:, n : n + 1], y[n, hf][:], ALU.max, ALU.add)
            if by_gpsimd:
                nc.gpsimd.tensor_scalar(window[n][:, half], target, FLOAT32_MAX, 0.0, ALU.min, ALU.max)

        def w8_product(n):
            b, t = divmod(n, 4)
            own[n] = psum.tile([P, BANK], F32, name="own", tag="callee", bufs=2)
            for a in range(2):
                nc.tensor.matmul_mx(out=own[n][:], lhsT=w8_half[b][:, a, P * t : P * (t + 1)].bitcast(FP8X4),
                                    lhsT_scale=callee_s[4:P, a, W8_AT + P * n : W8_AT + P * (n + 1)],
                                    rhs=v2_w[a][:].bitcast(FP8X4), rhs_scale=callee_s[4:P, a, V2_AT : V2_AT + M], start=(a == 0), stop=(a == 1))
            if n in FUSED:
                own_copy[n] = placed("own_copy%d" % n, [P, M], F32, AT_OWN_COPY[n % 2])
                nc.scalar.copy(own_copy[n][:], own[n][:])

        def pick(n):
            picked[n] = ring.tile([P, M], F32, name="picked", bufs=2, align_bytes=64)
            nc.vector.tensor_copy(picked[n][:], window[n][:].indirect(pos_t[:]))

        def subtract(n, lo, hi):
            target = held("natural%d" % n, [P, M], F32)[:] if n < NATURAL else minus_excess[1][:, n - NATURAL, lo:hi]
            if n in FUSED:
                nc.vector.tensor_tensor(target, window[n][:].indirect(pos_t[:, lo // 16 : hi // 16]), own_copy[n][:, lo:hi], ALU.subtract)
            else:
                nc.vector.scalar_tensor_tensor(target, picked[n][:], 0.0, own[n][:], ALU.max, ALU.subtract)
            if n < NATURAL:
                nc.sync.dma_start(minus_excess[0][32 * n : 32 * (n + 1)], target)

        h_rounded = {}
        h_c = {}
        h_s = {}

        def h_views(b, lo):
            if b == 0:
                h_rounded[b, lo] = after_y(6, lo // PIECE, "h_rounded", [P, PIECE, 4], BF16)
            else:
                h_rounded[b, lo] = placed("h_rounded%d" % lo, [P, PIECE, 4], BF16, AT_EXCESS + 2 * (lo // PIECE))
            return (h_rounded[b, lo][:].rearrange("p (c i) t -> p c t i", i=4),
                    minus_excess[b][:, :, lo : lo + PIECE].rearrange("p t (c i) -> p c t i", i=4))

        def round_h(b, lo):
            dst, src = h_views(b, lo)
            nc.scalar.activation(dst, src, RELU, scale=-1.0)

        def quantize_h(b, lo):
            h_c[b, lo] = held("h_c%d_%d" % (b, lo), [P, PIECE], U32)
            h_s[b, lo] = held("h_s%d_%d" % (b, lo), [P, PIECE], U8)
            nc.vector.quantize_mx(out=h_c[b, lo][:].bitcast(FP8X4), scales=h_s[b, lo][:], in_=h_rounded[b, lo][:].rearrange("p m t -> p (m t)"))

        v2_w = {}

        def gather_callees(a):
            v2_w[a] = after((y_tag(1, 0), "next_rounded3")[a], "v2_w", [P, M], U32)
            nc.vector.tensor_copy(v2_w[a][:], tab2_w[:, a, :].bitcast(U32).indirect(offs2_t[:]))

        for hf in range(2):
            w4_pass(0, hf, 0)
            w1_pass(0, hf, 0)
        round_natural(1)
        quantize_w1(1)
        for hf in range(2):
            w4_pass(1, hf, 0)
            w1_pass(1, hf, 0)
        for hf in range(2):
            for n in range(2):
                w4_pass(n, hf, 1)
                w1_product_and_add(n, hf, passes=(1,))
        round_natural(2)
        pick(0)
        deal_w4(after_y(0, 1, "w4_dealt", [P, 2, H], U8))
        pick(1)
        quantize_w1(2)
        gather_callees(0)

        w4_product(2)
        round_natural(3)
        for b in range(2):
            load_wo(b)
        for hf in range(2):
            w1_product_and_add(2, hf)
        quantize_w1(3)
        gather_callees(1)
        w4_product(3)
        for n in range(2):
            w8_product(n)
            subtract(n, 0, M)
        w4_product(NATURAL)
        for n in range(NATURAL, TILES):
            round_dealt(n)
            quantize_w1(n)
        round_and_quantize_wo(0)

        for n in range(NATURAL - 1, TILES):
            for hf in range(2):
                w1_product_and_add(n, hf)
            w8_product(n - 1)
            subtract(n - 1, 0, M)
            if n == NATURAL - 1:
                deal_w8(placed("w8_dealt", [P, 2, HALF], I32, AT_W8_DEALT))
            elif n + 1 < TILES:
                w4_product(n + 1)
            if n == NATURAL + 1:
                round_and_quantize_wo(1)
        for lo in (0, PIECE):
            round_h(0, lo)
        for lo in (0, PIECE):
            quantize_h(0, lo)

        w8_product(LAST)
        for lo in (0, PIECE):
            subtract(LAST, lo, lo + PIECE)
        round_h(1, 0)
        dst, src = h_views(1, PIECE)
        groups = PIECE // 4
        nc.vector.tensor_scalar(dst[:, 0 : groups // 2], src[:, 0 : groups // 2], -1.0, 0.0, ALU.mult, ALU.max)
        nc.scalar.activation(dst[:, groups // 2 : groups], src[:, groups // 2 : groups], RELU, scale=-1.0)

        def score_pass(b, lo, c):
            cols = slice(N * b + P * c, N * b + P * (c + 1))
            nc.tensor.matmul_mx(out=scores[lo, c][:, 0:PIECE], lhsT=wo_c[:, cols].bitcast(FP8X4), lhsT_scale=wo_s[:, cols],
                                rhs=h_c[b, lo][:].bitcast(FP8X4), rhs_scale=h_s[b, lo][:], start=(b == 0), stop=(b == 1))

        scores = {(lo, c): psum.tile([P, BANK], F32, name="scores", tag=tag) for lo, tag in ((0, "p1"), (PIECE, "p4")) for c in range(3)}
        for lo, c in scores:
            score_pass(0, lo, c)
        for lo in (0, PIECE):
            quantize_h(1, lo)
        copies = [nc.scalar.copy, nc.scalar.copy, nc.vector.tensor_copy, nc.vector.tensor_copy, nc.scalar.copy, nc.vector.tensor_copy]
        for copy, (lo, c) in zip(copies, scores):
            score_pass(1, lo, c)
            staged = held("staged%d_%d" % (lo, c), [P, PIECE], F32)
            copy(staged[:], scores[lo, c][:, 0:PIECE])
            nc.sync.dma_start(out[P * c : P * (c + 1), lo : lo + PIECE], staged[:])
